import numpy as np, ml_dtypes
CORES = [1,5,17,21,33,37,49,53]
N = 8
BF = ml_dtypes.bfloat16
def gentries(a):
    return np.ascontiguousarray(a.reshape(8, 16, -1).transpose(0, 2, 1)).reshape(8, -1)
def gtable(e):
    e = np.asarray(e); return np.ascontiguousarray(e.reshape(8, -1, 16).transpose(0, 2, 1)).reshape(128, -1).astype(np.int32)
P, L, S, F, RO = 4096, 2048, 4, 512, 3
H = P - F
def depths(rng, up, top):
    s = np.where(rng.random((N, 8, P)) < up, 1, 1 - rng.geometric(0.5, (N, 8, P))); d = np.zeros((N, 8, P), np.int64); now = np.zeros((N, 8), np.int64)
    for v in range(1, P):
        now = np.minimum(np.maximum(now + s[:, :, v], 0), top); d[:, :, v] = now
    return d
def closed(d):
    e = np.zeros(d.shape, np.int64); last = np.full(d.shape[:-1] + (1,), P, np.int64)
    for k in range(int(np.max(d)) + 1):
        m = np.minimum.accumulate(np.where(d <= k, np.arange(P), P)[..., ::-1], axis=-1)[..., ::-1]
        e = np.where(d == k, np.concatenate([m[..., 1:], last], axis=-1), e)
    return e
def parts(rng):
    up = rng.choice(np.array([0.4, 0.5, 0.6]), (N, 8, 1)); top = rng.integers(3, 13, (N, 8))
    full = np.arange(P) < (P * rng.choice(np.array([8, 12, 14, 16]), (N, 8, 1))) // 16
    d = np.where(full, depths(rng, up, top), 0)
    x = np.where(rng.random((N, 8, 16, P)) < 0.25, rng.integers(0, 4, (N, 8, 16, P)), rng.integers(0, 256, (N, 8, 16, P))) * full[:, :, None, :]
    return x, d, rng.integers(0, 256, (N, 8, 16, L)), rng.integers(0, P, (N, 8, RO, L))
def pack(x, e, w, st):
    return {"x": np.ascontiguousarray(x.reshape(N, 128, P)).astype(np.float32).astype(BF), "w": np.ascontiguousarray(w.reshape(N, 128, L)).astype(np.float32).astype(BF),
            "ends": np.ascontiguousarray(e).astype(np.int32), "start": np.stack([gtable(a.reshape(8, -1)) for a in st])}
def setup_inputs(rng):
    x, d, w, st = parts(rng)
    return pack(x, closed(d), w, st)
def setup_inputs_room(rng):
    x, d, w, st = parts(rng); x = rng.integers(0, 256, x.shape); Q = P // 16; z = F // 4
    at = ((H - z, H), (H - z + 1, H + 1), (H, H + z), (H - 1, H - 1 + z), (P - z, P), (P - z + 1, P + 1), (P - 1, P - 1 + z), (H - z, -1))
    for q in range(N):
        for g in range(8):
            n = int(rng.integers(Q // 2, Q + 1)); a, b = at[(g + q) % 8]; a = a - n; b = P if b < 0 else b - n; D = d[q, g].copy()
            d[q, g] = np.concatenate([np.tile(np.arange(3), Q), D[:a - 3 * Q], np.zeros(1, np.int64), 1 + D[:b - a - 1], D[:P - b]])
            hot = 3 * rng.permutation(Q)[:n]
            st[q, g, 0] = rng.permutation(np.concatenate([hot, rng.choice(hot, L - n)]))
    return pack(x, closed(d), w, st)
def setup_inputs_ties(rng):
    x, d, w, st = parts(rng); lo = rng.choice(np.array([0, 100, 252]), (N, 8, 1, 1))
    x = lo + rng.integers(0, 4, x.shape); x[:, 1::2] = (lo + 2 * rng.integers(0, 2, (N, 8, 1, P)))[:, 1::2]
    return pack(x, closed(d), np.minimum(lo + rng.integers(0, 5, w.shape), 255), st)
def setup_inputs_alike(rng):
    x, d, w, st = parts(rng); x = rng.integers(0, 256, x.shape); e = closed(d); at = np.arange(P)
    names = rng.integers(0, P, (N, 8, RO, 6)); names[..., 0] = 0; names[..., 1] = P - 1
    st = np.take_along_axis(names, rng.integers(0, 6, st.shape), 3)
    for q in range(N):
        g = (np.arange(4) + q) % 8
        e[q, g[0]] = P; st[q, g[0], 0] = rng.choice(np.array([0, P - 1, P - 2, P - 3, P - 1 - S, P - 2 - S]), L)
        e[q, g[1]] = at + 1; e[q, g[1], :2] = P; st[q, g[1], 0] = 0
        e[q, g[2]] = at + 1
        e[q, g[3]] = np.where(at % 2 == 0, P, at + 1); st[q, g[3], 0] = rng.integers(0, P, L)
    return pack(x, e, w, st)
def setup_inputs_far(rng):
    x, d, w, st = parts(rng); x = rng.integers(0, 256, x.shape); w = rng.integers(1, 256, w.shape); g = rng.permutation(8); odd = np.arange(N) % 2 == 1; i4 = np.arange(16)[:, None] % 4
    kid = np.where(odd, rng.integers(3 * P // 4 + 2, P - 1, N), P - 1); low = np.where(odd, rng.integers(3 * P // 4, H, N), P - 1)
    left = np.where(odd, rng.integers(15 * P // 32, P // 2 - 4, N), rng.integers(7 * P // 16 + 1, 15 * P // 32, N)); T = min(P // 7, L // 4)
    st[:, g[:4]] = P - 1
    for q in range(N):
        D = d[q].copy(); b = int(kid[q]); z = int(low[q]); s = int(left[q]); m = D[g[0]]
        d[q, g[0]] = np.concatenate([np.array([0, 1, 2, 3]), 3 + m[:b - 4], np.array([2]), m[:P - b - 1]])
        x[q, g[0], :, b] = 0; st[q, g[0], 0] = 0
        d[q, g[1]] = np.concatenate([np.zeros(z + 1, np.int64), D[g[1]][:P - z - 1]])
        v = rng.choice(np.array([0, z - 2]), L); v[0] = 0; v[1] = z - 2; st[q, g[1], 0] = v
        m = D[g[2]]; d[q, g[2]] = np.concatenate([np.arange(3), 2 + m[:s - 1], m[:P - s - 2]]); st[q, g[2], 0] = 0
        m = D[g[3]]; a = H - 4 + q % 2
        d[q, g[3]] = np.concatenate([m[:H - 4], np.array([0, 0, 1, 2, 3]) if q % 2 else np.array([0, 1, 2, 3, 3]), m[:P - H - 1]])
        v = np.where(rng.random(L) < 0.5, a, rng.integers(H, P, L)); v[0] = a; st[q, g[3], 1] = v
        d[q, g[4]] = np.concatenate([np.tile(np.array([0, 1, 2, 2, 1, 2, 2]), T), D[g[4]][:P - 7 * T]])
        few = np.array([4, 0, 2, 3, 1, 2, 3])[np.arange(P) % 7]
        x[q, g[4]] = np.where(i4 == few, rng.integers(0, 61, (16, P)), rng.integers(200, 256, (16, P)))
        j = rng.permutation(np.concatenate([np.arange(4 * T), rng.integers(0, 4 * T, L - 4 * T)])); st[q, g[4], 0] = 7 * (j // 4)
        w[q, g[4]] = np.where((i4 == (j % 4) // 2) | (i4 == 2 + j % 2), rng.integers(100, 201, (16, L)), 0)
    x[:, g[0], :, 2] = 255; x[:, g[0], :, 3] = 0; x[:, g[0], :, 4] = 255; x[:, g[3], :, H - 1] = 255; x[:, g[3], :, H] = 0
    for k in (1, 2):
        x[:, g[k], :, 2] = 0; x[:, g[k], :, 3] = 255
    e = closed(d)
    for q in range(N):
        z = int(low[q]); e[q, g[1], :z + 1] = z + 1; e[q, g[1], 2] = 3
    return pack(x, e, w, st)
def setup_inputs_spread(rng):
    x, d, w, st = parts(rng)
    d = depths(rng, 0.35 + 0.35 * rng.random((N, 8, 1)), np.exp2(1 + 5 * rng.random((N, 8))).astype(np.int64) + 1)
    x = np.minimum((np.exp2(8 * rng.random((N, 8, 1, P))) * rng.random((N, 8, 16, P))).astype(np.int64), 255)
    w = np.minimum((np.exp2(8 * rng.random((N, 8, 1, L))) * rng.random((N, 8, 16, L))).astype(np.int64), 255)
    st = np.minimum((P * rng.random((N, 8, RO, L)) ** rng.choice(np.array([1, 2, 4]), (N, 8, 1, 1))).astype(np.int64), P - 1)
    return pack(x, closed(d), w, st)
def check_inputs(d):
    bad = []
    for k in ("x", "w"):
        v = d[k].astype(np.float32)
        if not np.all((v >= 0) & (v <= 255) & (v == np.floor(v))): bad.append("whole numbers from 0 to 255 in " + k)
    e = d["ends"].astype(np.int64); n = e - np.arange(P)
    if np.min(n) < 1 or np.max(e) > P: bad.append("range of ends")
    else:
        big = e; most = np.zeros(e.shape, np.int64); k = 1
        while k <= P:
            sel = (n >= k) & (n < 2 * k)
            most = np.where(sel, np.maximum(big, np.take_along_axis(big, np.where(sel, e - k, 0), 2)), most)
            big = np.concatenate([np.maximum(big[..., :P - k], big[..., k:]), big[..., P - k:]], axis=2); k = 2 * k
        if np.any(most > e): bad.append("runs that cross")
    if np.min(d["start"]) < 0 or np.max(d["start"]) > P - 1: bad.append("range of start")
    return bad
def grow(x, e, w, v):
    G = np.arange(8)[:, None]; at = np.arange(P); n = np.zeros((8, L), np.int64); par = v
    for i in range(S):
        ev = e[G, v]; a = np.minimum(v + 1, P - 1); b = e[G, a]; kids = ev > v + 1; two = kids & (b < ev); b = np.minimum(b, P - 1)
        ra = np.add.reduce(np.maximum(w - x[G, a], 0), axis=2); rb = np.add.reduce(np.maximum(w - x[G, b], 0), axis=2)
        par = np.where(kids, v, par); n = n + kids; v = np.where(kids, np.where(two & (rb > ra), b, a), v)
    hit = (n >= 2) & (e[G, v] == v + 1); gi = np.broadcast_to(G, v.shape)[hit]
    head = np.zeros((8, P), bool); head[gi, v[hit]] = True; mark = np.zeros((8, P), bool); mark[gi, par[hit]] = True
    zero = np.zeros((8, 1), np.int64); reach = np.maximum.accumulate(np.where(mark, e, 0), axis=1)
    top = mark & (np.concatenate([zero, reach[:, :-1]], axis=1) <= at); inside = reach > at; keep = ~head
    first = np.maximum.accumulate(np.where(top, at, 0), axis=1)
    K = np.concatenate([zero, np.add.accumulate(keep.astype(np.int64), axis=1)], axis=1)
    M = np.concatenate([zero, np.add.accumulate(keep * (1 + 2 * inside), axis=1)], axis=1)
    size = np.where(inside, K[G, e] - K[:, :P], M[G, e] - M[:, :P]); s = K[G, e[G, first]] - K[G, first]
    nx = np.zeros((8, P, 16), np.int64); ne = np.zeros((8, P), np.int64) + at + 1
    for c in range(3):
        q = np.where(inside, M[G, first] + c * s + K[:, :P] - K[G, first], M[:, :P])
        gk, vk = np.nonzero(keep & (inside | (c == 0)) & (q < P)); qk = q[gk, vk]
        nx[gk, qk] = np.maximum(x[gk, vk] - c, 0); ne[gk, qk] = qk + size[gk, vk]
    return nx, ne
def reference(x, w, ends, start):
    X = np.ascontiguousarray(x.astype(np.float32).astype(np.int64).reshape(N, 8, 16, P).transpose(0, 1, 3, 2)); E = ends.astype(np.int64)
    W = np.ascontiguousarray(w.astype(np.float32).astype(np.int64).reshape(N, 8, 16, L).transpose(0, 1, 3, 2))
    st = np.stack([gentries(a) for a in start]).astype(np.int64).reshape(N, 8, RO, L)
    for t in range(RO):
        both = [grow(X[r], E[r], W[r], st[r, :, t]) for r in range(N)]
        gx = np.stack([a for a, b in both]); ge = np.stack([b for a, b in both])
        X = np.concatenate([gx[:, :, :H], np.roll(gx[:, :, H:], 1, axis=0)], axis=2)
        E = np.concatenate([np.minimum(ge[:, :, :H], H), np.roll(np.minimum(ge[:, :, H:], P), 1, axis=0)], axis=2)
    return {"y": np.ascontiguousarray(X.transpose(0, 1, 3, 2)).reshape(N, 128, P).astype(np.float32).astype(BF), "ye": E.astype(np.float32)}

@@ -1,0 +1,675 @@
+import numpy as np
+from concourse.bass import DstId, RemoteDMATransfer
+from concourse.mybir import dt, AluOpType, AxisListType, ActivationFunctionType
+import comms_topo
+
+RO = 3
+NLO = 20
+
+SCRATCH = {
+    "BIG": ("sbuf", [128, 20736], "bfloat16"),
+    "VPAY": ("sbuf", [128, 4096], "bfloat16"),
+    "WP": ("sbuf", [128, 2048], "bfloat16"),
+    "INFO": ("sbuf", [128, 4112], "bfloat16"),
+    "GH": ("sbuf", [128, 4128], "bfloat16"),
+    "GV": ("sbuf", [128, 4096], "bfloat16"),
+    "G1": ("sbuf", [128, 4112], "bfloat16"),
+    "VLS": ("sbuf", [128, 4096], "bfloat16"),
+    "SZB": ("sbuf", [128, 3584], "bfloat16"),
+    "XS": ("sbuf", [128, 512], "bfloat16"),
+    "SZS": ("sbuf", [128, 512], "bfloat16"),
+    "HB": ("sbuf", [128, 256], "bfloat16"),
+    "STI": ("sbuf", [128, 384], "int32"),
+    "EI": ("sbuf", [128, 256], "int32"),
+    "AL": ("sbuf", [128, 128], "uint16"),
+    "BL": ("sbuf", [128, 128], "uint16"),
+    "EL": ("sbuf", [128, 264], "uint16"),
+    "OFF": ("sbuf", [128, 256], "uint16"),
+    "VLL": ("sbuf", [128, 256], "uint16"),
+    "QL": ("sbuf", [128, 256], "uint16"),
+    "XL": ("sbuf", [128, 256], "uint16"),
+    "PI": ("sbuf", [128, 4], "int32"),
+    "COL": ("sbuf", [128, 32], "float32"),
+    "ROW": ("sbuf", [128, 160], "float32"),
+    "ROW2": ("sbuf", [128, 160], "float32"),
+    "RC": ("sbuf", [128, 8], "float32"),
+}
+for _t in range(RO + 1):
+    SCRATCH["X%d" % _t] = ("sbuf", [128, 4112], "bfloat16")
+for _t in range(RO):
+    SCRATCH["LZ%d" % _t] = ("sbuf", [128, 512], "bfloat16")
+for _n in ("LP", "LN", "LB", "L1", "L2", "L3", "L4", "SELH"):
+    SCRATCH[_n] = ("sbuf", [128, 2048], "bfloat16")
+for _n in ("ID", "TRI", "TRI2", "SHF", "ONE", "CODE", "MISS", "NV", "MM", "GQ", "NID", "AF0", "AF1"):
+    SCRATCH[_n] = ("sbuf", [128, 128], "float32")
+for _n in ("PKI", "PPI", "PSI"):
+    SCRATCH[_n] = ("sbuf", [128, 256], "int32")
+for _n in ("TI", "THI", "TLO"):
+    SCRATCH[_n] = ("sbuf", [128, 128], "int32")
+for _n in ("HIb", "LOb", "IDB", "NIDB", "ID2B", "ID64"):
+    SCRATCH[_n] = ("sbuf", [128, 128], "bfloat16")
+for _n in ("VG", "VC", "REM", "QW", "ZERO", "KD", "TW", "TWE", "HF", "EG", "HK", "HINC", "HEC", "KDE", "CK", "CV",
+           "OX", "OUT", "KI", "POS", "T1", "T2", "T3", "T4", "T5", "T6"):
+    SCRATCH[_n] = ("sbuf", [128, 256], "float32")
+for _n in ("SZ", "HM", "HME", "RS", "J2", "EF"):
+    SCRATCH[_n] = ("sbuf", [128, 264], "float32")
+for _n in ("B0", "B1", "H0", "H1", "HMb", "J0", "J1", "P0", "P1", "Z0", "Z1", "S20", "S21"):
+    SCRATCH[_n] = ("sbuf", [128, 256], "bfloat16")
+for _n in range(8):
+    SCRATCH["b%d" % _n] = ("psum", [128, 512], "float32")
+
+SEMAPHORES = (["sV", "sS", "sP", "sG"] + ["d%d" % _k for _k in range(72)]
+              + ["%s%d" % (_a, _k) for _a in ("rx", "rz", "lx", "lz") for _k in range(RO)])
+
+ALL = (0, 128, 1)
+ONEROW = (0, 1, 1)
+ACT = ActivationFunctionType
+OP = AluOpType
+
+
+def v(name, c0=0, c1=None, cs=1, p=ALL):
+    if c1 is None:
+        c1 = 4096 if name in ("y", "ye", "x", "ends") else SCRATCH[name][1][1]
+    return (name, p, c0, c1, cs)
+
+
+BO = 4096
+
+
+def bg(c0, c1, cs=1):
+    return v("BIG", BO + c0, BO + c1, cs)
+
+
+def ind(win, off):
+    return ("@", win, off)
+
+
+def pmask(p):
+    m = 0
+    for k in range(p[0], p[1], p[2]):
+        m |= 1 << k
+    return m
+
+
+def rank_program(g, core, T, topo):
+    rank = T.rank_of(core)
+    if rank is None:
+        return
+    ops = []
+    masks = {}
+
+    def pm(p):
+        if p not in masks:
+            masks[p] = pmask(p)
+        return masks[p]
+
+    def flat(x, out):
+        if isinstance(x, tuple):
+            if x[0] == "@":
+                out.append(x[1])
+                out.append(x[2])
+            elif len(x) == 5:
+                out.append(x)
+        return out
+
+    def add(q, reads, writes, call, sem=None, n=1):
+        rd = []
+        for x in reads:
+            flat(x, rd)
+        wr = []
+        for x in writes:
+            if x[0] == "@":
+                wr.append(x[1])
+                rd.append(x[2])
+            else:
+                wr.append(x)
+        ops.append({"q": q, "r": rd, "w": wr, "call": call, "sem": sem, "n": n})
+
+    def ap(x):
+        if not isinstance(x, tuple):
+            return x
+        if x[0] == "@":
+            return ap(x[1]).indirect(ap(x[2]))
+        name, p, c0, c1, cs = x
+        return T[name][p[0]:p[1]:p[2], c0:c1:cs] if (p[2] != 1 or cs != 1) else T[name][p[0]:p[1], c0:c1]
+
+    def copy(out, i):
+        add("V", [i], [out], lambda: g.vector.tensor_copy(ap(out), ap(i)))
+
+    def tt(out, a, b, op):
+        add("V", [a, b], [out], lambda: g.vector.tensor_tensor(ap(out), ap(a), ap(b), op))
+
+    def ts(out, a, s1, op0, s2=None, op1=None):
+        if op1 is None:
+            add("V", [a, s1], [out], lambda: g.vector.tensor_scalar(ap(out), ap(a), ap(s1), None, op0))
+        else:
+            add("V", [a, s1, s2], [out], lambda: g.vector.tensor_scalar(ap(out), ap(a), ap(s1), ap(s2), op0, op1))
+
+    def red(out, i, op):
+        add("V", [i], [out], lambda: g.vector.tensor_reduce(ap(out), ap(i), AxisListType.X, op))
+
+    def scan(out, d0, d1, init, op0, op1):
+        add("V", [d0, d1, init], [out], lambda: g.vector.tensor_tensor_scan(ap(out), ap(d0), ap(d1), ap(init), op0, op1))
+
+    def fill(out, c):
+        add("V", [], [out], lambda: g.vector.memset(ap(out), c))
+
+    def act(out, i, func, bias=None, scale=None):
+        def call():
+            kw = {}
+            if bias is not None:
+                kw["bias"] = bias
+            if scale is not None:
+                kw["scale"] = ap(scale)
+            return g.scalar.activation(ap(out), ap(i), func, **kw)
+        add("S", [i, scale], [out], call)
+
+    def mm(out, l, r, start, stop):
+        add("P", [l, r], [out], lambda: g.tensor.matmul(ap(out), ap(l), ap(r), start, stop))
+
+    def tr(out, i, idn):
+        add("P", [i, idn], [out], lambda: g.tensor.transpose(ap(out), ap(i), ap(idn)))
+
+    def iota(out, pattern, base, cm, small=True):
+        if small:
+            add("G", [], [out], lambda: g.iota(ap(out), pattern, base, cm, allow_small_or_imprecise_dtypes=True))
+        else:
+            add("G", [], [out], lambda: g.iota(ap(out), pattern, base, cm))
+
+    def asel(out, i, pattern, cop, fillv, base, cm):
+        add("G", [i], [out], lambda: g.affine_select(ap(out), ap(i), pattern, cop, fillv, base, cm))
+
+    nd = [0]
+
+    def dma(out, i):
+        sem = "d%d" % nd[0]
+        nd[0] += 1
+        add("Y", [i], [out], lambda: g.sync.dma_start(ap(out), ap(i)), sem, 16)
+
+    def rows(name, r, c0, src):
+        dma(v(name, c0, c0 + 4096, 1, (r, 128, 16)), v(src))
+
+    def bwd(out, lname, src, c0, k, first=True, last=True):
+        for i in range(16):
+            mm(out, v(lname, 128 * i, 128 * i + 128), v(src, c0 + i, c0 + 16 * k, 16), first and i == 0, last and i == 15)
+
+    dma(v("EI"), v("ends", 0, 4096, 1, (0, 8, 1)))
+    dma(v("STI"), v("start", 0, 384))
+    dma(v("X0", 0, 4096), v("x"))
+    dma(v("WP"), v("w", 0, 2048))
+    PIc = v("PI", 0, 1)
+
+    def col(k):
+        return v("COL", k, k + 1)
+    iota(PIc, [[0, 1]], 0, 1, False)
+    iota(v("VG"), [[1, 256]], 0, 256)
+    iota(bg(0, 2048), [[-1, 16], [1, 128]], 0, 0)
+    fill(v("ONE"), 1.0)
+    fill(v("INFO"), 0.0)
+    asel(v("SHF"), v("ONE"), [[-1, 128]], OP.is_equal, 0.0, -1, 1)
+    asel(v("ID"), v("ONE"), [[-1, 128]], OP.is_equal, 0.0, 0, 1)
+    ts(v("PI", 1, 2), PIc, 4, OP.arith_shift_right)
+    ts(v("PI", 2, 3), PIc, 15, OP.bitwise_and)
+    G16, GB, II, GB2 = col(0), col(1), col(2), col(3)
+    ts(GB, v("PI", 1, 2), 4096.0, OP.mult)
+    ts(v("VC"), v("VG"), GB, OP.subtract)
+    ts(G16, v("PI", 1, 2), 16.0, OP.mult)
+    ts(GB2, v("PI", 1, 2), 8192.0, OP.mult)
+    copy(II, v("PI", 2, 3))
+    for t in range(RO + 1):
+        fill(v("X%d" % t, 4096, 4112), 0.0)
+    fill(v("ZERO"), 0.0)
+    fill(v("ROW"), 0.0)
+    fill(v("ROW2"), 0.0)
+    SZ = v("SZ", 0, 256)
+    SZ1 = v("SZ", 1, 257)
+
+    def edge(name):
+        mm(v("b6", 0, 1), v("SHF"), v(name, 0, 1), True, True)
+        copy(v(name, 256, 257), v("b6", 0, 1))
+
+    def tables():
+        ts(v("T1"), SZ, -1.0, OP.add)
+        ts(v("KD"), v("T1"), 1.0, OP.min)
+        edge("SZ")
+        tt(v("TW"), SZ1, v("T1"), OP.is_lt)
+        tt(v("T3"), v("KD"), v("VC"), OP.add)
+        tt(v("T2"), v("TW"), SZ1, OP.mult)
+        tt(v("T4"), v("T2"), v("T3"), OP.add)
+        copy(v("B0"), v("T4"))
+        rows("INFO", 0, 1, "B0")
+        tt(v("B1"), v("T4"), v("B0"), OP.subtract)
+        rows("INFO", 1, 1, "B1")
+
+    def tables2():
+        tt(v("EF", 0, 256), v("VC"), v("T1"), OP.add)
+        mm(v("b6", 0, 1), v("SHF"), v("EF", 0, 1), True, True)
+        tt(v("EG"), v("VG"), SZ, OP.add)
+        ts(v("HF"), v("KD"), -1.0, OP.mult, 1.0, OP.add)
+        tt(v("TWE"), v("TW"), v("EG"), OP.mult)
+        tt(v("KDE"), v("KD"), v("EG"), OP.mult)
+
+    tt(SZ, v("EI"), v("VC"), OP.subtract)
+    tables()
+    ts(v("LP"), bg(0, 2048), G16, OP.is_equal)
+
+    def weight(name, k, terms, onv):
+        c = col(k)
+        for n, (row, wgt) in enumerate(terms):
+            if n == 0:
+                ts(c, II, float(row), OP.is_equal, float(wgt), OP.mult)
+            else:
+                ts(col(31), II, float(row), OP.is_equal, float(wgt), OP.mult)
+                tt(c, c, col(31), OP.add)
+        if onv:
+            ts(v(name), v("LP"), c, OP.mult)
+        else:
+            act(v(name), v("LP"), ACT.Copy, None, c)
+    weight("LB", 8, [(0, 1), (1, 1)], True)
+    act(v("LN"), v("LP"), ACT.Copy, None, -1.0)
+    ts(col(4), II, 14.0, OP.is_ge, 512.0, OP.mult)
+    ts(v("REM"), v("VC"), col(4), OP.subtract, -1.0, OP.mult)
+    ts(v("REM"), v("REM"), 3584.0, OP.add)
+    iota(v("SELH"), [[0, 2048]], 1, 0)
+    iota(v("TRI"), [[16, 8], [0, 16]], 0, 0)
+    iota(v("QW"), [[16, 256]], 0, 1)
+    ts(v("QW"), v("QW"), G16, OP.subtract)
+    ts(v("TRI"), v("TRI"), G16, OP.is_equal)
+    asel(v("TRI"), v("TRI"), [[1, 128]], OP.is_gt, 0.0, 0, -1)
+    ts(v("TRI2"), v("TRI"), 2.0, OP.mult)
+    asel(v("SELH"), v("SELH"), [[128, 4], [-1, 4], [-4, 128]], OP.is_equal, 0.0, 0, 1)
+    iota(v("GH"), [[0, 4128]], 0, 0)
+    iota(v("BIG", 0, 4096), [[0, 16], [1, 16], [0, 16]], 0, -1)
+    iota(v("VPAY"), [[1, 16], [0, 16], [16, 16]], 0, 0)
+    iota(v("GV"), [[0, 4096]], 0, 0)
+    for name, k in (("IDB", 1.0), ("NIDB", -1.0), ("ID2B", 2.0), ("ID64", 65536.0), ("NID", -1.0)):
+        act(v(name), v("ID"), ACT.Copy, None, k)
+    ts(v("CK"), v("VC"), GB2, OP.subtract)
+    ts(v("CV"), v("VC"), -1.0, OP.mult, 12288.0, OP.add)
+
+    IG = (0, 1024)
+    TA = (2048, 3072)
+    RA = (9216, 4096)
+    TB = (5120, 6144)
+    RB = (7168, 8192)
+
+    for t in range(RO):
+        X, XN = "X%d" % t, "X%d" % (t + 1)
+        AFn = ["AF0", "AF1"]
+
+        def w64(name, h):
+            return v(name, 64 * h, 64 * h + 64)
+
+        def big(base, h):
+            return bg(base[h], base[h] + 1024)
+
+        def info(h):
+            act(big(IG, h), ind(v("INFO", 0, 4112), w64("AL", h)), ACT.Copy)
+            bwd(v("b%d" % h, 0, 64), "LB", "BIG", BO + IG[h], 64)
+
+        def first_kid(h):
+            tt(big(TA, h), ind(v(X), w64("AL", h)), v("WP", 1024 * h, 1024 * h + 1024), OP.subtract)
+            act(big(RA, h), big(TA, h), ACT.Relu, None, -1.0)
+
+        def first_sum(h):
+            bwd(v("b%d" % (2 + h), 0, 64), "LN", "BIG", BO + RA[h], 64, True, False)
+
+        def second_kid(h, s):
+            copy(w64("BL", h), v("b%d" % h, 0, 64))
+            tt(big(TB, h), ind(v(X), w64("BL", h)), v("WP", 1024 * h, 1024 * h + 1024), OP.subtract)
+            act(big(RB, h), big(TB, h), ACT.Relu, None, -1.0)
+            bwd(v("b%d" % (2 + h), 0, 64), "LP", "BIG", BO + RB[h], 64, False, True)
+            tt(w64("MM", h), v("b%d" % h, 0, 64), w64(AFn[s % 2], h), OP.min)
+
+        def decide(h, s):
+            ts(w64("GQ", h), v("b%d" % (2 + h), 0, 64), 0.0, OP.is_gt)
+            tt(w64("GQ", h), w64("GQ", h), v("b%d" % h, 0, 64), OP.mult)
+            tt(w64("NV", h), w64("GQ", h), w64("MM", h), OP.max)
+            if s < 3:
+                ts(w64("AL", h), w64("NV", h), 1.0, OP.add)
+                ts(w64(AFn[(s + 1) % 2], h), w64("NV", h), 1.0, OP.add)
+            if s == 1:
+                tt(w64("MISS", h), w64(AFn[0], h), w64(AFn[1], h), OP.is_le)
+                ts(w64("MISS", h), w64("MISS", h), 8192.0, OP.mult)
+
+        def starts(t):
+            s0 = v("STI", 128 * t, 128 * t + 128)
+            ts(v("AL"), s0, 1.0, OP.add)
+            ts(v("AF0"), s0, 1.0, OP.add)
+        if t == 0:
+            starts(0)
+        info(0)
+        info(1)
+        for s in range(4):
+            first_kid(0)
+            first_sum(0)
+            if s > 0:
+                decide(1, s - 1)
+                info(1)
+            else:
+                first_kid(1)
+                first_sum(1)
+            second_kid(0, s)
+            if s > 0:
+                first_kid(1)
+                first_sum(1)
+            second_kid(1, s)
+            decide(0, s)
+            if s < 3:
+                info(0)
+        decide(1, 3)
+        tt(v("CODE"), v("NV"), v("MISS"), OP.add)
+        tr(v("b7", 0, 128), v("CODE"), v("ID"))
+        copy(v("TI"), v("b7", 0, 128))
+        ts(v("TLO"), v("TI"), 63, OP.bitwise_and)
+        copy(v("LOb"), v("TLO"))
+        ts(v("THI"), v("TI"), 6, OP.arith_shift_right)
+        copy(v("HIb"), v("THI"))
+        for k in range(64):
+            ts(bg(128 * k, 128 * k + 128), v("HIb"), float(k), OP.is_equal)
+            if NLO + k < 64:
+                n = NLO + k
+                act(bg(8192 + 128 * n, 8192 + 128 * n + 128), v("LOb"), ACT.Sign, 0.5 - n)
+        for n in range(NLO):
+            ts(bg(8192 + 128 * n, 8192 + 128 * n + 128), v("LOb"), float(n), OP.is_equal)
+        fill(bg(16384, 16512), -1.0)
+        mm(v("b0", 0, 256), v("ID"), v("CK"), True, False)
+        mm(v("b1", 0, 256), v("ID"), v("CV"), True, False)
+        mm(v("b2", 0, 256), v("ID"), v("VG"), True, False)
+        mm(v("b3", 0, 256), v("ID"), SZ, True, False)
+        tables2()
+        if t < RO - 1:
+            starts(t + 1)
+
+        def payload(a, b):
+            if t == 0:
+                tt(v("VPAY", a, b), v("VPAY", a, b), v("BIG", a, b), OP.add)
+        if t == 0:
+            weight("L1", 9, [(0, 1), (1, 1), (2, 8192)], False)
+            weight("L2", 10, [(3, 1), (4, 1)], False)
+            weight("L3", 11, [(0, 4096), (1, 4096), (2, 0.5), (3, 0.5)], False)
+            weight("L4", 13, [(4, 1), (5, 1)], False)
+            ts(v("BIG", 0, 4096), v("BIG", 0, 4096), G16, OP.add, 0.0, OP.is_ge)
+        payload(0, 2048)
+        for gg in range(8):
+            for i in range(16):
+                c = 16 * gg + i
+                mm(v("b4", gg // 2, 260, 4, (64 * (gg % 2), 64 * (gg % 2) + 64, 1)), bg(c, 8192, 128), bg(8192 + c, 16512, 128), i == 0, i == 15)
+        copy(v("EF", 256, 257), v("b6", 0, 1))
+        copy(v("EL", 0, 257), v("EF", 0, 257))
+        copy(v("T1"), v("b4", 4, 260))
+        copy(v("HB", 0, 4 * NLO), v("b4", 0, 4 * NLO))
+        tt(v("HB", 4 * NLO, 256), v("b4", 4 * NLO, 256), v("T1", 4 * NLO, 256), OP.subtract)
+        for cc in range(4):
+            for gh in range(4):
+                mm(v("b5", 64 * cc, 64 * cc + 64), v("SELH", 128 * (4 * gh + cc), 128 * (4 * gh + cc) + 128), v("HB", gh, 256, 4), gh == 0, gh == 3)
+        HM = v("HM", 0, 256)
+        tt(HM, v("b5", 0, 256), v("HF"), OP.min)
+        red(v("RC", 0, 1), HM, OP.add)
+        mm(v("b6", 2, 3), v("TRI"), v("RC", 0, 1), True, True)
+        act(v("HMb"), HM, ACT.Copy)
+        rows("GH", 2, 15, "HMb")
+        scan(v("HINC"), v("ZERO"), HM, v("b6", 2, 3), OP.add, OP.add)
+        copy(v("H0"), v("HINC"))
+        rows("GH", 0, 16, "H0")
+        tt(v("H1"), v("HINC"), v("H0"), OP.subtract)
+        rows("GH", 1, 16, "H1")
+        edge("HM")
+        tt(v("HK"), v("HM", 1, 257), v("KDE"), OP.mult)
+        mm(v("b2", 0, 256), v("ID64"), v("HMb"), False, True)
+        mm(v("b1", 0, 256), v("ID2B"), v("H0"), False, False)
+        mm(v("b1", 0, 256), v("ID2B"), v("H1"), False, True)
+        tt(v("T2"), HM, v("b1", 0, 256), OP.mult)
+        payload(2048, 2816)
+        mm(v("b0", 0, 256), v("NIDB"), v("H0"), False, False)
+        mm(v("b0", 0, 256), v("NIDB"), v("H1"), False, False)
+        for k in (0, 2, 1, 3):
+            w = 65 if k == 3 else 64
+            o, i = v("G1", 1024 * k, 1024 * k + 16 * w), ind(v("GH", 16, 4112), v("EL", 64 * k, 64 * k + w))
+            if k < 2:
+                copy(o, i)
+            else:
+                act(o, i, ACT.Copy)
+            bwd(v("b7", 64 * k, 64 * k + w), "L1", "G1", 1024 * k, w)
+        mm(v("b0", 0, 256), v("ID"), v("T2"), False, True)
+        mm(v("b3", 0, 256), v("IDB"), v("H0"), False, False)
+        mm(v("b3", 0, 256), v("IDB"), v("H1"), False, False)
+        mm(v("b3", 0, 256), v("NIDB"), v("HMb"), False, False)
+        payload(2816, 4096)
+        iota(v("BIG", 0, 4096), [[0, 4096]], 0, 0)
+        ts(v("HME", 0, 257), v("b7", 0, 257), 8192.0, OP.is_ge)
+        tt(v("T4"), v("TWE"), v("HME", 1, 257), OP.mult)
+        tt(v("T4"), v("T4"), v("HK"), OP.max)
+
+        def maxscan(out, src, rc, ini, fillers):
+            red(v("RC", rc, rc + 1), src, OP.max)
+            tr(v("b6", 128, 256, 1, ONEROW), v("RC", rc, rc + 1), v("ID"))
+            fillers[0]()
+            scan(v("ROW", 1, 129, 1, ONEROW), v("ROW2", 0, 128, 1, ONEROW), v("b6", 128, 256, 1, ONEROW), 0.0, OP.max, OP.max)
+            mm(v("b6", ini, ini + 1), v("ROW", 0, 128, 1, ONEROW), v("ID", 0, 1, 1, ONEROW), True, True)
+            fillers[1]()
+            scan(out, src, src, v("b6", ini, ini + 1), OP.max, OP.max)
+
+        def f1():
+            ts(v("HEC"), v("HME", 0, 256), -8192.0, OP.mult)
+
+        def f2():
+            tt(v("HEC"), v("HEC"), v("b7", 0, 256), OP.add)
+        maxscan(v("RS", 1, 257), v("T4"), 1, 4, (f1, f2))
+        tt(v("KI"), v("RS", 1, 257), v("b2", 0, 256), OP.is_gt)
+        red(v("RC", 2, 3), v("KI"), OP.add)
+        mm(v("b6", 6, 7), v("ID"), GB2, True, False)
+        mm(v("b6", 6, 7), v("TRI2"), v("RC", 2, 3), False, True)
+        copy(v("RS", 0, 1), v("b6", 4, 5))
+        tt(v("OX"), v("RS", 0, 256), v("VG"), OP.is_le)
+        scan(v("J2", 1, 257), v("KI"), v("KI"), v("b6", 6, 7), OP.add, OP.add)
+        copy(v("J2", 0, 1), v("b6", 6, 7))
+        act(v("J0"), v("J2", 1, 257), ACT.Copy)
+        rows("GH", 3, 16, "J0")
+        tt(v("T5"), v("J2", 0, 256), v("OX"), OP.mult)
+
+        def f3():
+            tt(v("J1"), v("J2", 1, 257), v("J0"), OP.subtract)
+            rows("GH", 4, 16, "J1")
+
+        def f4():
+            ts(v("OUT"), v("KI"), -1.0, OP.mult, 1.0, OP.add)
+        maxscan(v("T6"), v("T5"), 3, 8, (f3, f4))
+        tt(v("POS"), v("b0", 0, 256), v("T6"), OP.add)
+        copy(v("OFF"), v("POS"))
+        act(v("P0"), v("POS"), ACT.Copy)
+        rows("GV", 0, 0, "P0")
+        mm(v("b1", 0, 256), v("IDB"), v("J0"), True, False)
+        mm(v("b1", 0, 256), v("IDB"), v("J1"), False, False)
+        mm(v("b1", 0, 256), v("NID"), v("T6"), False, True)
+        act(v("S20"), v("b1", 0, 256), ACT.Copy)
+        rows("GV", 2, 0, "S20")
+        tt(v("P1"), v("POS"), v("P0"), OP.subtract)
+        rows("GV", 1, 0, "P1")
+        copy(ind(v("BIG", 0, 20480), v("OFF", 0, 192)), v("VPAY", 0, 3072))
+        mm(v("b3", 0, 256), v("NID"), v("HEC"), False, True)
+        mm(v("b5", 0, 256), v("NID"), v("J2", 0, 256), True, False)
+        for k in range(4):
+            act(v("G1", 1024 * k, 1024 * k + 1024), ind(v("GH", 16, 4112), v("EL", 64 * k, 64 * k + 64)), ACT.Copy)
+            bwd(v("b5", 64 * k, 64 * k + 64), "L2", "G1", 1024 * k, 64, False, k == 3)
+        tt(v("S21"), v("b1", 0, 256), v("S20"), OP.subtract)
+        rows("GV", 3, 0, "S21")
+        tt(v("T5"), v("OUT"), v("b5", 0, 256), OP.mult)
+        tt(v("T5"), v("T5"), v("b3", 0, 256), OP.add)
+        act(v("Z0"), v("T5"), ACT.Copy)
+        rows("GV", 4, 0, "Z0")
+        tt(v("Z1"), v("T5"), v("Z0"), OP.subtract)
+        rows("GV", 5, 0, "Z1")
+        copy(ind(v("BIG", 0, 20480), v("OFF", 192, 256)), v("VPAY", 3072, 4096))
+        for k in range(4):
+            a = 1024 * k
+            scan(v("VLS", a, a + 1024), v("BIG", a, a + 1024), v("BIG", a, a + 1024), 0.0 if k == 0 else v("VLS", a - 1, a), OP.max, OP.max)
+            bwd(v("b%d" % k, 0, 64), "LP", "VLS", a, 64)
+            if k == 2:
+                ts(v("VLL", 0, 64), v("b0", 0, 64), -1.0, OP.add)
+        for k in range(1, 3):
+            ts(v("VLL", 64 * k, 64 * k + 64), v("b%d" % k, 0, 64), -1.0, OP.add)
+
+        def gat(k, out, win):
+            i = ind(win, v("VLL", 64 * k, 64 * k + 64))
+            if k < 2:
+                act(out, i, ACT.Copy)
+            else:
+                copy(out, i)
+        for k in (0, 2, 1, 3):
+            a = 1024 * k
+            if k == 3:
+                ts(v("VLL", 192, 256), v("b3", 0, 64), -1.0, OP.add)
+            gat(k, bg(12288 + a, 12288 + a + 1024), v("GV"))
+            bwd(v("b4", 64 * k, 64 * k + 64), "L3", "BIG", BO + 12288 + a, 64)
+        for k in (0, 2, 1, 3):
+            gat(k, bg(1024 * k, 1024 * k + 1024), v(X))
+        act(bg(4096, 6144), bg(0, 2048), ACT.Relu, -1.0)
+        act(bg(6144, 8192), bg(2048, 4096), ACT.Relu, -1.0)
+        copy(v("PKI"), v("b4", 0, 256))
+        ts(v("PPI"), v("PKI"), 12, OP.arith_shift_right)
+        ts(v("PSI"), v("PKI"), 4095, OP.bitwise_and)
+        tt(v("T1"), v("QW"), v("PPI"), OP.subtract)
+        tt(v("T2"), v("T1"), v("PSI"), OP.is_gt)
+        ts(v("T3"), v("T1"), 0.0, OP.is_gt)
+        tt(v("T3"), v("T3"), v("T2"), OP.add)
+        tt(v("T4"), v("T3"), v("PSI"), OP.mult)
+        tt(v("T4"), v("QW"), v("T4"), OP.subtract)
+        copy(v("QL"), v("T4"))
+        dst = T.cores[(rank + 1) % len(T.cores)]
+        src = T.cores[(rank - 1) % len(T.cores)]
+
+        def send(name, to, rsem, lsem):
+            rid, pid, _se = topo.addr(dst)
+            add("G", [v(name)], [], lambda: g.remote_dma(ap(to), ap(v(name)), T.sem[rsem], T.sem[lsem], pid, rid, topo.mask(core, dst)),
+                lsem, len(topo.engines(core, dst)))
+            add("R", [], [to], None, rsem, len(topo.engines(src, core)))
+
+        def sizes(out, lo, hi, onv):
+            i = ind(bg(12288, 16384), v("QL", lo // 16, hi // 16))
+            if onv:
+                copy(out, i)
+            else:
+                act(out, i, ACT.Copy)
+
+        def szc(i):
+            s = v("SZB", 256 * i, 256 * i + 256) if i < 14 else v("LZ%d" % t, 256 * (i - 14), 256 * (i - 14) + 256)
+            mm(v("b7", 0, 256), v("L4", 128 * i, 128 * i + 128), s, i == 0, i == 15)
+
+        def xl(lo, hi):
+            return ind(bg(0, 12288), v("XL", lo // 16, hi // 16))
+        sizes(v("SZS"), 3584, 4096, False)
+        send("SZS", v("LZ%d" % t), "rz%d" % t, "lz%d" % t)
+        for k in (0, 3, 1, 4, 2, 5, 6):
+            sizes(v("SZB", 512 * k, 512 * k + 512), 512 * k, 512 * k + 512, k < 3)
+            szc(2 * k)
+            szc(2 * k + 1)
+            if k == 0:
+                ts(v("T3"), v("T3"), 4096.0, OP.mult)
+                tt(v("T5"), v("T3"), v("T4"), OP.add)
+                copy(v("XL"), v("T5"))
+        szc(14)
+        szc(15)
+        ts(bg(8192, 12288), bg(0, 4096), 2.0, OP.subtract, 0.0, OP.max)
+        act(v("XS"), xl(3584, 4096), ACT.Copy)
+        send("XS", v(XN, 3584, 4096), "rx%d" % t, "lx%d" % t)
+        if t < RO - 1:
+            act(v(XN, 1024, 3584), xl(1024, 3584), ACT.Copy)
+            tt(SZ, v("b7", 0, 256), v("REM"), OP.min)
+            tables()
+            copy(v(XN, 0, 1024), xl(0, 1024))
+        else:
+            copy(v(XN, 0, 1024), xl(0, 1024))
+            dma(v("y", 0, 1024), v(XN, 0, 1024))
+            act(v(XN, 2048, 3584), xl(2048, 3584), ACT.Copy)
+            copy(v(XN, 1024, 2048), xl(1024, 2048))
+            dma(v("y", 1024, 2048), v(XN, 1024, 2048))
+            tt(SZ, v("b7", 0, 256), v("REM"), OP.min)
+            tt(v("T1"), v("VC"), SZ, OP.add)
+            dma(v("y", 2048, 3584), v(XN, 2048, 3584))
+            dma(v("ye", 0, 4096, 1, (0, 8, 1)), v("T1"))
+            dma(v("y", 3584, 4096), v(XN, 3584, 4096))
+
+    qidx = {}
+    hist = {}
+    known = {}
+    need = set()
+    for k, o in enumerate(ops):
+        q = o["q"]
+        o["k"] = k
+        if o["sem"] is None:
+            o["tok"] = (q, qidx.get(q, 0))
+            qidx[q] = qidx.get(q, 0) + 1
+        else:
+            o["tok"] = ("*" + o["sem"], 0)
+        deps = []
+        for wr, lst in ((0, o["r"]), (1, o["w"])):
+            for x in lst:
+                name = x[0]
+                psum = name[0] == "b" and len(name) == 2
+                m = pm(x[1])
+                keep = []
+                for h in hist.get(name, []):
+                    ho, hw, hx = h
+                    over = (pm(hx[1]) & m) and hx[2] < x[3] and x[2] < hx[3]
+                    same = ho["q"] == q and o["sem"] is None and ho["sem"] is None
+                    if psum and not same:
+                        deps.append(ho)
+                    elif psum and q == "P":
+                        pass
+                    elif over and (wr or hw):
+                        deps.append(ho)
+                    if wr and not psum and hx[2] >= x[2] and hx[3] <= x[3] and (pm(hx[1]) & ~m) == 0 and x[4] == 1:
+                        continue
+                    keep.append(h)
+                if psum and len(keep) > 200:
+                    keep = keep[-200:]
+                hist[name] = keep
+        kn = known.setdefault(q if q != "R" else ("R", k), {})
+        waits = []
+        best = {}
+        for ho in deps:
+            tq, ti = ho["tok"]
+            if tq not in best or best[tq]["tok"][1] < ti:
+                best[tq] = ho
+        for ho in sorted(best.values(), key=lambda z: -z["k"]):
+            tq, ti = ho["tok"]
+            if kn.get(tq, -1) >= ti:
+                continue
+            waits.append(ho)
+            need.add(ho["tok"])
+            for a, b in ho["kn"].items():
+                if kn.get(a, -1) < b:
+                    kn[a] = b
+            kn[tq] = max(kn.get(tq, -1), ti)
+        o["waits"] = waits
+        o["kn"] = dict(kn)
+        for wr, lst in ((0, o["r"]), (1, o["w"])):
+            for x in lst:
+                hist.setdefault(x[0], []).append((o, wr, x))
+    cnt = {}
+    eng_of = {"V": g.vector, "S": g.scalar, "P": g.tensor, "G": g, "Y": g.sync}
+    sem_of = {"V": "sV", "S": "sS", "P": "sP", "G": "sG"}
+    for o in ops:
+        q = o["q"]
+        if q == "R":
+            o["val"] = o["n"]
+            continue
+        e = eng_of[q]
+        for ho in o["waits"]:
+            e.wait_ge(T.sem[ho["sem"] or sem_of[ho["q"]]], ho["val"])
+        r = o["call"]()
+        if o["sem"] is not None:
+            o["val"] = o["n"]
+            if q != "G":
+                r.then_inc(T.sem[o["sem"]], o["n"])
+        elif o["tok"] in need:
+            cnt[q] = cnt.get(q, 0) + 1
+            o["val"] = cnt[q]
+            r.then_inc(T.sem[sem_of[q]], 1)
+    for q in ("V", "S", "P", "G"):
+        if cnt.get(q, 0):
+            g.wait_ge(T.sem[sem_of[q]], cnt[q])
+    for o in ops:
+        if o["sem"] is not None:
+            g.wait_ge(T.sem[o["sem"]], o["n"])

@@ -5,64 +5,61 @@ import comms_topo
 
 RO = 3
 NLO = 20
+SL = 4224
+BIGW = 8192.0
 
 SCRATCH = {
     "BIG": ("sbuf", [128, 20736], "bfloat16"),
-    "VPAY": ("sbuf", [128, 4096], "bfloat16"),
+    "XX": ("sbuf", [128, 5 * SL], "bfloat16"),
+    "QB": ("sbuf", [128, 4096], "float32"),
     "WP": ("sbuf", [128, 2048], "bfloat16"),
     "INFO": ("sbuf", [128, 4112], "bfloat16"),
     "GH": ("sbuf", [128, 4128], "bfloat16"),
-    "GV": ("sbuf", [128, 4096], "bfloat16"),
-    "G1": ("sbuf", [128, 4112], "bfloat16"),
-    "VLS": ("sbuf", [128, 4096], "bfloat16"),
-    "SZB": ("sbuf", [128, 3584], "bfloat16"),
+    "G": ("sbuf", [128, 4096], "bfloat16"),
+    "GQ": ("sbuf", [128, 4096], "bfloat16"),
     "XS": ("sbuf", [128, 512], "bfloat16"),
-    "SZS": ("sbuf", [128, 512], "bfloat16"),
-    "HB": ("sbuf", [128, 256], "bfloat16"),
+    "LX": ("sbuf", [128, 512], "bfloat16"),
+    "SEL": ("sbuf", [128, 1024], "bfloat16"),
     "STI": ("sbuf", [128, 384], "int32"),
     "EI": ("sbuf", [128, 256], "int32"),
+    "FI": ("sbuf", [128, 256], "int32"),
     "AL": ("sbuf", [128, 128], "uint16"),
     "BL": ("sbuf", [128, 128], "uint16"),
     "EL": ("sbuf", [128, 264], "uint16"),
-    "OFF": ("sbuf", [128, 256], "uint16"),
-    "VLL": ("sbuf", [128, 256], "uint16"),
-    "QL": ("sbuf", [128, 256], "uint16"),
-    "XL": ("sbuf", [128, 256], "uint16"),
+    "OFF": ("sbuf", [128, 16], "uint16"),
     "PI": ("sbuf", [128, 4], "int32"),
-    "COL": ("sbuf", [128, 32], "float32"),
-    "ROW": ("sbuf", [128, 160], "float32"),
-    "ROW2": ("sbuf", [128, 160], "float32"),
+    "COL": ("sbuf", [128, 48], "float32"),
     "RC": ("sbuf", [128, 8], "float32"),
+    "PW": ("sbuf", [128, 544], "float32"),
+    "P0": ("sbuf", [128, 288], "float32"),
+    "LB0": ("sbuf", [128, 144], "float32"),
+    "KS": ("sbuf", [128, 64], "bfloat16"),
 }
-for _t in range(RO + 1):
-    SCRATCH["X%d" % _t] = ("sbuf", [128, 4112], "bfloat16")
+for _n in ("ML", "UL", "QL", "XL"):
+    SCRATCH[_n] = ("sbuf", [128, 256], "uint16")
 for _t in range(RO):
     SCRATCH["LZ%d" % _t] = ("sbuf", [128, 512], "bfloat16")
-for _n in ("LP", "LN", "LB", "L1", "L2", "L3", "L4", "SELH"):
-    SCRATCH[_n] = ("sbuf", [128, 2048], "bfloat16")
-for _n in ("ID", "TRI", "TRI2", "SHF", "ONE", "CODE", "MISS", "NV", "MM", "GQ", "NID", "AF0", "AF1"):
+for _n in ("LP", "LN", "L1", "LI", "LM1", "LM2", "LE", "LH", "LJ", "LD", "LS", "LV", "LZ"):
+    SCRATCH[_n] = ("sbuf", [128, 144], "bfloat16")
+for _n in ("ID", "IDM", "TRI", "SHF", "ONE", "MISS", "TY", "Y0", "Y1", "Y2", "Y3", "Y4"):
     SCRATCH[_n] = ("sbuf", [128, 128], "float32")
-for _n in ("PKI", "PPI", "PSI"):
-    SCRATCH[_n] = ("sbuf", [128, 256], "int32")
-for _n in ("TI", "THI", "TLO"):
-    SCRATCH[_n] = ("sbuf", [128, 128], "int32")
-for _n in ("HIb", "LOb", "IDB", "NIDB", "ID2B", "ID64"):
+for _n in ("HIb", "LOb", "IDB", "NIDB", "ID2B", "IDBIG", "IDN64", "IDA", "NIDA", "SHFB"):
     SCRATCH[_n] = ("sbuf", [128, 128], "bfloat16")
-for _n in ("VG", "VC", "REM", "QW", "ZERO", "KD", "TW", "TWE", "HF", "EG", "HK", "HINC", "HEC", "KDE", "CK", "CV",
-           "OX", "OUT", "KI", "POS", "T1", "T2", "T3", "T4", "T5", "T6"):
+for _n in ("I16", "DM", "DO", "DG", "O16"):
+    SCRATCH[_n] = ("sbuf", [128, 16], "float32")
+for _n in ("VC", "REM", "QW", "SZ", "HF", "TWE", "KDE", "HK", "OX", "OUT", "LQ", "T6", "SF", "SG", "T1", "T2", "T4", "T5"):
     SCRATCH[_n] = ("sbuf", [128, 256], "float32")
-for _n in ("SZ", "HM", "HME", "RS", "J2", "EF"):
+for _n in ("HL", "RL", "RS", "JL"):
     SCRATCH[_n] = ("sbuf", [128, 264], "float32")
-for _n in ("B0", "B1", "H0", "H1", "HMb", "J0", "J1", "P0", "P1", "Z0", "Z1", "S20", "S21"):
+for _n in ("HB", "CP", "TWO", "KD", "TW", "HM", "KI", "CC", "M0", "M1", "H0", "H1", "J0", "J1", "U0", "U1", "Z0", "Z1", "V0", "V1", "Q0", "Q1"):
     SCRATCH[_n] = ("sbuf", [128, 256], "bfloat16")
 for _n in range(8):
     SCRATCH["b%d" % _n] = ("psum", [128, 512], "float32")
 
-SEMAPHORES = (["sV", "sS", "sP", "sG"] + ["d%d" % _k for _k in range(72)]
+SEMAPHORES = (["sV", "sS", "sP", "sG"] + ["d%d" % _k for _k in range(80)] + ["a%d" % _k for _k in range(2 * RO)]
               + ["%s%d" % (_a, _k) for _a in ("rx", "rz", "lx", "lz") for _k in range(RO)])
 
 ALL = (0, 128, 1)
-ONEROW = (0, 1, 1)
 ACT = ActivationFunctionType
 OP = AluOpType
 
@@ -74,6 +71,8 @@ def v(name, c0=0, c1=None, cs=1, p=ALL):
 
 
 BO = 4096
+VLS = 12544
+CMP = 16640
 
 
 def bg(c0, c1, cs=1):
@@ -112,7 +111,7 @@ def rank_program(g, core, T, topo):
                 out.append(x)
         return out
 
-    def add(q, reads, writes, call, sem=None, n=1):
+    def add(q, reads, writes, call, sem=None, n=1, own=True):
         rd = []
         for x in reads:
             flat(x, rd)
@@ -123,7 +122,7 @@ def rank_program(g, core, T, topo):
                 rd.append(x[2])
             else:
                 wr.append(x)
-        ops.append({"q": q, "r": rd, "w": wr, "call": call, "sem": sem, "n": n})
+        ops.append({"q": q, "r": rd, "w": wr, "call": call, "sem": sem, "n": n, "own": own})
 
     def ap(x):
         if not isinstance(x, tuple):
@@ -151,6 +150,9 @@ def rank_program(g, core, T, topo):
     def scan(out, d0, d1, init, op0, op1):
         add("V", [d0, d1, init], [out], lambda: g.vector.tensor_tensor_scan(ap(out), ap(d0), ap(d1), ap(init), op0, op1))
 
+    def vtr(out, i):
+        add("V", [i], [out], lambda: g.vector.transpose(ap(out), ap(i)))
+
     def fill(out, c):
         add("V", [], [out], lambda: g.vector.memset(ap(out), c))
 
@@ -158,17 +160,14 @@ def rank_program(g, core, T, topo):
         def call():
             kw = {}
             if bias is not None:
-                kw["bias"] = bias
+                kw["bias"] = ap(bias)
             if scale is not None:
                 kw["scale"] = ap(scale)
             return g.scalar.activation(ap(out), ap(i), func, **kw)
-        add("S", [i, scale], [out], call)
+        add("S", [i, scale, bias], [out], call)
 
     def mm(out, l, r, start, stop):
         add("P", [l, r], [out], lambda: g.tensor.matmul(ap(out), ap(l), ap(r), start, stop))
-
-    def tr(out, i, idn):
-        add("P", [i, idn], [out], lambda: g.tensor.transpose(ap(out), ap(i), ap(idn)))
 
     def iota(out, pattern, base, cm, small=True):
         if small:
@@ -179,123 +178,182 @@ def rank_program(g, core, T, topo):
     def asel(out, i, pattern, cop, fillv, base, cm):
         add("G", [i], [out], lambda: g.affine_select(ap(out), ap(i), pattern, cop, fillv, base, cm))
 
-    nd = [0]
+    nd = [0, 0]
 
     def dma(out, i):
         sem = "d%d" % nd[0]
         nd[0] += 1
         add("Y", [i], [out], lambda: g.sync.dma_start(ap(out), ap(i)), sem, 16)
 
+    def dma_add(out, i):
+        sem = "a%d" % nd[1]
+        nd[1] += 1
+        add("G", [i, out], [out], lambda: g.dma_start(ap(out), ap(i), accum_op=OP.add, max_dma_last_dim=4096), sem, 16)
+
     def rows(name, r, c0, src):
         dma(v(name, c0, c0 + 4096, 1, (r, 128, 16)), v(src))
 
+    def blk(lname, i):
+        return v(lname, 15 - i, 143 - i)
+
     def bwd(out, lname, src, c0, k, first=True, last=True):
         for i in range(16):
-            mm(out, v(lname, 128 * i, 128 * i + 128), v(src, c0 + i, c0 + 16 * k, 16), first and i == 0, last and i == 15)
+            mm(out, blk(lname, i), v(src, c0 + i, c0 + 16 * k, 16), first and i == 0, last and i == 15)
 
-    dma(v("EI"), v("ends", 0, 4096, 1, (0, 8, 1)))
-    dma(v("STI"), v("start", 0, 384))
-    dma(v("X0", 0, 4096), v("x"))
-    dma(v("WP"), v("w", 0, 2048))
-    PIc = v("PI", 0, 1)
+    def gather(onv, out, win, lst, relu=False):
+        if onv and relu:
+            ts(out, ind(win, lst), 0.0, OP.max)
+        elif onv:
+            copy(out, ind(win, lst))
+        else:
+            act(out, ind(win, lst), ACT.Relu if relu else ACT.Copy)
+
+    def xs(k, a=0, b=4096):
+        return v("XX", SL * k + a, SL * k + b)
 
     def col(k):
         return v("COL", k, k + 1)
+
+    def ps(k, a=0, b=256):
+        return v("b%d" % k, a, b)
+
+    dma(v("EI"), v("ends", 0, 4096, 1, (0, 8, 1)))
+    dma(v("STI", 0, 128), v("start", 0, 128))
+    dma(xs(0), v("x"))
+    dma(v("WP", 0, 1024), v("w", 0, 1024))
+    PIc = v("PI", 0, 1)
     iota(PIc, [[0, 1]], 0, 1, False)
-    iota(v("VG"), [[1, 256]], 0, 256)
-    iota(bg(0, 2048), [[-1, 16], [1, 128]], 0, 0)
+    iota(v("VC"), [[1, 256]], 0, 256)
     fill(v("ONE"), 1.0)
-    fill(v("INFO"), 0.0)
-    asel(v("SHF"), v("ONE"), [[-1, 128]], OP.is_equal, 0.0, -1, 1)
     asel(v("ID"), v("ONE"), [[-1, 128]], OP.is_equal, 0.0, 0, 1)
+    asel(v("SHF"), v("ONE"), [[-1, 128]], OP.is_equal, 0.0, -1, 1)
+    iota(v("LB0"), [[1, 144]], -15, 0)
+    iota(v("I16"), [[1, 16]], 0, 0)
+    fill(v("TWO"), 2.0)
     ts(v("PI", 1, 2), PIc, 4, OP.arith_shift_right)
     ts(v("PI", 2, 3), PIc, 15, OP.bitwise_and)
-    G16, GB, II, GB2 = col(0), col(1), col(2), col(3)
+    ts(v("PI", 3, 4), v("PI", 1, 2), 1, OP.bitwise_and)
+    G16, GB, II, AA, COFF = col(0), col(1), col(2), col(3), col(5)
     ts(GB, v("PI", 1, 2), 4096.0, OP.mult)
-    ts(v("VC"), v("VG"), GB, OP.subtract)
+    ts(v("VC"), v("VC"), GB, OP.subtract)
+    fill(v("INFO"), 0.0)
     ts(G16, v("PI", 1, 2), 16.0, OP.mult)
-    ts(GB2, v("PI", 1, 2), 8192.0, OP.mult)
     copy(II, v("PI", 2, 3))
-    for t in range(RO + 1):
-        fill(v("X%d" % t, 4096, 4112), 0.0)
-    fill(v("ZERO"), 0.0)
-    fill(v("ROW"), 0.0)
-    fill(v("ROW2"), 0.0)
-    SZ = v("SZ", 0, 256)
-    SZ1 = v("SZ", 1, 257)
+    copy(AA, v("PI", 3, 4))
+    act(v("IDB"), v("ID"), ACT.Copy)
 
-    def edge(name):
-        mm(v("b6", 0, 1), v("SHF"), v(name, 0, 1), True, True)
-        copy(v(name, 256, 257), v("b6", 0, 1))
-
-    def tables():
-        ts(v("T1"), SZ, -1.0, OP.add)
-        ts(v("KD"), v("T1"), 1.0, OP.min)
-        edge("SZ")
-        tt(v("TW"), SZ1, v("T1"), OP.is_lt)
-        tt(v("T3"), v("KD"), v("VC"), OP.add)
-        tt(v("T2"), v("TW"), SZ1, OP.mult)
-        tt(v("T4"), v("T2"), v("T3"), OP.add)
-        copy(v("B0"), v("T4"))
-        rows("INFO", 0, 1, "B0")
-        tt(v("B1"), v("T4"), v("B0"), OP.subtract)
-        rows("INFO", 1, 1, "B1")
-
-    def tables2():
-        tt(v("EF", 0, 256), v("VC"), v("T1"), OP.add)
-        mm(v("b6", 0, 1), v("SHF"), v("EF", 0, 1), True, True)
-        tt(v("EG"), v("VG"), SZ, OP.add)
-        ts(v("HF"), v("KD"), -1.0, OP.mult, 1.0, OP.add)
-        tt(v("TWE"), v("TW"), v("EG"), OP.mult)
-        tt(v("KDE"), v("KD"), v("EG"), OP.mult)
-
-    tt(SZ, v("EI"), v("VC"), OP.subtract)
-    tables()
-    ts(v("LP"), bg(0, 2048), G16, OP.is_equal)
-
-    def weight(name, k, terms, onv):
-        c = col(k)
-        for n, (row, wgt) in enumerate(terms):
-            if n == 0:
-                ts(c, II, float(row), OP.is_equal, float(wgt), OP.mult)
-            else:
-                ts(col(31), II, float(row), OP.is_equal, float(wgt), OP.mult)
-                tt(c, c, col(31), OP.add)
-        if onv:
-            ts(v(name), v("LP"), c, OP.mult)
+    def tables(last, cut=True, between=None):
+        if cut:
+            tt(v("SZ"), ps(6), v("REM"), OP.min)
         else:
-            act(v(name), v("LP"), ACT.Copy, None, c)
-    weight("LB", 8, [(0, 1), (1, 1)], True)
-    act(v("LN"), v("LP"), ACT.Copy, None, -1.0)
+            tt(v("SZ"), v("EI"), v("VC"), OP.subtract)
+        if last:
+            return
+        mm(ps(7), v("IDB"), v("TWO"), True, False)
+        mm(ps(7, 255, 256), v("SHF"), v("SZ", 0, 1), False, False)
+        mm(ps(7, 0, 255), v("ID"), v("SZ", 1, 256), False, True)
+        act(v("KD"), v("SZ"), ACT.Sign, -1.0)
+        rows("INFO", 2, 1, "KD")
+        if between:
+            between()
+        tt(ps(5), ps(7), v("SZ"), OP.min)
+        act(v("M0"), ps(5), ACT.Copy)
+        rows("INFO", 0, 1, "M0")
+        tt(v("TW"), ps(7), v("SZ"), OP.is_le)
+        rows("INFO", 3, 1, "TW")
+        tt(v("M1"), ps(5), v("M0"), OP.subtract)
+        rows("INFO", 1, 1, "M1")
+        act(v("HF"), v("SZ"), ACT.Relu, 2.0, -1.0)
+    tables(False, False)
+    dma(v("WP", 1024, 2048), v("w", 1024, 2048))
+    dma(v("STI", 128, 384), v("start", 128, 384))
+    ts(v("LB0"), v("LB0"), G16, OP.is_equal)
+    ts(v("I16"), v("I16"), II, OP.is_equal)
+    ts(v("LP"), v("LB0"), BIGW, OP.mult)
+    ts(v("LN"), v("LB0"), -BIGW, OP.mult)
+    nw = [8]
+
+    def weight(name, terms):
+        c = None
+        for row, wgt in terms:
+            n = col(nw[0])
+            nw[0] += 1
+            act(n, v("I16", row, row + 1), ACT.Identity, c, float(wgt))
+            c = n
+        act(v(name), v("LB0"), ACT.Copy, None, c)
+    weight("LI", [(0, 1), (1, 1), (2, BIGW), (3, -BIGW)])
+    fill(v("KS"), -2.0)
+    for k in range(5):
+        fill(xs(k, 4096, SL), 255.0)
+
+    def starts(t):
+        s0 = v("STI", 128 * t, 128 * t + 128)
+        ts(v("AL"), s0, 1.0, OP.add)
+        ts(v("Y0"), s0, 4.0, OP.add)
+    starts(0)
     ts(col(4), II, 14.0, OP.is_ge, 512.0, OP.mult)
     ts(v("REM"), v("VC"), col(4), OP.subtract, -1.0, OP.mult)
     ts(v("REM"), v("REM"), 3584.0, OP.add)
-    iota(v("SELH"), [[0, 2048]], 1, 0)
+    act(v("V0"), v("VC"), ACT.Copy)
+    tt(v("V1"), v("VC"), v("V0"), OP.subtract)
+    copy(ps(1, 256, 512), v("VC"))
+    for name in ("HL", "RL", "JL"):
+        fill(v(name, 0, 1), 0.0)
+    fill(v("P0"), 0.0)
+    fill(v("T2", 0, 4 * NLO), 0.0)
     iota(v("TRI"), [[16, 8], [0, 16]], 0, 0)
     iota(v("QW"), [[16, 256]], 0, 1)
-    ts(v("QW"), v("QW"), G16, OP.subtract)
+    iota(v("T4"), [[1, 16], [16, 16]], 0, 0)
+    iota(v("T5"), [[0, 16], [1, 16]], 0, 0)
+    iota(v("DM"), [[1, 16]], 12288, 16)
     ts(v("TRI"), v("TRI"), G16, OP.is_equal)
     asel(v("TRI"), v("TRI"), [[1, 128]], OP.is_gt, 0.0, 0, -1)
-    ts(v("TRI2"), v("TRI"), 2.0, OP.mult)
-    asel(v("SELH"), v("SELH"), [[128, 4], [-1, 4], [-4, 128]], OP.is_equal, 0.0, 0, 1)
+    ts(v("QW"), v("QW"), G16, OP.subtract)
+    ts(col(6), G16, 16.0, OP.mult)
+    ts(v("DM"), v("DM"), col(6), OP.subtract)
+    ts(COFF, AA, 272.0, OP.mult, -288.0, OP.add)
+    ts(v("FI"), v("T4"), AA, OP.add)
+    ts(v("FI"), v("FI"), 1, OP.arith_shift_right)
+    ts(v("T4"), v("T4"), 1.0, OP.add, v("I16", 0, 1), OP.mult)
+    ts(v("T5"), v("T5"), v("I16", 1, 2), OP.mult)
+    tt(v("T4"), v("T4"), v("T5"), OP.add)
+    ts(v("T5"), v("FI"), v("I16", 2, 3), OP.mult)
+    tt(v("CP"), v("T4"), v("T5"), OP.add)
+    iota(v("SEL"), [[0, 1024]], 1, 0)
+    asel(v("SEL"), v("SEL"), [[-1, 1024]], OP.is_equal, 0.0, 384, 1)
     iota(v("GH"), [[0, 4128]], 0, 0)
-    iota(v("BIG", 0, 4096), [[0, 16], [1, 16], [0, 16]], 0, -1)
-    iota(v("VPAY"), [[1, 16], [0, 16], [16, 16]], 0, 0)
-    iota(v("GV"), [[0, 4096]], 0, 0)
-    for name, k in (("IDB", 1.0), ("NIDB", -1.0), ("ID2B", 2.0), ("ID64", 65536.0), ("NID", -1.0)):
-        act(v(name), v("ID"), ACT.Copy, None, k)
-    ts(v("CK"), v("VC"), GB2, OP.subtract)
-    ts(v("CV"), v("VC"), -1.0, OP.mult, 12288.0, OP.add)
+    rows("GH", 7, 16, "V0")
+    rows("GH", 8, 16, "V1")
+    iota(v("BIG", 0, 4096), [[0, 4096]], 0, 0)
+    iota(v("QB"), [[1, 4096]], 0, 0)
 
-    IG = (0, 1024)
-    TA = (2048, 3072)
-    RA = (9216, 4096)
-    TB = (5120, 6144)
-    RB = (7168, 8192)
+    def late_constants():
+        for name, src, k in (("NIDB", "ID", -1.0), ("ID2B", "ID", 2.0), ("IDBIG", "ID", BIGW), ("IDN64", "ID", -64.0), ("IDA", "ID", float(SL)),
+                             ("NIDA", "ID", -float(SL)), ("IDM", "ID", 4096.0), ("SHFB", "SHF", 1.0), ("L1", "LB0", 1.0), ("Q0", "QW", 1.0)):
+            act(v(name), v(src), ACT.Copy, None, k)
+        weight("LM1", [(0, 288), (1, -255), (2, -544)])
+        weight("LM2", [(0, 16)])
+        weight("LE", [(0, 1)])
+        weight("LH", [(1, -1), (2, -1)])
+        weight("LJ", [(3, 1), (4, 1)])
+        weight("LD", [(1, 1), (2, 1), (5, -1), (6, -1), (7, -1), (8, -1)])
+        weight("LS", [(3, 0.5), (4, 0.5), (5, -0.5), (6, -0.5)])
+        weight("LV", [(7, 1), (8, 1)])
+        weight("LZ", [(9, 1), (10, 1)])
+    late_constants()
+    tt(v("Q1"), v("QW"), v("Q0"), OP.subtract)
+
+    IG, MA, MB = (0, 1024), (2048, 3072), (4096, 5120)
+    XSLOT = (0, 3, 4, 0)
+    LESS = ((1, 2), (2, 1), (3, 2))
 
     for t in range(RO):
-        X, XN = "X%d" % t, "X%d" % (t + 1)
-        AFn = ["AF0", "AF1"]
+        X = xs(XSLOT[t], 0, 4112)
+        last = t == RO - 1
+        for c in range(2):
+            iota(xs(LESS[t][c]), [[0, 4096]], -1 - c, 0)
+        for c in range(2):
+            dma_add(xs(LESS[t][c]), xs(XSLOT[t]))
 
         def w64(name, h):
             return v(name, 64 * h, 64 * h + 64)
@@ -303,292 +361,274 @@ def rank_program(g, core, T, topo):
         def big(base, h):
             return bg(base[h], base[h] + 1024)
 
-        def info(h):
+        def info(h, s):
             act(big(IG, h), ind(v("INFO", 0, 4112), w64("AL", h)), ACT.Copy)
-            bwd(v("b%d" % h, 0, 64), "LB", "BIG", BO + IG[h], 64)
+            mm(ps(h, 0, 64), v("IDB"), v("KS"), True, False)
+            mm(ps(h, 0, 64), v("ID"), w64("Y%d" % s, h), False, False)
+            bwd(ps(h, 0, 64), "LI", "BIG", BO + IG[h], 64, False, True)
 
-        def first_kid(h):
-            tt(big(TA, h), ind(v(X), w64("AL", h)), v("WP", 1024 * h, 1024 * h + 1024), OP.subtract)
-            act(big(RA, h), big(TA, h), ACT.Relu, None, -1.0)
+        def first(h):
+            tt(big(MA, h), ind(X, w64("AL", h)), v("WP", 1024 * h, 1024 * h + 1024), OP.min)
+            bwd(ps(2 + h, 0, 64), "LP", "BIG", BO + MA[h], 64, True, False)
 
-        def first_sum(h):
-            bwd(v("b%d" % (2 + h), 0, 64), "LN", "BIG", BO + RA[h], 64, True, False)
-
-        def second_kid(h, s):
-            copy(w64("BL", h), v("b%d" % h, 0, 64))
-            tt(big(TB, h), ind(v(X), w64("BL", h)), v("WP", 1024 * h, 1024 * h + 1024), OP.subtract)
-            act(big(RB, h), big(TB, h), ACT.Relu, None, -1.0)
-            bwd(v("b%d" % (2 + h), 0, 64), "LP", "BIG", BO + RB[h], 64, False, True)
-            tt(w64("MM", h), v("b%d" % h, 0, 64), w64(AFn[s % 2], h), OP.min)
+        def second(h, s):
+            ts(w64("BL", h), ps(h, 0, 64), s - 3.0, OP.add, 4096.0, OP.min)
+            tt(big(MB, h), ind(X, w64("BL", h)), v("WP", 1024 * h, 1024 * h + 1024), OP.min)
+            bwd(ps(2 + h, 0, 64), "LN", "BIG", BO + MB[h], 64, False, True)
 
         def decide(h, s):
-            ts(w64("GQ", h), v("b%d" % (2 + h), 0, 64), 0.0, OP.is_gt)
-            tt(w64("GQ", h), w64("GQ", h), v("b%d" % h, 0, 64), OP.mult)
-            tt(w64("NV", h), w64("GQ", h), w64("MM", h), OP.max)
+            tt(w64("TY", h), ps(2 + h, 0, 64), w64("Y%d" % s, h), OP.max)
+            tt(w64("Y%d" % (s + 1), h), ps(h, 0, 64), w64("TY", h), OP.min)
             if s < 3:
-                ts(w64("AL", h), w64("NV", h), 1.0, OP.add)
-                ts(w64(AFn[(s + 1) % 2], h), w64("NV", h), 1.0, OP.add)
-            if s == 1:
-                tt(w64("MISS", h), w64(AFn[0], h), w64(AFn[1], h), OP.is_le)
-                ts(w64("MISS", h), w64("MISS", h), 8192.0, OP.mult)
-
-        def starts(t):
-            s0 = v("STI", 128 * t, 128 * t + 128)
-            ts(v("AL"), s0, 1.0, OP.add)
-            ts(v("AF0"), s0, 1.0, OP.add)
-        if t == 0:
-            starts(0)
-        info(0)
-        info(1)
-        for s in range(4):
-            first_kid(0)
-            first_sum(0)
-            if s > 0:
-                decide(1, s - 1)
-                info(1)
+                ts(w64("AL", h), w64("Y%d" % (s + 1), h), s - 2.0, OP.add)
+                info(h, s + 1)
             else:
-                first_kid(1)
-                first_sum(1)
-            second_kid(0, s)
-            if s > 0:
-                first_kid(1)
-                first_sum(1)
-            second_kid(1, s)
+                p = (64 * h, 64 * h + 64, 1)
+                mm(v("b4", 0, 128, 1, p), w64("MISS", h), v("IDM"), True, False)
+                mm(v("b4", 0, 128, 1, p), w64("Y4", h), v("ID"), False, True)
+                if h == 1:
+                    mm(ps(5, 0, 128), v("MISS"), v("IDM"), True, False)
+                    mm(ps(5, 0, 128), v("Y4"), v("ID"), False, False)
+        info(0, 0)
+        info(1, 0)
+        first(0)
+        first(1)
+        second(0, 0)
+        second(1, 0)
+        for s in range(4):
             decide(0, s)
+            if s > 0:
+                second(1, s)
             if s < 3:
-                info(0)
-        decide(1, 3)
-        tt(v("CODE"), v("NV"), v("MISS"), OP.add)
-        tr(v("b7", 0, 128), v("CODE"), v("ID"))
-        copy(v("TI"), v("b7", 0, 128))
-        ts(v("TLO"), v("TI"), 63, OP.bitwise_and)
-        copy(v("LOb"), v("TLO"))
-        ts(v("THI"), v("TI"), 6, OP.arith_shift_right)
-        copy(v("HIb"), v("THI"))
+                first(0)
+            else:
+                fill(bg(16384, 16512), -1.0)
+            decide(1, s)
+            if s == 1:
+                tt(v("MISS"), v("Y2"), v("Y1"), OP.is_lt)
+            if s < 3:
+                second(0, s + 1)
+                first(1)
+        ts(v("HIb"), ps(4, 0, 128), 1.0 / 64, OP.mult, 129 - 31.5 / 64, OP.add)
+        mm(ps(5, 0, 128), v("IDN64"), v("HIb"), False, True)
+        act(v("LOb"), ps(5, 0, 128), ACT.Identity, 64.0 * 129)
         for k in range(64):
-            ts(bg(128 * k, 128 * k + 128), v("HIb"), float(k), OP.is_equal)
+            ts(bg(128 * k, 128 * k + 128), v("HIb"), 129.0 + k, OP.is_equal)
             if NLO + k < 64:
                 n = NLO + k
                 act(bg(8192 + 128 * n, 8192 + 128 * n + 128), v("LOb"), ACT.Sign, 0.5 - n)
         for n in range(NLO):
             ts(bg(8192 + 128 * n, 8192 + 128 * n + 128), v("LOb"), float(n), OP.is_equal)
-        fill(bg(16384, 16512), -1.0)
-        mm(v("b0", 0, 256), v("ID"), v("CK"), True, False)
-        mm(v("b1", 0, 256), v("ID"), v("CV"), True, False)
-        mm(v("b2", 0, 256), v("ID"), v("VG"), True, False)
-        mm(v("b3", 0, 256), v("ID"), SZ, True, False)
-        tables2()
-        if t < RO - 1:
-            starts(t + 1)
-
-        def payload(a, b):
-            if t == 0:
-                tt(v("VPAY", a, b), v("VPAY", a, b), v("BIG", a, b), OP.add)
-        if t == 0:
-            weight("L1", 9, [(0, 1), (1, 1), (2, 8192)], False)
-            weight("L2", 10, [(3, 1), (4, 1)], False)
-            weight("L3", 11, [(0, 4096), (1, 4096), (2, 0.5), (3, 0.5)], False)
-            weight("L4", 13, [(4, 1), (5, 1)], False)
-            ts(v("BIG", 0, 4096), v("BIG", 0, 4096), G16, OP.add, 0.0, OP.is_ge)
-        payload(0, 2048)
+        mm(ps(0), v("ID"), v("VC"), True, False)
+        mm(ps(0), v("ID"), v("SZ"), False, False)
+        mm(ps(0, 256, 257), v("SHF"), v("VC", 0, 1), False, False)
+        mm(ps(0, 256, 257), v("SHF"), v("SZ", 0, 1), False, True)
+        mm(ps(1), v("ID"), v("VC"), True, False)
+        mm(ps(2), v("ID"), v("VC"), True, False)
         for gg in range(8):
             for i in range(16):
                 c = 16 * gg + i
-                mm(v("b4", gg // 2, 260, 4, (64 * (gg % 2), 64 * (gg % 2) + 64, 1)), bg(c, 8192, 128), bg(8192 + c, 16512, 128), i == 0, i == 15)
-        copy(v("EF", 256, 257), v("b6", 0, 1))
-        copy(v("EL", 0, 257), v("EF", 0, 257))
-        copy(v("T1"), v("b4", 4, 260))
-        copy(v("HB", 0, 4 * NLO), v("b4", 0, 4 * NLO))
-        tt(v("HB", 4 * NLO, 256), v("b4", 4 * NLO, 256), v("T1", 4 * NLO, 256), OP.subtract)
+                mm(v("b6", gg // 2, 260, 4, (64 * (gg % 2), 64 * (gg % 2) + 64, 1)), bg(c, 8192, 128), bg(8192 + c, 16512, 128), i == 0, i == 15)
+        ts(v("EL", 0, 257), ps(0, 0, 257), -1.0, OP.add)
+        tt(v("TWE"), ps(0), v("TW"), OP.mult)
+        tt(v("KDE"), ps(0), v("KD"), OP.mult)
+        if not last:
+            starts(t + 1)
+        copy(v("T2", 4 * NLO, 256), ps(6, 4 * NLO + 4, 260))
+        tt(v("HB"), ps(6), v("T2"), OP.subtract)
         for cc in range(4):
             for gh in range(4):
-                mm(v("b5", 64 * cc, 64 * cc + 64), v("SELH", 128 * (4 * gh + cc), 128 * (4 * gh + cc) + 128), v("HB", gh, 256, 4), gh == 0, gh == 3)
-        HM = v("HM", 0, 256)
-        tt(HM, v("b5", 0, 256), v("HF"), OP.min)
-        red(v("RC", 0, 1), HM, OP.add)
-        mm(v("b6", 2, 3), v("TRI"), v("RC", 0, 1), True, True)
-        act(v("HMb"), HM, ACT.Copy)
-        rows("GH", 2, 15, "HMb")
-        scan(v("HINC"), v("ZERO"), HM, v("b6", 2, 3), OP.add, OP.add)
-        copy(v("H0"), v("HINC"))
-        rows("GH", 0, 16, "H0")
-        tt(v("H1"), v("HINC"), v("H0"), OP.subtract)
-        rows("GH", 1, 16, "H1")
-        edge("HM")
-        tt(v("HK"), v("HM", 1, 257), v("KDE"), OP.mult)
-        mm(v("b2", 0, 256), v("ID64"), v("HMb"), False, True)
-        mm(v("b1", 0, 256), v("ID2B"), v("H0"), False, False)
-        mm(v("b1", 0, 256), v("ID2B"), v("H1"), False, True)
-        tt(v("T2"), HM, v("b1", 0, 256), OP.mult)
-        payload(2048, 2816)
-        mm(v("b0", 0, 256), v("NIDB"), v("H0"), False, False)
-        mm(v("b0", 0, 256), v("NIDB"), v("H1"), False, False)
+                a = 384 - 128 * gh + cc
+                mm(ps(7, 64 * cc, 64 * cc + 64), v("SEL", a, a + 512, 4), v("HB", gh, 256, 4), gh == 0, gh == 3)
+        tt(v("HM"), ps(7), v("HF"), OP.min)
+        rows("GH", 0, 15, "HM")
+        scan(v("HL", 1, 257), v("HM"), v("HM"), 0.0, OP.add, OP.max)
+        mm(ps(3, 0, 255), v("IDB"), v("HM", 1, 256), True, False)
+        mm(ps(3, 255, 256), v("SHFB"), v("HM", 0, 1), False, True)
+        mm(ps(7, 256, 257), v("TRI"), v("HL", 256, 257), True, True)
+        mm(ps(1), v("IDBIG"), v("HM"), False, True)
+        tt(v("HK"), ps(3), v("KDE"), OP.mult)
+        ts(ps(4), v("HL", 1, 257), ps(7, 256, 257), OP.add)
+        act(v("H0"), ps(4), ACT.Copy)
+        tt(v("DO"), v("HL", 16, 257, 16), v("HL", 0, 256, 16), OP.subtract)
+        ts(v("DO"), v("DO"), 15.5, OP.is_gt)
+        tt(v("DO"), v("DO"), v("DM"), OP.mult)
+        tt(v("H1"), ps(4), v("H0"), OP.subtract)
+        mm(ps(2), v("NIDB"), v("H0"), False, False)
+        mm(ps(2), v("NIDB"), v("H1"), False, False)
+        mm(ps(2), v("IDB"), v("HM"), False, True)
+        GHW = v("GH", 16, 4112)
         for k in (0, 2, 1, 3):
             w = 65 if k == 3 else 64
-            o, i = v("G1", 1024 * k, 1024 * k + 16 * w), ind(v("GH", 16, 4112), v("EL", 64 * k, 64 * k + w))
-            if k < 2:
-                copy(o, i)
-            else:
-                act(o, i, ACT.Copy)
-            bwd(v("b7", 64 * k, 64 * k + w), "L1", "G1", 1024 * k, w)
-        mm(v("b0", 0, 256), v("ID"), v("T2"), False, True)
-        mm(v("b3", 0, 256), v("IDB"), v("H0"), False, False)
-        mm(v("b3", 0, 256), v("IDB"), v("H1"), False, False)
-        mm(v("b3", 0, 256), v("NIDB"), v("HMb"), False, False)
-        payload(2816, 4096)
-        iota(v("BIG", 0, 4096), [[0, 4096]], 0, 0)
-        ts(v("HME", 0, 257), v("b7", 0, 257), 8192.0, OP.is_ge)
-        tt(v("T4"), v("TWE"), v("HME", 1, 257), OP.mult)
-        tt(v("T4"), v("T4"), v("HK"), OP.max)
+            gather(k < 2, bg(1024 * k, 1024 * k + 16 * w), GHW, v("EL", 64 * k, 64 * k + w))
+            bwd(ps(5, 64 * k, 64 * k + w), "LE", "BIG", BO + 1024 * k, w)
+        rows("GH", 1, 16, "H0")
+        rows("GH", 2, 16, "H1")
 
-        def maxscan(out, src, rc, ini, fillers):
-            red(v("RC", rc, rc + 1), src, OP.max)
-            tr(v("b6", 128, 256, 1, ONEROW), v("RC", rc, rc + 1), v("ID"))
-            fillers[0]()
-            scan(v("ROW", 1, 129, 1, ONEROW), v("ROW2", 0, 128, 1, ONEROW), v("b6", 128, 256, 1, ONEROW), 0.0, OP.max, OP.max)
-            mm(v("b6", ini, ini + 1), v("ROW", 0, 128, 1, ONEROW), v("ID", 0, 1, 1, ONEROW), True, True)
-            fillers[1]()
-            scan(out, src, src, v("b6", ini, ini + 1), OP.max, OP.max)
-
-        def f1():
-            ts(v("HEC"), v("HME", 0, 256), -8192.0, OP.mult)
-
-        def f2():
-            tt(v("HEC"), v("HEC"), v("b7", 0, 256), OP.add)
-        maxscan(v("RS", 1, 257), v("T4"), 1, 4, (f1, f2))
-        tt(v("KI"), v("RS", 1, 257), v("b2", 0, 256), OP.is_gt)
-        red(v("RC", 2, 3), v("KI"), OP.add)
-        mm(v("b6", 6, 7), v("ID"), GB2, True, False)
-        mm(v("b6", 6, 7), v("TRI2"), v("RC", 2, 3), False, True)
-        copy(v("RS", 0, 1), v("b6", 4, 5))
-        tt(v("OX"), v("RS", 0, 256), v("VG"), OP.is_le)
-        scan(v("J2", 1, 257), v("KI"), v("KI"), v("b6", 6, 7), OP.add, OP.add)
-        copy(v("J2", 0, 1), v("b6", 6, 7))
-        act(v("J0"), v("J2", 1, 257), ACT.Copy)
+        def carry(src):
+            ts(v("DG"), v("I16"), src, OP.mult)
+            mm(ps(7, 272, 288), v("TRI"), v("DG"), True, True)
+        tt(v("T4"), ps(5, 1, 257), v("TWE"), OP.mult)
+        scan(v("RL", 1, 257), v("T4"), v("HK"), 0.0, OP.max, OP.max)
+        carry(v("RL", 256, 257))
+        red(v("RC", 0, 1), ps(7, 272, 288), OP.max)
+        ts(v("RS", 0, 257), v("RL", 0, 257), v("RC", 0, 1), OP.max)
+        tt(v("KI"), v("RS", 1, 257), ps(1), OP.is_gt)
+        scan(v("JL", 1, 257), v("KI"), v("KI"), 0.0, OP.add, OP.add)
+        mm(ps(7, 257, 258), v("TRI"), v("JL", 256, 257), True, True)
+        act(v("OUT"), v("KI"), ACT.Identity, 1.0, -1.0)
+        tt(v("OX"), v("RS", 0, 256), ps(1, 256, 512), OP.is_le)
+        ts(ps(4, 0, 257), v("JL", 0, 257), ps(7, 257, 258), OP.add)
+        tt(v("T5"), ps(4), v("OX"), OP.mult)
+        act(v("J0"), ps(4, 1, 257), ACT.Copy)
         rows("GH", 3, 16, "J0")
-        tt(v("T5"), v("J2", 0, 256), v("OX"), OP.mult)
+        scan(v("LQ"), v("T5"), v("T5"), 0.0, OP.max, OP.max)
+        carry(v("LQ", 255, 256))
+        tt(v("J1"), ps(4, 1, 257), v("J0"), OP.subtract)
+        rows("GH", 4, 16, "J1")
+        red(v("RC", 1, 2), ps(7, 272, 288), OP.max)
+        ts(v("T6"), v("LQ"), v("RC", 1, 2), OP.max)
+        tt(v("P0", 16, 272), ps(2), v("T6"), OP.add)
+        act(v("U0"), v("T6"), ACT.Copy)
+        tt(v("O16"), v("P0", 16, 272, 16), v("DO"), OP.max)
+        copy(v("OFF"), v("O16"))
+        copy(ind(v("BIG", 0, VLS), v("OFF")), v("CP"))
+        mm(ps(1), v("ID"), v("SZ"), True, False)
+        mm(ps(1), v("IDB"), v("H0"), False, False)
+        mm(ps(1), v("IDB"), v("H1"), False, False)
+        mm(ps(1), v("NIDB"), v("HM"), False, False)
+        mm(ps(2), v("NIDB"), v("J0"), True, False)
+        mm(ps(2), v("NIDB"), v("J1"), False, False)
+        mm(ps(2), v("ID2B"), v("KI"), False, False)
 
-        def f3():
-            tt(v("J1"), v("J2", 1, 257), v("J0"), OP.subtract)
-            rows("GH", 4, 16, "J1")
-
-        def f4():
-            ts(v("OUT"), v("KI"), -1.0, OP.mult, 1.0, OP.add)
-        maxscan(v("T6"), v("T5"), 3, 8, (f3, f4))
-        tt(v("POS"), v("b0", 0, 256), v("T6"), OP.add)
-        copy(v("OFF"), v("POS"))
-        act(v("P0"), v("POS"), ACT.Copy)
-        rows("GV", 0, 0, "P0")
-        mm(v("b1", 0, 256), v("IDB"), v("J0"), True, False)
-        mm(v("b1", 0, 256), v("IDB"), v("J1"), False, False)
-        mm(v("b1", 0, 256), v("NID"), v("T6"), False, True)
-        act(v("S20"), v("b1", 0, 256), ACT.Copy)
-        rows("GV", 2, 0, "S20")
-        tt(v("P1"), v("POS"), v("P0"), OP.subtract)
-        rows("GV", 1, 0, "P1")
-        copy(ind(v("BIG", 0, 20480), v("OFF", 0, 192)), v("VPAY", 0, 3072))
-        mm(v("b3", 0, 256), v("NID"), v("HEC"), False, True)
-        mm(v("b5", 0, 256), v("NID"), v("J2", 0, 256), True, False)
+        def ends2_sums(k):
+            bwd(ps(1, 64 * k, 64 * k + 64), "LH", "G", 1024 * k, 64, False, k == 3)
+            bwd(ps(2, 64 * k, 64 * k + 64), "LJ", "G", 1024 * k, 64, False, k == 3)
         for k in range(4):
-            act(v("G1", 1024 * k, 1024 * k + 1024), ind(v("GH", 16, 4112), v("EL", 64 * k, 64 * k + 64)), ACT.Copy)
-            bwd(v("b5", 64 * k, 64 * k + 64), "L2", "G1", 1024 * k, 64, False, k == 3)
-        tt(v("S21"), v("b1", 0, 256), v("S20"), OP.subtract)
-        rows("GV", 3, 0, "S21")
-        tt(v("T5"), v("OUT"), v("b5", 0, 256), OP.mult)
-        tt(v("T5"), v("T5"), v("b3", 0, 256), OP.add)
-        act(v("Z0"), v("T5"), ACT.Copy)
-        rows("GV", 4, 0, "Z0")
-        tt(v("Z1"), v("T5"), v("Z0"), OP.subtract)
-        rows("GV", 5, 0, "Z1")
-        copy(ind(v("BIG", 0, 20480), v("OFF", 192, 256)), v("VPAY", 3072, 4096))
+            gather(False, v("G", 1024 * k, 1024 * k + 1024), GHW, w64("EL", k))
         for k in range(4):
             a = 1024 * k
-            scan(v("VLS", a, a + 1024), v("BIG", a, a + 1024), v("BIG", a, a + 1024), 0.0 if k == 0 else v("VLS", a - 1, a), OP.max, OP.max)
-            bwd(v("b%d" % k, 0, 64), "LP", "VLS", a, 64)
-            if k == 2:
-                ts(v("VLL", 0, 64), v("b0", 0, 64), -1.0, OP.add)
-        for k in range(1, 3):
-            ts(v("VLL", 64 * k, 64 * k + 64), v("b%d" % k, 0, 64), -1.0, OP.add)
+            scan(v("BIG", VLS + a, VLS + a + 1024), v("BIG", a, a + 1024), v("BIG", a, a + 1024),
+                 0.0 if k == 0 else v("BIG", VLS + a - 1, VLS + a), OP.max, OP.max)
+            bwd(ps(5, 64 * k, 64 * k + 64), "LM1", "BIG", VLS + a, 64)
+        iota(v("BIG", 0, 4096), [[0, 4096]], 0, 0)
+        vtr(v("PW", 0, 256), v("P0", 16, 272))
+        vtr(v("PW", 256, 544), v("P0", 0, 288))
+        ts(v("ML"), ps(5), COFF, OP.add)
 
-        def gat(k, out, win):
-            i = ind(win, v("VLL", 64 * k, 64 * k + 64))
-            if k < 2:
-                act(out, i, ACT.Copy)
-            else:
-                copy(out, i)
-        for k in (0, 2, 1, 3):
+        def ub(k):
+            return ps(3 * (k % 2), 64 * (k // 2), 64 * (k // 2) + 64)
+
+        def ulist(k):
+            ts(w64("UL", k), ub(k), -17.0, OP.add)
+        for n, k in enumerate((3, 2, 1, 0)):
             a = 1024 * k
-            if k == 3:
-                ts(v("VLL", 192, 256), v("b3", 0, 64), -1.0, OP.add)
-            gat(k, bg(12288 + a, 12288 + a + 1024), v("GV"))
-            bwd(v("b4", 64 * k, 64 * k + 64), "L3", "BIG", BO + 12288 + a, 64)
-        for k in (0, 2, 1, 3):
-            gat(k, bg(1024 * k, 1024 * k + 1024), v(X))
-        act(bg(4096, 6144), bg(0, 2048), ACT.Relu, -1.0)
-        act(bg(6144, 8192), bg(2048, 4096), ACT.Relu, -1.0)
-        copy(v("PKI"), v("b4", 0, 256))
-        ts(v("PPI"), v("PKI"), 12, OP.arith_shift_right)
-        ts(v("PSI"), v("PKI"), 4095, OP.bitwise_and)
-        tt(v("T1"), v("QW"), v("PPI"), OP.subtract)
-        tt(v("T2"), v("T1"), v("PSI"), OP.is_gt)
-        ts(v("T3"), v("T1"), 0.0, OP.is_gt)
-        tt(v("T3"), v("T3"), v("T2"), OP.add)
-        tt(v("T4"), v("T3"), v("PSI"), OP.mult)
-        tt(v("T4"), v("QW"), v("T4"), OP.subtract)
-        copy(v("QL"), v("T4"))
+            if n == 3:
+                tt(v("T5"), ps(2), v("OUT"), OP.mult)
+                tt(ps(1), ps(1), v("T5"), OP.add)
+                act(v("Z0"), ps(1), ACT.Copy)
+                rows("GH", 9, 16, "Z0")
+                ulist(2)
+                tt(v("Z1"), ps(1), v("Z0"), OP.subtract)
+                rows("GH", 10, 16, "Z1")
+            if n == 2:
+                tt(v("U1"), v("T6"), v("U0"), OP.subtract)
+                rows("GH", 5, 16, "U0")
+                rows("GH", 6, 16, "U1")
+                ulist(3)
+            if n < 2:
+                ends2_sums(2 * n)
+            bwd(ub(k), "LM2", "BIG", VLS + a, 64, True, False)
+            if n < 2:
+                ends2_sums(2 * n + 1)
+            tt(v("BIG", CMP + a, CMP + a + 1024), ind(v("PW"), w64("ML", k)), v("QB", a, a + 1024), OP.is_le)
+            bwd(ub(k), "L1", "BIG", CMP + a, 64, False, True)
+        ulist(1)
+
+        def h128(name, h):
+            return v(name, 128 * h, 128 * h + 128)
+        for h in (1, 0):
+            mm(ps(4 + h, 0, 128), v("IDB"), h128("Q0", h), True, False)
+            mm(ps(4 + h, 0, 128), v("IDB"), h128("Q1", h), False, False)
+        for k, opens in ((3, True), (2, False), (1, True), (0, False)):
+            h, a, c = k // 2, 1024 * k, 64 * (k % 2)
+            if k == 1:
+                ulist(0)
+            gather(k % 2 == 1, v("G", a, a + 1024), GHW, w64("UL", k))
+            bwd(ps(4 + h, c, c + 64), "LD", "G", a, 64, False, not opens)
+            bwd(ps(6 + h, c, c + 64), "LS", "G", a, 64, opens, not opens)
+
+        def decode(h):
+            bd, bs = ps(4 + h, 0, 128), ps(6 + h, 0, 128)
+            act(h128("SF", h), bs, ACT.Copy)
+            act(h128("SG", h), bd, ACT.Sign)
+            tt(h128("T4", h), bd, h128("SF", h), OP.is_gt)
+            tt(h128("CC", h), h128("T4", h), h128("SG", h), OP.add)
+            tt(bd, bs, h128("CC", h), OP.mult)
+            tt(h128("T4", h), h128("QW", h), bd, OP.subtract)
+            copy(h128("QL", h), h128("T4", h))
         dst = T.cores[(rank + 1) % len(T.cores)]
         src = T.cores[(rank - 1) % len(T.cores)]
 
-        def send(name, to, rsem, lsem):
+        def send(frm, to, rsem, lsem):
             rid, pid, _se = topo.addr(dst)
-            add("G", [v(name)], [], lambda: g.remote_dma(ap(to), ap(v(name)), T.sem[rsem], T.sem[lsem], pid, rid, topo.mask(core, dst)),
-                lsem, len(topo.engines(core, dst)))
+            add("G", [frm], [], lambda: g.remote_dma(ap(to), ap(frm), T.sem[rsem], T.sem[lsem], pid, rid, topo.mask(core, dst)),
+                lsem, len(topo.engines(core, dst)), False)
             add("R", [], [to], None, rsem, len(topo.engines(src, core)))
 
-        def sizes(out, lo, hi, onv):
-            i = ind(bg(12288, 16384), v("QL", lo // 16, hi // 16))
-            if onv:
-                copy(out, i)
-            else:
-                act(out, i, ACT.Copy)
+        def copy0(onv, a, b):
+            gather(onv, v("GQ", a, b), v("G", 0, 2048 if b <= 2048 else 4096), v("QL", a // 16, b // 16))
 
-        def szc(i):
-            s = v("SZB", 256 * i, 256 * i + 256) if i < 14 else v("LZ%d" % t, 256 * (i - 14), 256 * (i - 14) + 256)
-            mm(v("b7", 0, 256), v("L4", 128 * i, 128 * i + 128), s, i == 0, i == 15)
+        def xlist(bank, a, b):
+            o = ps(bank, 0, (b - a) // 16)
+            mm(o, v("IDA" if t == 0 else "NIDA"), v("CC", a // 16, b // 16), True, False)
+            bwd(o, "LV", "GQ", a, (b - a) // 16, False, True)
+            ts(v("XL", a // 16, b // 16), o, 0.0 if t == 0 else 2.0 * SL, OP.add)
+        XW = v("XX", SL * min(LESS[t] + (XSLOT[t],)), SL * (min(LESS[t] + (XSLOT[t],)) + 3))
+        XN = XSLOT[t + 1]
 
-        def xl(lo, hi):
-            return ind(bg(0, 12288), v("XL", lo // 16, hi // 16))
-        sizes(v("SZS"), 3584, 4096, False)
-        send("SZS", v("LZ%d" % t), "rz%d" % t, "lz%d" % t)
-        for k in (0, 3, 1, 4, 2, 5, 6):
-            sizes(v("SZB", 512 * k, 512 * k + 512), 512 * k, 512 * k + 512, k < 3)
-            szc(2 * k)
-            szc(2 * k + 1)
-            if k == 0:
-                ts(v("T3"), v("T3"), 4096.0, OP.mult)
-                tt(v("T5"), v("T3"), v("T4"), OP.add)
-                copy(v("XL"), v("T5"))
-        szc(14)
-        szc(15)
-        ts(bg(8192, 12288), bg(0, 4096), 2.0, OP.subtract, 0.0, OP.max)
-        act(v("XS"), xl(3584, 4096), ACT.Copy)
-        send("XS", v(XN, 3584, 4096), "rx%d" % t, "lx%d" % t)
-        if t < RO - 1:
-            act(v(XN, 1024, 3584), xl(1024, 3584), ACT.Copy)
-            tt(SZ, v("b7", 0, 256), v("REM"), OP.min)
-            tables()
-            copy(v(XN, 0, 1024), xl(0, 1024))
-        else:
-            copy(v(XN, 0, 1024), xl(0, 1024))
-            dma(v("y", 0, 1024), v(XN, 0, 1024))
-            act(v(XN, 2048, 3584), xl(2048, 3584), ACT.Copy)
-            copy(v(XN, 1024, 2048), xl(1024, 2048))
-            dma(v("y", 1024, 2048), v(XN, 1024, 2048))
-            tt(SZ, v("b7", 0, 256), v("REM"), OP.min)
-            tt(v("T1"), v("VC"), SZ, OP.add)
-            dma(v("y", 2048, 3584), v(XN, 2048, 3584))
+        def newx(onv, a, b):
+            gather(onv, xs(XN, a, b) if a < 3584 else v("XS"), XW, v("XL", a // 16, b // 16), True)
+            if last and a < 3584:
+                dma(v("y", a, b), xs(XN, a, b))
+
+        def size_sums(lo, hi):
+            for i in range(lo, hi):
+                a = 256 * i
+                s = v("GQ", a, a + 256) if i < 14 else v("LZ%d" % t, a - 3584, a - 3584 + 256)
+                mm(ps(6), blk("LZ", i), s, i == 8, i == 15)
+        decode(1)
+        copy0(False, 3584, 4096)
+        send(v("GQ", 3584, 4096), v("LZ%d" % t), "rz%d" % t, "lz%d" % t)
+        decode(0)
+        copy0(False, 2048, 3584)
+        xlist(0, 3584, 4096)
+        copy0(True, 0, 1024)
+        newx(False, 3584, 4096)
+        land = v("LX") if last else xs(XN, 3584, 4096)
+        send(v("XS"), land, "rx%d" % t, "lx%d" % t)
+        size_sums(8, 14)
+        copy0(True, 1024, 2048)
+        xlist(3, 2048, 3584)
+        size_sums(0, 8)
+        xlist(0, 0, 1024)
+        size_sums(14, 16)
+        newx(False, 2048, 3584)
+        if last:
+            newx(True, 0, 1024)
+            xlist(3, 1024, 2048)
+            newx(False, 1536, 2048)
+            newx(True, 1024, 1536)
+            tables(True)
+            tt(v("T1"), ps(1, 256, 512), v("SZ"), OP.add)
             dma(v("ye", 0, 4096, 1, (0, 8, 1)), v("T1"))
-            dma(v("y", 3584, 4096), v(XN, 3584, 4096))
+            dma(v("y", 3584, 4096), land)
+        else:
+            newx(True, 0, 512)
+            tables(False, True, lambda: newx(True, 512, 1024))
+            xlist(3, 1024, 2048)
+            newx(False, 1536, 2048)
+            newx(True, 1024, 1536)
 
     qidx = {}
     hist = {}
@@ -661,7 +701,7 @@ def rank_program(g, core, T, topo):
         r = o["call"]()
         if o["sem"] is not None:
             o["val"] = o["n"]
-            if q != "G":
+            if o["own"]:
                 r.then_inc(T.sem[o["sem"]], o["n"])
         elif o["tok"] in need:
             cnt[q] = cnt.get(q, 0) + 1

@@ -4,9 +4,17 @@ from concourse.mybir import dt, AluOpType, AxisListType, ActivationFunctionType
 import comms_topo
 
 RO = 3
-NLO = 20
 SL = 4224
 BIGW = 8192.0
+THIRD = 11184811 / 2 ** 25
+CUTS = (0, 48, 56, 64)
+NS = (12, 12)
+ENDS1 = ((True, 0, 64), (False, 144, 208), (False, 208, 257), (True, 64, 144))
+ENDS2 = ((False, 0, 64), (False, 64, 128), (False, 128, 224), (True, 224, 256))
+RUNS = ((False, 3), (False, 2), (True, 1), (False, 0))
+COPY = ((False, 3072, 3584), (False, 2048, 3072), (False, 1024, 2048), (True, 0, 1024))
+NEWX = ((False, 2048, 3584), (True, 0, 1024), (False, 1536, 2048), (True, 1024, 1536))
+CYCLE, PE, WAKE, GATHER, SCATTER, SLACK = 0.00083, 0.00058, 0.18, 1.3, 2.5, 0.2
 
 SCRATCH = {
     "BIG": ("sbuf", [128, 20736], "bfloat16"),
@@ -15,6 +23,8 @@ SCRATCH = {
     "WP": ("sbuf", [128, 2048], "bfloat16"),
     "INFO": ("sbuf", [128, 4112], "bfloat16"),
     "GH": ("sbuf", [128, 4128], "bfloat16"),
+    "GT": ("sbuf", [128, 4128], "bfloat16"),
+    "DI": ("sbuf", [128, 256], "bfloat16"),
     "G": ("sbuf", [128, 4096], "bfloat16"),
     "GQ": ("sbuf", [128, 4096], "bfloat16"),
     "XS": ("sbuf", [128, 512], "bfloat16"),
@@ -33,25 +43,26 @@ SCRATCH = {
     "PW": ("sbuf", [128, 544], "float32"),
     "P0": ("sbuf", [128, 288], "float32"),
     "LB0": ("sbuf", [128, 144], "float32"),
+    "HB": ("sbuf", [128, 512], "bfloat16"),
     "KS": ("sbuf", [128, 64], "bfloat16"),
 }
 for _n in ("ML", "UL", "QL", "XL"):
     SCRATCH[_n] = ("sbuf", [128, 256], "uint16")
 for _t in range(RO):
-    SCRATCH["LZ%d" % _t] = ("sbuf", [128, 512], "bfloat16")
-for _n in ("LP", "LN", "L1", "LI", "LM1", "LM2", "LE", "LH", "LJ", "LD", "LS", "LV", "LZ"):
+    SCRATCH["LZ%d" % _t] = ("sbuf", [128, 528], "bfloat16")
+for _n in ("LP", "LN", "L1", "LI", "LM1", "LM2", "LE", "LJ", "LD", "LS", "LV", "LZ"):
     SCRATCH[_n] = ("sbuf", [128, 144], "bfloat16")
-for _n in ("ID", "IDM", "TRI", "SHF", "ONE", "MISS", "TY", "Y0", "Y1", "Y2", "Y3", "Y4"):
+for _n in ("ID", "IDP", "TRI", "SHF", "ONE", "TY", "Y0", "Y1", "Y2", "Y3", "Y4"):
     SCRATCH[_n] = ("sbuf", [128, 128], "float32")
-for _n in ("HIb", "LOb", "IDB", "NIDB", "ID2B", "IDBIG", "IDN64", "IDA", "NIDA", "SHFB"):
+for _n in ("IDM", "MISS", "IDB", "NIDB", "ID2B", "IDBIG", "IDN64", "IDA", "NIDA", "SHFB"):
     SCRATCH[_n] = ("sbuf", [128, 128], "bfloat16")
 for _n in ("I16", "DM", "DO", "DG", "O16"):
     SCRATCH[_n] = ("sbuf", [128, 16], "float32")
-for _n in ("VC", "REM", "QW", "SZ", "HF", "TWE", "KDE", "HK", "OX", "OUT", "LQ", "T6", "SF", "SG", "T1", "T2", "T4", "T5"):
+for _n in ("VC", "REM", "QW", "SZ", "HF", "TWE", "KDE", "HK", "OX", "OUT", "LQ", "T6", "SF", "T1", "T4", "T5"):
     SCRATCH[_n] = ("sbuf", [128, 256], "float32")
 for _n in ("HL", "RL", "RS", "JL"):
     SCRATCH[_n] = ("sbuf", [128, 264], "float32")
-for _n in ("HB", "CP", "TWO", "KD", "TW", "HM", "KI", "CC", "M0", "M1", "H0", "H1", "J0", "J1", "U0", "U1", "Z0", "Z1", "V0", "V1", "Q0", "Q1"):
+for _n in ("CP", "ONEB", "KD", "TW", "HM", "KI", "CC", "M0", "M1", "H0", "H1", "J0", "J1", "U0", "U1", "Z0", "Z1", "V0", "V1", "Q0", "Q1"):
     SCRATCH[_n] = ("sbuf", [128, 256], "bfloat16")
 for _n in range(8):
     SCRATCH["b%d" % _n] = ("psum", [128, 512], "float32")
@@ -96,6 +107,7 @@ def rank_program(g, core, T, topo):
         return
     ops = []
     masks = {}
+    row = [None]
 
     def pm(p):
         if p not in masks:
@@ -111,7 +123,26 @@ def rank_program(g, core, T, topo):
                 out.append(x)
         return out
 
-    def add(q, reads, writes, call, sem=None, n=1, own=True):
+    def width(x):
+        if x[0] == "@":
+            return 16 * width(x[2])
+        return len(range(x[2], x[3], x[4]))
+
+    def two(x):
+        return SCRATCH.get(x[0], (0, 0, "x"))[2] in ("bfloat16", "uint16")
+
+    def cost(q, out, ins, per):
+        full = [x for x in ins if isinstance(x, tuple) and (x[0] == "@" or width(x) > 1)]
+        n = max([width(out)] + [width(x) for x in full])
+        if out[0] == "@":
+            return 0.05 + n * SCATTER * CYCLE
+        if any(x[0] == "@" for x in full):
+            return 0.05 + n * GATHER * CYCLE
+        if per is None:
+            per = 0.5 if all(two(x) for x in full + [out]) else 1
+        return max(64, n * per) * CYCLE + (0.015 if q == "V" else 0.035)
+
+    def add(q, reads, writes, call, time, sem=None, n=1, own=True, lat=None, join=False):
         rd = []
         for x in reads:
             flat(x, rd)
@@ -122,7 +153,15 @@ def rank_program(g, core, T, topo):
                 rd.append(x[2])
             else:
                 wr.append(x)
-        ops.append({"q": q, "r": rd, "w": wr, "call": call, "sem": sem, "n": n, "own": own})
+        if join:
+            o = ops[-1]
+            o["r"] += rd
+            o["w"] += [x for x in wr if x not in o["w"]]
+            o["calls"].append(call)
+            o["cost"] += time
+            return
+        ops.append({"q": q, "r": rd, "w": wr, "calls": [call], "sem": sem, "n": n, "own": own, "row": row[0], "cost": time,
+                    "lat": WAKE if lat is None else lat})
 
     def ap(x):
         if not isinstance(x, tuple):
@@ -133,28 +172,29 @@ def rank_program(g, core, T, topo):
         return T[name][p[0]:p[1]:p[2], c0:c1:cs] if (p[2] != 1 or cs != 1) else T[name][p[0]:p[1], c0:c1]
 
     def copy(out, i):
-        add("V", [i], [out], lambda: g.vector.tensor_copy(ap(out), ap(i)))
+        add("V", [i], [out], lambda: g.vector.tensor_copy(ap(out), ap(i)), cost("V", out, [i], None))
 
     def tt(out, a, b, op):
-        add("V", [a, b], [out], lambda: g.vector.tensor_tensor(ap(out), ap(a), ap(b), op))
+        per = 1 if "psum" in (SCRATCH.get(a[0], "s")[0], SCRATCH[b[0]][0]) else 2
+        add("V", [a, b], [out], lambda: g.vector.tensor_tensor(ap(out), ap(a), ap(b), op), cost("V", out, [a, b], per))
 
     def ts(out, a, s1, op0, s2=None, op1=None):
         if op1 is None:
-            add("V", [a, s1], [out], lambda: g.vector.tensor_scalar(ap(out), ap(a), ap(s1), None, op0))
+            add("V", [a, s1], [out], lambda: g.vector.tensor_scalar(ap(out), ap(a), ap(s1), None, op0), cost("V", out, [a], None))
         else:
-            add("V", [a, s1, s2], [out], lambda: g.vector.tensor_scalar(ap(out), ap(a), ap(s1), ap(s2), op0, op1))
+            add("V", [a, s1, s2], [out], lambda: g.vector.tensor_scalar(ap(out), ap(a), ap(s1), ap(s2), op0, op1), cost("V", out, [a], None))
 
     def red(out, i, op):
-        add("V", [i], [out], lambda: g.vector.tensor_reduce(ap(out), ap(i), AxisListType.X, op))
+        add("V", [i], [out], lambda: g.vector.tensor_reduce(ap(out), ap(i), AxisListType.X, op), cost("V", out, [i], 1))
 
     def scan(out, d0, d1, init, op0, op1):
-        add("V", [d0, d1, init], [out], lambda: g.vector.tensor_tensor_scan(ap(out), ap(d0), ap(d1), ap(init), op0, op1))
+        add("V", [d0, d1, init], [out], lambda: g.vector.tensor_tensor_scan(ap(out), ap(d0), ap(d1), ap(init), op0, op1), cost("V", out, [d0, d1], None))
 
     def vtr(out, i):
-        add("V", [i], [out], lambda: g.vector.transpose(ap(out), ap(i)))
+        add("V", [i], [out], lambda: g.vector.transpose(ap(out), ap(i)), cost("V", out, [i], None))
 
     def fill(out, c):
-        add("V", [], [out], lambda: g.vector.memset(ap(out), c))
+        add("V", [], [out], lambda: g.vector.memset(ap(out), c), cost("V", out, [], None))
 
     def act(out, i, func, bias=None, scale=None):
         def call():
@@ -164,31 +204,33 @@ def rank_program(g, core, T, topo):
             if scale is not None:
                 kw["scale"] = ap(scale)
             return g.scalar.activation(ap(out), ap(i), func, **kw)
-        add("S", [i, scale, bias], [out], call)
+        add("S", [i, scale, bias], [out], call, cost("S", out, [i], 1))
 
-    def mm(out, l, r, start, stop):
-        add("P", [l, r], [out], lambda: g.tensor.matmul(ap(out), ap(l), ap(r), start, stop))
+    def mm(out, l, r, start, stop, join=False):
+        time = max(min(64, width(l)), width(r)) * (1 if two(l) else 4) * PE
+        add("P", [l, r], [out], lambda: g.tensor.matmul(ap(out), ap(l), ap(r), start, stop), time, lat=WAKE + 0.1, join=join)
 
     def iota(out, pattern, base, cm, small=True):
+        time = 0.13 + 2 * width(out) * CYCLE
         if small:
-            add("G", [], [out], lambda: g.iota(ap(out), pattern, base, cm, allow_small_or_imprecise_dtypes=True))
+            add("G", [], [out], lambda: g.iota(ap(out), pattern, base, cm, allow_small_or_imprecise_dtypes=True), time)
         else:
-            add("G", [], [out], lambda: g.iota(ap(out), pattern, base, cm))
+            add("G", [], [out], lambda: g.iota(ap(out), pattern, base, cm), time)
 
     def asel(out, i, pattern, cop, fillv, base, cm):
-        add("G", [i], [out], lambda: g.affine_select(ap(out), ap(i), pattern, cop, fillv, base, cm))
+        add("G", [i], [out], lambda: g.affine_select(ap(out), ap(i), pattern, cop, fillv, base, cm), 0.17 + 2 * width(out) * CYCLE)
 
     nd = [0, 0]
 
     def dma(out, i):
         sem = "d%d" % nd[0]
         nd[0] += 1
-        add("Y", [i], [out], lambda: g.sync.dma_start(ap(out), ap(i)), sem, 16)
+        add("Y", [i], [out], lambda: g.sync.dma_start(ap(out), ap(i)), 0.05, sem, 16, lat=1.6 + min(width(out), width(i)) / 1500)
 
     def dma_add(out, i):
         sem = "a%d" % nd[1]
         nd[1] += 1
-        add("G", [i, out], [out], lambda: g.dma_start(ap(out), ap(i), accum_op=OP.add, max_dma_last_dim=4096), sem, 16)
+        add("G", [i, out], [out], lambda: g.dma_start(ap(out), ap(i), accum_op=OP.add, max_dma_last_dim=4096), 0.5, sem, 16, lat=6.0)
 
     def rows(name, r, c0, src):
         dma(v(name, c0, c0 + 4096, 1, (r, 128, 16)), v(src))
@@ -198,7 +240,7 @@ def rank_program(g, core, T, topo):
 
     def bwd(out, lname, src, c0, k, first=True, last=True):
         for i in range(16):
-            mm(out, blk(lname, i), v(src, c0 + i, c0 + 16 * k, 16), first and i == 0, last and i == 15)
+            mm(out, blk(lname, i), v(src, c0 + i, c0 + 16 * k, 16), first and i == 0, last and i == 15, i > 0)
 
     def gather(onv, out, win, lst, relu=False):
         if onv and relu:
@@ -214,8 +256,11 @@ def rank_program(g, core, T, topo):
     def col(k):
         return v("COL", k, k + 1)
 
-    def ps(k, a=0, b=256):
-        return v("b%d" % k, a, b)
+    def ps(k, a=0, b=256, step=1):
+        return v("b%d" % k, a, b, step)
+
+    def w64(name, h):
+        return v(name, 64 * h, 64 * h + 64)
 
     dma(v("EI"), v("ends", 0, 4096, 1, (0, 8, 1)))
     dma(v("STI", 0, 128), v("start", 0, 128))
@@ -229,7 +274,7 @@ def rank_program(g, core, T, topo):
     asel(v("SHF"), v("ONE"), [[-1, 128]], OP.is_equal, 0.0, -1, 1)
     iota(v("LB0"), [[1, 144]], -15, 0)
     iota(v("I16"), [[1, 16]], 0, 0)
-    fill(v("TWO"), 2.0)
+    fill(v("ONEB"), 1.0)
     ts(v("PI", 1, 2), PIc, 4, OP.arith_shift_right)
     ts(v("PI", 2, 3), PIc, 15, OP.bitwise_and)
     ts(v("PI", 3, 4), v("PI", 1, 2), 1, OP.bitwise_and)
@@ -242,26 +287,24 @@ def rank_program(g, core, T, topo):
     copy(AA, v("PI", 3, 4))
     act(v("IDB"), v("ID"), ACT.Copy)
 
-    def tables(last, cut=True, between=None):
+    def tables(last, cut=True):
         if cut:
             tt(v("SZ"), ps(6), v("REM"), OP.min)
         else:
             tt(v("SZ"), v("EI"), v("VC"), OP.subtract)
         if last:
             return
-        mm(ps(7), v("IDB"), v("TWO"), True, False)
-        mm(ps(7, 255, 256), v("SHF"), v("SZ", 0, 1), False, False)
-        mm(ps(7, 0, 255), v("ID"), v("SZ", 1, 256), False, True)
+        if not cut:
+            mm(ps(6, 256, 257), v("SHF"), v("SZ", 0, 1), True, False)
+            mm(ps(6, 1, 256), v("ID"), v("SZ", 1, 256), False, True)
         act(v("KD"), v("SZ"), ACT.Sign, -1.0)
-        rows("INFO", 2, 1, "KD")
-        if between:
-            between()
-        tt(ps(5), ps(7), v("SZ"), OP.min)
-        act(v("M0"), ps(5), ACT.Copy)
+        tt(ps(5), v("SZ"), ps(6, 1, 257), OP.subtract)
+        ts(v("TW"), ps(5), 1.0, OP.is_gt)
+        tt(ps(5), ps(6, 1, 257), v("TW"), OP.mult)
+        copy(v("M0"), ps(5))
         rows("INFO", 0, 1, "M0")
-        tt(v("TW"), ps(7), v("SZ"), OP.is_le)
-        rows("INFO", 3, 1, "TW")
-        tt(v("M1"), ps(5), v("M0"), OP.subtract)
+        tt(ps(5, 256, 512), ps(5), v("KD"), OP.add)
+        tt(v("M1"), ps(5, 256, 512), v("M0"), OP.subtract)
         rows("INFO", 1, 1, "M1")
         act(v("HF"), v("SZ"), ACT.Relu, 2.0, -1.0)
     tables(False, False)
@@ -275,75 +318,74 @@ def rank_program(g, core, T, topo):
 
     def weight(name, terms):
         c = None
-        for row, wgt in terms:
+        for r, wgt in terms:
             n = col(nw[0])
             nw[0] += 1
-            act(n, v("I16", row, row + 1), ACT.Identity, c, float(wgt))
+            act(n, v("I16", r, r + 1), ACT.Identity, c, float(wgt))
             c = n
         act(v(name), v("LB0"), ACT.Copy, None, c)
-    weight("LI", [(0, 1), (1, 1), (2, BIGW), (3, -BIGW)])
-    fill(v("KS"), -2.0)
+    weight("LI", [(0, 1), (1, 1)])
+    fill(v("KS"), -1.0)
     for k in range(5):
         fill(xs(k, 4096, SL), 255.0)
-
-    def starts(t):
-        s0 = v("STI", 128 * t, 128 * t + 128)
-        ts(v("AL"), s0, 1.0, OP.add)
-        ts(v("Y0"), s0, 4.0, OP.add)
-    starts(0)
-    ts(col(4), II, 14.0, OP.is_ge, 512.0, OP.mult)
-    ts(v("REM"), v("VC"), col(4), OP.subtract, -1.0, OP.mult)
-    ts(v("REM"), v("REM"), 3584.0, OP.add)
+    ts(v("AL"), v("STI", 0, 128), 1.0, OP.add)
+    ts(v("Y0"), v("STI", 0, 128), 4.0, OP.add)
     act(v("V0"), v("VC"), ACT.Copy)
     tt(v("V1"), v("VC"), v("V0"), OP.subtract)
     copy(ps(1, 256, 512), v("VC"))
     for name in ("HL", "RL", "JL"):
         fill(v(name, 0, 1), 0.0)
     fill(v("P0"), 0.0)
-    fill(v("T2", 0, 4 * NLO), 0.0)
-    iota(v("TRI"), [[16, 8], [0, 16]], 0, 0)
+    for t in range(RO - 1):
+        fill(v("LZ%d" % t, 512, 528), 0.0)
+    asel(v("TRI"), v("ONE"), [[1, 128]], OP.is_gt, 0.0, 0, -1)
+    asel(v("TRI"), v("TRI"), [[-16, 8], [0, 16]], OP.is_ge, 0.0, 0, 1)
+    asel(v("IDP"), v("ONE"), [[-8, 2], [-16, 8], [-1, 8]], OP.is_equal, 0.0, 0, 1)
     iota(v("QW"), [[16, 256]], 0, 1)
-    iota(v("T4"), [[1, 16], [16, 16]], 0, 0)
+    iota(v("OX"), [[1, 16], [16, 16]], 0, 0)
     iota(v("T5"), [[0, 16], [1, 16]], 0, 0)
     iota(v("DM"), [[1, 16]], 12288, 16)
-    ts(v("TRI"), v("TRI"), G16, OP.is_equal)
-    asel(v("TRI"), v("TRI"), [[1, 128]], OP.is_gt, 0.0, 0, -1)
     ts(v("QW"), v("QW"), G16, OP.subtract)
-    ts(col(6), G16, 16.0, OP.mult)
-    ts(v("DM"), v("DM"), col(6), OP.subtract)
-    ts(COFF, AA, 272.0, OP.mult, -288.0, OP.add)
-    ts(v("FI"), v("T4"), AA, OP.add)
-    ts(v("FI"), v("FI"), 1, OP.arith_shift_right)
-    ts(v("T4"), v("T4"), 1.0, OP.add, v("I16", 0, 1), OP.mult)
-    ts(v("T5"), v("T5"), v("I16", 1, 2), OP.mult)
-    tt(v("T4"), v("T4"), v("T5"), OP.add)
-    ts(v("T5"), v("FI"), v("I16", 2, 3), OP.mult)
-    tt(v("CP"), v("T4"), v("T5"), OP.add)
-    iota(v("SEL"), [[0, 1024]], 1, 0)
-    asel(v("SEL"), v("SEL"), [[-1, 1024]], OP.is_equal, 0.0, 384, 1)
-    iota(v("GH"), [[0, 4128]], 0, 0)
-    rows("GH", 7, 16, "V0")
-    rows("GH", 8, 16, "V1")
-    iota(v("BIG", 0, 4096), [[0, 4096]], 0, 0)
-    iota(v("QB"), [[1, 4096]], 0, 0)
 
-    def late_constants():
-        for name, src, k in (("NIDB", "ID", -1.0), ("ID2B", "ID", 2.0), ("IDBIG", "ID", BIGW), ("IDN64", "ID", -64.0), ("IDA", "ID", float(SL)),
-                             ("NIDA", "ID", -float(SL)), ("IDM", "ID", 4096.0), ("SHFB", "SHF", 1.0), ("L1", "LB0", 1.0), ("Q0", "QW", 1.0)):
-            act(v(name), v(src), ACT.Copy, None, k)
-        weight("LM1", [(0, 288), (1, -255), (2, -544)])
-        weight("LM2", [(0, 16)])
-        weight("LE", [(0, 1)])
-        weight("LH", [(1, -1), (2, -1)])
-        weight("LJ", [(3, 1), (4, 1)])
-        weight("LD", [(1, 1), (2, 1), (5, -1), (6, -1), (7, -1), (8, -1)])
-        weight("LS", [(3, 0.5), (4, 0.5), (5, -0.5), (6, -0.5)])
-        weight("LV", [(7, 1), (8, 1)])
-        weight("LZ", [(9, 1), (10, 1)])
-    late_constants()
-    tt(v("Q1"), v("QW"), v("Q0"), OP.subtract)
+    def growth_constants():
+        ts(col(4), II, 14.0, OP.is_ge, 512.0, OP.mult)
+        ts(v("REM"), v("VC"), col(4), OP.subtract, -1.0, OP.mult)
+        ts(v("REM"), v("REM"), 3584.0, OP.add)
+        ts(col(6), G16, 16.0, OP.mult)
+        ts(v("DM"), v("DM"), col(6), OP.subtract)
+        ts(COFF, AA, 272.0, OP.mult, -288.0, OP.add)
+        ts(v("FI"), v("OX"), AA, OP.add)
+        ts(v("FI"), v("FI"), 1, OP.arith_shift_right)
+        ts(v("OX"), v("OX"), 1.0, OP.add, v("I16", 0, 1), OP.mult)
+        ts(v("T5"), v("T5"), v("I16", 1, 2), OP.mult)
+        tt(v("OX"), v("OX"), v("T5"), OP.add)
+        ts(v("T5"), v("FI"), v("I16", 2, 3), OP.mult)
+        tt(v("CP"), v("OX"), v("T5"), OP.add)
+        tt(v("Q1"), v("QW"), v("Q0"), OP.subtract)
 
-    IG, MA, MB = (0, 1024), (2048, 3072), (4096, 5120)
+    def clear_windows():
+        iota(v("SEL"), [[0, 1024]], 1, 0)
+        asel(v("SEL"), v("SEL"), [[-1, 1024]], OP.is_equal, 0.0, 384, 1)
+        iota(v("GT"), [[0, 4128]], 0, 0)
+        rows("GT", 7, 16, "V0")
+        rows("GT", 8, 16, "V1")
+        iota(v("GH"), [[0, 4128]], 0, 0)
+        iota(v("BIG", 0, 4096), [[0, 4096]], 0, 0)
+        iota(v("QB"), [[1, 4096]], 0, 0)
+
+    for name, src, k in (("NIDB", "ID", -1.0), ("ID2B", "ID", 2.0), ("IDBIG", "ID", BIGW), ("IDN64", "ID", -64.0), ("IDA", "ID", float(SL)),
+                         ("NIDA", "ID", -float(SL)), ("IDM", "IDP", 4096.0), ("SHFB", "SHF", 1.0), ("L1", "LB0", 1.0), ("Q0", "QW", 1.0)):
+        act(v(name), v(src), ACT.Copy, None, k)
+    weight("LM1", [(0, 288), (1, -255), (2, -544)])
+    weight("LM2", [(0, 16)])
+    weight("LE", [(0, 1)])
+    weight("LJ", [(3, 1), (4, 1)])
+    weight("LD", [(1, 1), (2, 1), (5, -1), (6, -1), (7, -1), (8, -1)])
+    weight("LS", [(1, 0.5), (2, 0.5), (3, 0.5), (4, 0.5), (5, -0.5), (6, -0.5), (7, -0.5), (8, -0.5)])
+    weight("LV", [(7, 1), (8, 1)])
+    weight("LZ", [(9, 1), (10, 1)])
+
+    IG, MA, MB, OH = (0, 1024), (2048, 3072), (4096, 5120), (8192, 0)
     XSLOT = (0, 3, 4, 0)
     LESS = ((1, 2), (2, 1), (3, 2))
 
@@ -354,9 +396,10 @@ def rank_program(g, core, T, topo):
             iota(xs(LESS[t][c]), [[0, 4096]], -1 - c, 0)
         for c in range(2):
             dma_add(xs(LESS[t][c]), xs(XSLOT[t]))
-
-        def w64(name, h):
-            return v(name, 64 * h, 64 * h + 64)
+        if t == 0:
+            clear_windows()
+        else:
+            iota(v("BIG", 0, 4096), [[0, 4096]], 0, 0)
 
         def big(base, h):
             return bg(base[h], base[h] + 1024)
@@ -364,84 +407,124 @@ def rank_program(g, core, T, topo):
         def info(h, s):
             act(big(IG, h), ind(v("INFO", 0, 4112), w64("AL", h)), ACT.Copy)
             mm(ps(h, 0, 64), v("IDB"), v("KS"), True, False)
-            mm(ps(h, 0, 64), v("ID"), w64("Y%d" % s, h), False, False)
+            mm(ps(h, 0, 64), v("ID"), w64("Y%d" % s, h), False, False, True)
             bwd(ps(h, 0, 64), "LI", "BIG", BO + IG[h], 64, False, True)
 
-        def first(h):
-            tt(big(MA, h), ind(X, w64("AL", h)), v("WP", 1024 * h, 1024 * h + 1024), OP.min)
-            bwd(ps(2 + h, 0, 64), "LP", "BIG", BO + MA[h], 64, True, False)
+        def first(h, k):
+            a, b = CUTS[k], CUTS[k + 1]
+            tt(bg(MA[h] + 16 * a, MA[h] + 16 * b), ind(X, v("AL", 64 * h + a, 64 * h + b)), v("WP", 1024 * h + 16 * a, 1024 * h + 16 * b), OP.min)
+            if b == 64:
+                bwd(ps(2 + h, 0, 64), "LP", "BIG", BO + MA[h], 64, True, False)
 
-        def second(h, s):
-            ts(w64("BL", h), ps(h, 0, 64), s - 3.0, OP.add, 4096.0, OP.min)
+        def second_list(h, s):
+            ts(w64("BL", h), ps(h, 0, 64), s - 3.0, OP.add)
+
+        def second(h):
             tt(big(MB, h), ind(X, w64("BL", h)), v("WP", 1024 * h, 1024 * h + 1024), OP.min)
             bwd(ps(2 + h, 0, 64), "LN", "BIG", BO + MB[h], 64, False, True)
 
-        def decide(h, s):
+        def choose(h, s):
             tt(w64("TY", h), ps(2 + h, 0, 64), w64("Y%d" % s, h), OP.max)
+
+        def enter(h, s):
             tt(w64("Y%d" % (s + 1), h), ps(h, 0, 64), w64("TY", h), OP.min)
-            if s < 3:
-                ts(w64("AL", h), w64("Y%d" % (s + 1), h), s - 2.0, OP.add)
-                info(h, s + 1)
-            else:
-                p = (64 * h, 64 * h + 64, 1)
-                mm(v("b4", 0, 128, 1, p), w64("MISS", h), v("IDM"), True, False)
-                mm(v("b4", 0, 128, 1, p), w64("Y4", h), v("ID"), False, True)
-                if h == 1:
-                    mm(ps(5, 0, 128), v("MISS"), v("IDM"), True, False)
-                    mm(ps(5, 0, 128), v("Y4"), v("ID"), False, False)
+
+        def first_list(h, s):
+            ts(w64("AL", h), w64("Y%d" % (s + 1), h), s - 2.0, OP.add)
+            info(h, s + 1)
         info(0, 0)
         info(1, 0)
-        first(0)
-        first(1)
-        second(0, 0)
-        second(1, 0)
-        for s in range(4):
-            decide(0, s)
-            if s > 0:
-                second(1, s)
+        for k in range(3):
+            first(0, k)
+        second_list(0, 0)
+        second(0)
+        first(1, 0)
+        row[0] = "walk"
+        for n in range(7):
+            h, s = n % 2, n // 2
+            o, so = 1 - h, (n + 1) // 2
+            choose(h, s)
+            first(o, 1)
+            enter(h, s)
+            second_list(o, so)
+            first(o, 2)
             if s < 3:
-                first(0)
-            else:
-                fill(bg(16384, 16512), -1.0)
-            decide(1, s)
-            if s == 1:
+                first_list(h, s)
+            second(o)
+            if s < 3:
+                first(h, 0)
+            if n == 4:
                 tt(v("MISS"), v("Y2"), v("Y1"), OP.is_lt)
-            if s < 3:
-                second(0, s + 1)
-                first(1)
-        ts(v("HIb"), ps(4, 0, 128), 1.0 / 64, OP.mult, 129 - 31.5 / 64, OP.add)
-        mm(ps(5, 0, 128), v("IDN64"), v("HIb"), False, True)
-        act(v("LOb"), ps(5, 0, 128), ACT.Identity, 64.0 * 129)
-        for k in range(64):
-            ts(bg(128 * k, 128 * k + 128), v("HIb"), 129.0 + k, OP.is_equal)
-            if NLO + k < 64:
-                n = NLO + k
-                act(bg(8192 + 128 * n, 8192 + 128 * n + 128), v("LOb"), ACT.Sign, 0.5 - n)
-        for n in range(NLO):
-            ts(bg(8192 + 128 * n, 8192 + 128 * n + 128), v("LOb"), float(n), OP.is_equal)
+
+        def digits(h):
+            HI, LO = v("DI", 128 * h, 128 * h + 64), v("DI", 128 * h + 64, 128 * h + 128)
+            for a in (0, 64):
+                o = v("b%d" % (4 + h), 0, 64, 1, (a, a + 64, 1))
+                mm(o, w64("MISS", h), v("IDM", a, a + 64), True, False)
+                mm(o, w64("Y4", h), v("IDP", a, a + 64), False, True, True)
+            ts(HI, ps(4 + h, 0, 64), 1.0 / 64, OP.mult, 129 - 31.5 / 64, OP.add)
+            for a in (0, 64):
+                o = v("b%d" % (4 + h), 64, 128, 1, (a, a + 64, 1))
+                mm(o, w64("Y4", h), v("IDP", a, a + 64), True, False)
+                mm(o, v("IDN64", a, a + 64), HI, False, True, True)
+            act(LO, ps(4 + h, 64, 128), ACT.Identity, 65.0 * 129)
+
+        def one_hot(h, a, b):
+            for k in range(a, b):
+                ts(bg(OH[h] + 128 * k, OH[h] + 128 * k + 128), v("DI", 128 * h, 128 * h + 128), 129.0 + k, OP.is_equal)
+
+        def one_hot_scalar(h):
+            for k in range(NS[h]):
+                o = bg(OH[h] + 128 * k, OH[h] + 128 * k + 128)
+                act(o, v("DI", 128 * h, 128 * h + 128), ACT.Abs, -129.0 - k)
+                act(o, o, ACT.Relu, 1.0, -1.0)
+
+        def counts(h, gh):
+            bank = (3, 4, 5, 6)[gh] if h else (6, 3)[gh % 2]
+            for gg in (2 * gh, 2 * gh + 1):
+                for i in range(8):
+                    c = OH[h] + 8 * gg + i
+                    mm(v("b%d" % bank, 0, 64, 1, (64 * (gg % 2), 64 * (gg % 2) + 64, 1)), bg(c, OH[h] + 8192, 128), bg(c + 64, OH[h] + 8192, 128),
+                       i == 0, i == 7, i > 0)
+            o = v("HB", 256 * h + 64 * gh, 256 * h + 64 * gh + 64)
+            if h == 1 and gh >= 2:
+                copy(o, ps(bank, 0, 64))
+            else:
+                act(o, ps(bank, 0, 64), ACT.Copy)
+            for cc in range(4):
+                a = 384 - 128 * gh + cc
+                mm(ps(7, 64 * cc, 64 * cc + 64), v("SEL", a, a + 512, 4), o, h + gh + cc == 0, h + gh + cc == 7, cc > 0)
+        digits(0)
+        one_hot_scalar(0)
         mm(ps(0), v("ID"), v("VC"), True, False)
         mm(ps(0), v("ID"), v("SZ"), False, False)
         mm(ps(0, 256, 257), v("SHF"), v("VC", 0, 1), False, False)
         mm(ps(0, 256, 257), v("SHF"), v("SZ", 0, 1), False, True)
+        if not last:
+            ts(v("Y0"), v("STI", 128 * t + 128, 128 * t + 256), 4.0, OP.add)
+        choose(1, 3)
+        one_hot(0, NS[0], NS[0] + 3)
+        enter(1, 3)
+        one_hot(0, NS[0] + 3, NS[0] + 14)
+        digits(1)
+        one_hot_scalar(1)
+        one_hot(0, NS[0] + 14, 64)
+        one_hot(1, NS[1], 64)
+        row[0] = None
         mm(ps(1), v("ID"), v("VC"), True, False)
         mm(ps(2), v("ID"), v("VC"), True, False)
-        for gg in range(8):
-            for i in range(16):
-                c = 16 * gg + i
-                mm(v("b6", gg // 2, 260, 4, (64 * (gg % 2), 64 * (gg % 2) + 64, 1)), bg(c, 8192, 128), bg(8192 + c, 16512, 128), i == 0, i == 15)
         ts(v("EL", 0, 257), ps(0, 0, 257), -1.0, OP.add)
         tt(v("TWE"), ps(0), v("TW"), OP.mult)
         tt(v("KDE"), ps(0), v("KD"), OP.mult)
         if not last:
-            starts(t + 1)
-        copy(v("T2", 4 * NLO, 256), ps(6, 4 * NLO + 4, 260))
-        tt(v("HB"), ps(6), v("T2"), OP.subtract)
-        for cc in range(4):
+            ts(v("AL"), v("STI", 128 * t + 128, 128 * t + 256), 1.0, OP.add)
+        if t == 0:
+            growth_constants()
+        for h in range(2):
             for gh in range(4):
-                a = 384 - 128 * gh + cc
-                mm(ps(7, 64 * cc, 64 * cc + 64), v("SEL", a, a + 512, 4), v("HB", gh, 256, 4), gh == 0, gh == 3)
+                counts(h, gh)
         tt(v("HM"), ps(7), v("HF"), OP.min)
-        rows("GH", 0, 15, "HM")
+        rows("GT", 0, 15, "HM")
         scan(v("HL", 1, 257), v("HM"), v("HM"), 0.0, OP.add, OP.max)
         mm(ps(3, 0, 255), v("IDB"), v("HM", 1, 256), True, False)
         mm(ps(3, 255, 256), v("SHFB"), v("HM", 0, 1), False, True)
@@ -454,127 +537,104 @@ def rank_program(g, core, T, topo):
         ts(v("DO"), v("DO"), 15.5, OP.is_gt)
         tt(v("DO"), v("DO"), v("DM"), OP.mult)
         tt(v("H1"), ps(4), v("H0"), OP.subtract)
+        tt(v("T1"), v("VC"), ps(4), OP.subtract)
         mm(ps(2), v("NIDB"), v("H0"), False, False)
         mm(ps(2), v("NIDB"), v("H1"), False, False)
         mm(ps(2), v("IDB"), v("HM"), False, True)
-        GHW = v("GH", 16, 4112)
-        for k in (0, 2, 1, 3):
-            w = 65 if k == 3 else 64
-            gather(k < 2, bg(1024 * k, 1024 * k + 16 * w), GHW, v("EL", 64 * k, 64 * k + w))
-            bwd(ps(5, 64 * k, 64 * k + w), "LE", "BIG", BO + 1024 * k, w)
-        rows("GH", 1, 16, "H0")
-        rows("GH", 2, 16, "H1")
+        GHW, GTW = v("GH", 16, 4112), v("GT", 16, 4112)
+        for onv, a, b in ENDS1:
+            gather(onv, bg(16 * a, 16 * b), GTW, v("EL", a, b))
+            bwd(ps(5, a, b), "LE", "BIG", BO + 16 * a, b - a)
+        rows("GT", 1, 16, "H0")
+        rows("GT", 2, 16, "H1")
 
-        def carry(src):
+        def carry(src, k):
             ts(v("DG"), v("I16"), src, OP.mult)
             mm(ps(7, 272, 288), v("TRI"), v("DG"), True, True)
+            red(v("RC", k, k + 1), ps(7, 272, 288), OP.max)
+            return v("RC", k, k + 1)
         tt(v("T4"), ps(5, 1, 257), v("TWE"), OP.mult)
         scan(v("RL", 1, 257), v("T4"), v("HK"), 0.0, OP.max, OP.max)
-        carry(v("RL", 256, 257))
-        red(v("RC", 0, 1), ps(7, 272, 288), OP.max)
-        ts(v("RS", 0, 257), v("RL", 0, 257), v("RC", 0, 1), OP.max)
+        ts(v("RS", 0, 257), v("RL", 0, 257), carry(v("RL", 256, 257), 0), OP.max)
         tt(v("KI"), v("RS", 1, 257), ps(1), OP.is_gt)
         scan(v("JL", 1, 257), v("KI"), v("KI"), 0.0, OP.add, OP.add)
         mm(ps(7, 257, 258), v("TRI"), v("JL", 256, 257), True, True)
         act(v("OUT"), v("KI"), ACT.Identity, 1.0, -1.0)
+        act(v("OUT"), v("OUT"), ACT.Identity, THIRD, 1.0 - THIRD)
         tt(v("OX"), v("RS", 0, 256), ps(1, 256, 512), OP.is_le)
         ts(ps(4, 0, 257), v("JL", 0, 257), ps(7, 257, 258), OP.add)
-        tt(v("T5"), ps(4), v("OX"), OP.mult)
-        act(v("J0"), ps(4, 1, 257), ACT.Copy)
+        tt(ps(3), ps(4, 1, 257), v("T1"), OP.add)
+        act(v("J0"), ps(3), ACT.Copy)
         rows("GH", 3, 16, "J0")
-        scan(v("LQ"), v("T5"), v("T5"), 0.0, OP.max, OP.max)
-        carry(v("LQ", 255, 256))
-        tt(v("J1"), ps(4, 1, 257), v("J0"), OP.subtract)
+        tt(v("T5"), ps(4), v("OX"), OP.mult)
+        tt(v("J1"), ps(3), v("J0"), OP.subtract)
         rows("GH", 4, 16, "J1")
-        red(v("RC", 1, 2), ps(7, 272, 288), OP.max)
-        ts(v("T6"), v("LQ"), v("RC", 1, 2), OP.max)
+        rows("GT", 3, 16, "J0")
+        rows("GT", 4, 16, "J1")
+        scan(v("LQ"), v("T5"), v("T5"), 0.0, OP.max, OP.max)
+        above = carry(v("LQ", 255, 256), 1)
+        ts(v("T6"), v("LQ"), above, OP.max)
         tt(v("P0", 16, 272), ps(2), v("T6"), OP.add)
         act(v("U0"), v("T6"), ACT.Copy)
-        tt(v("O16"), v("P0", 16, 272, 16), v("DO"), OP.max)
-        copy(v("OFF"), v("O16"))
+        tt(v("O16"), ps(2, 0, 256, 16), v("LQ", 0, 256, 16), OP.add)
+        tt(v("O16"), v("O16"), v("DO"), OP.max)
+        ts(ps(7, 288, 304), ps(2, 0, 256, 16), above, OP.add)
+        tt(v("DO"), ps(7, 288, 304), v("O16"), OP.max)
+        copy(v("OFF"), v("DO"))
         copy(ind(v("BIG", 0, VLS), v("OFF")), v("CP"))
-        mm(ps(1), v("ID"), v("SZ"), True, False)
-        mm(ps(1), v("IDB"), v("H0"), False, False)
-        mm(ps(1), v("IDB"), v("H1"), False, False)
+        mm(ps(1), v("IDB"), v("ONEB"), True, False)
+        mm(ps(1), v("NIDB"), v("J0"), False, False)
+        mm(ps(1), v("NIDB"), v("J1"), False, False)
         mm(ps(1), v("NIDB"), v("HM"), False, False)
-        mm(ps(2), v("NIDB"), v("J0"), True, False)
-        mm(ps(2), v("NIDB"), v("J1"), False, False)
-        mm(ps(2), v("ID2B"), v("KI"), False, False)
-
-        def ends2_sums(k):
-            bwd(ps(1, 64 * k, 64 * k + 64), "LH", "G", 1024 * k, 64, False, k == 3)
-            bwd(ps(2, 64 * k, 64 * k + 64), "LJ", "G", 1024 * k, 64, False, k == 3)
-        for k in range(4):
-            gather(False, v("G", 1024 * k, 1024 * k + 1024), GHW, w64("EL", k))
+        mm(ps(1), v("ID2B"), v("KI"), False, False)
         for k in range(4):
             a = 1024 * k
             scan(v("BIG", VLS + a, VLS + a + 1024), v("BIG", a, a + 1024), v("BIG", a, a + 1024),
                  0.0 if k == 0 else v("BIG", VLS + a - 1, VLS + a), OP.max, OP.max)
             bwd(ps(5, 64 * k, 64 * k + 64), "LM1", "BIG", VLS + a, 64)
-        iota(v("BIG", 0, 4096), [[0, 4096]], 0, 0)
         vtr(v("PW", 0, 256), v("P0", 16, 272))
         vtr(v("PW", 256, 544), v("P0", 0, 288))
+        for onv, a, b in ENDS2:
+            gather(onv, v("G", 16 * a, 16 * b), GHW, v("EL", a, b))
+            bwd(ps(1, a, b), "LJ", "G", 16 * a, b - a, False, b == 256)
         ts(v("ML"), ps(5), COFF, OP.add)
-
-        def ub(k):
-            return ps(3 * (k % 2), 64 * (k // 2), 64 * (k // 2) + 64)
-
-        def ulist(k):
-            ts(w64("UL", k), ub(k), -17.0, OP.add)
-        for n, k in enumerate((3, 2, 1, 0)):
+        tt(v("U1"), v("T6"), v("U0"), OP.subtract)
+        rows("GT", 5, 16, "U0")
+        rows("GT", 6, 16, "U1")
+        tt(ps(1), ps(1), v("OUT"), OP.mult)
+        copy(v("Z0"), ps(1))
+        rows("GT", 9, 16, "Z0")
+        tt(v("Z1"), ps(1), v("Z0"), OP.subtract)
+        rows("GT", 10, 16, "Z1")
+        for k, bank in ((3, 0), (2, 3), (1, 2), (0, 4)):
             a = 1024 * k
-            if n == 3:
-                tt(v("T5"), ps(2), v("OUT"), OP.mult)
-                tt(ps(1), ps(1), v("T5"), OP.add)
-                act(v("Z0"), ps(1), ACT.Copy)
-                rows("GH", 9, 16, "Z0")
-                ulist(2)
-                tt(v("Z1"), ps(1), v("Z0"), OP.subtract)
-                rows("GH", 10, 16, "Z1")
-            if n == 2:
-                tt(v("U1"), v("T6"), v("U0"), OP.subtract)
-                rows("GH", 5, 16, "U0")
-                rows("GH", 6, 16, "U1")
-                ulist(3)
-            if n < 2:
-                ends2_sums(2 * n)
-            bwd(ub(k), "LM2", "BIG", VLS + a, 64, True, False)
-            if n < 2:
-                ends2_sums(2 * n + 1)
+            bwd(ps(bank, 0, 64), "LM2", "BIG", VLS + a, 64, True, False)
             tt(v("BIG", CMP + a, CMP + a + 1024), ind(v("PW"), w64("ML", k)), v("QB", a, a + 1024), OP.is_le)
-            bwd(ub(k), "L1", "BIG", CMP + a, 64, False, True)
-        ulist(1)
-
-        def h128(name, h):
-            return v(name, 128 * h, 128 * h + 128)
-        for h in (1, 0):
-            mm(ps(4 + h, 0, 128), v("IDB"), h128("Q0", h), True, False)
-            mm(ps(4 + h, 0, 128), v("IDB"), h128("Q1", h), False, False)
-        for k, opens in ((3, True), (2, False), (1, True), (0, False)):
-            h, a, c = k // 2, 1024 * k, 64 * (k % 2)
-            if k == 1:
-                ulist(0)
-            gather(k % 2 == 1, v("G", a, a + 1024), GHW, w64("UL", k))
-            bwd(ps(4 + h, c, c + 64), "LD", "G", a, 64, False, not opens)
-            bwd(ps(6 + h, c, c + 64), "LS", "G", a, 64, opens, not opens)
-
-        def decode(h):
-            bd, bs = ps(4 + h, 0, 128), ps(6 + h, 0, 128)
-            act(h128("SF", h), bs, ACT.Copy)
-            act(h128("SG", h), bd, ACT.Sign)
-            tt(h128("T4", h), bd, h128("SF", h), OP.is_gt)
-            tt(h128("CC", h), h128("T4", h), h128("SG", h), OP.add)
-            tt(bd, bs, h128("CC", h), OP.mult)
-            tt(h128("T4", h), h128("QW", h), bd, OP.subtract)
-            copy(h128("QL", h), h128("T4", h))
+            bwd(ps(bank, 0, 64), "L1", "BIG", CMP + a, 64, False, True)
+            ts(w64("UL", k), ps(bank, 0, 64), -17.0, OP.add)
+        for onv, k in RUNS:
+            gather(onv, v("G", 1024 * k, 1024 * k + 1024), GTW, w64("UL", k))
+        for n, (onv, k) in enumerate(RUNS):
+            bd, bs, one, cs = ps(4 + n % 2, 0, 64), ps(6 + n % 2, 0, 64), ps(4 + n % 2, 128, 192), ps(4 + n % 2, 256, 320)
+            mm(bd, v("IDB"), w64("Q0", k), True, False)
+            mm(bd, v("IDB"), w64("Q1", k), False, False, True)
+            bwd(bs, "LS", "G", 1024 * k, 64)
+            bwd(bd, "LD", "G", 1024 * k, 64, False, True)
+            copy(w64("SF", k), bs)
+            ts(one, bd, 1.0, OP.min)
+            tt(w64("T4", k), bd, w64("SF", k), OP.is_gt)
+            tt(w64("CC", k), one, w64("T4", k), OP.add)
+            tt(cs, bs, w64("CC", k), OP.mult)
+            tt(w64("T5", k), w64("QW", k), cs, OP.subtract)
+            copy(w64("QL", k), w64("T5", k))
         dst = T.cores[(rank + 1) % len(T.cores)]
         src = T.cores[(rank - 1) % len(T.cores)]
 
         def send(frm, to, rsem, lsem):
             rid, pid, _se = topo.addr(dst)
             add("G", [frm], [], lambda: g.remote_dma(ap(to), ap(frm), T.sem[rsem], T.sem[lsem], pid, rid, topo.mask(core, dst)),
-                lsem, len(topo.engines(core, dst)), False)
-            add("R", [], [to], None, rsem, len(topo.engines(src, core)))
+                0.3, lsem, len(topo.engines(core, dst)), False, 3.0)
+            add("R", [], [to], None, 0.0, rsem, len(topo.engines(src, core)), lat=0.1)
 
         def copy0(onv, a, b):
             gather(onv, v("GQ", a, b), v("G", 0, 2048 if b <= 2048 else 4096), v("QL", a // 16, b // 16))
@@ -593,48 +653,117 @@ def rank_program(g, core, T, topo):
                 dma(v("y", a, b), xs(XN, a, b))
 
         def size_sums(lo, hi):
+            w = 256 if last else 257
             for i in range(lo, hi):
                 a = 256 * i
-                s = v("GQ", a, a + 256) if i < 14 else v("LZ%d" % t, a - 3584, a - 3584 + 256)
-                mm(ps(6), blk("LZ", i), s, i == 8, i == 15)
-        decode(1)
-        copy0(False, 3584, 4096)
-        send(v("GQ", 3584, 4096), v("LZ%d" % t), "rz%d" % t, "lz%d" % t)
-        decode(0)
-        copy0(False, 2048, 3584)
-        xlist(0, 3584, 4096)
-        copy0(True, 0, 1024)
-        newx(False, 3584, 4096)
+                s = v("GQ", a, a + w) if i < 14 else v("LZ%d" % t, a - 3584, a - 3584 + w)
+                mm(ps(6, 0, w), blk("LZ", i), s, i == 8, i == 15)
         land = v("LX") if last else xs(XN, 3584, 4096)
+        copy0(False, 3584, 4096)
+        send(v("GQ", 3584, 4096), v("LZ%d" % t, 0, 512), "rz%d" % t, "lz%d" % t)
+        xlist(0, 3584, 4096)
+        newx(False, 3584, 4096)
         send(v("XS"), land, "rx%d" % t, "lx%d" % t)
+        for onv, a, b in COPY:
+            copy0(onv, a, b)
         size_sums(8, 14)
-        copy0(True, 1024, 2048)
-        xlist(3, 2048, 3584)
         size_sums(0, 8)
-        xlist(0, 0, 1024)
         size_sums(14, 16)
-        newx(False, 2048, 3584)
+        for bank, a, b in ((3, 2048, 3584), (0, 0, 1024), (2, 1024, 2048)):
+            xlist(bank, a, b)
+        tables(last)
+        for onv, a, b in NEWX:
+            newx(onv, a, b)
         if last:
-            newx(True, 0, 1024)
-            xlist(3, 1024, 2048)
-            newx(False, 1536, 2048)
-            newx(True, 1024, 1536)
-            tables(True)
             tt(v("T1"), ps(1, 256, 512), v("SZ"), OP.add)
             dma(v("ye", 0, 4096, 1, (0, 8, 1)), v("T1"))
             dma(v("y", 3584, 4096), land)
-        else:
-            newx(True, 0, 512)
-            tables(False, True, lambda: newx(True, 512, 1024))
-            xlist(3, 1024, 2048)
-            newx(False, 1536, 2048)
-            newx(True, 1024, 1536)
+
+    hist = {}
+    lastq = {}
+    for k, o in enumerate(ops):
+        q = o["q"]
+        o["k"] = k
+        deps, order = {}, {}
+        for wr, lst in ((0, o["r"]), (1, o["w"])):
+            for x in lst:
+                name = x[0]
+                psum = SCRATCH.get(name, "d")[0] == "psum"
+                m = pm(x[1])
+                keep = []
+                for h in hist.get(name, []):
+                    ho, hw, hx = h
+                    over = (pm(hx[1]) & m) and hx[2] < x[3] and x[2] < hx[3]
+                    if psum and ho["q"] != q:
+                        deps[ho["k"]] = ho
+                    elif psum and q == "P":
+                        order[ho["k"]] = ho
+                        continue
+                    elif over and (wr or hw):
+                        deps[ho["k"]] = ho
+                    if wr and not psum and hx[2] >= x[2] and hx[3] <= x[3] and (pm(hx[1]) & ~m) == 0 and x[4] == 1:
+                        continue
+                    keep.append(h)
+                hist[name] = keep
+        key = q if q == "G" else (q, o["row"])
+        if key in lastq and (q == "G" or q == "V" and o["row"]):
+            order[lastq[key]["k"]] = lastq[key]
+        if q == "R":
+            order[k - 1] = ops[k - 1]
+        lastq[key] = o
+        deps.pop(k, None)
+        order.pop(k, None)
+        o["deps"], o["order"] = list(deps.values()), list(order.values())
+        for wr, lst in ((0, o["r"]), (1, o["w"])):
+            for x in lst:
+                hist.setdefault(x[0], []).append((o, wr, x))
+
+    for o in ops:
+        o["next"] = []
+    for o in ops:
+        o["left"] = len(o["deps"]) + len(o["order"])
+        for d in o["deps"] + o["order"]:
+            d["next"].append(o)
+    for o in reversed(ops):
+        o["way"] = o["cost"] + o["lat"] + max([n["way"] for n in o["next"]] + [0.0])
+    ready = {q: [] for q in "VSPGYR"}
+    free = {q: 0.0 for q in ready}
+    for o in ops:
+        if o["left"] == 0:
+            o["at"] = 0.0
+            ready[o["q"]].append(o)
+
+    def pick(q):
+        now = free[q]
+        top = max(ready[q], key=lambda z: (z["way"], -z["k"]))
+        best, gain = top, None
+        for o in ready[q]:
+            if o is top or max(o["at"], now) >= max(top["at"], now):
+                continue
+            end = max(o["at"], now) + o["cost"]
+            before = max(max(end, top["at"]) + top["way"], max(o["at"], now) + o["way"])
+            after = max(top["at"] + top["way"], top["at"] + top["cost"] + o["way"])
+            if before <= after + SLACK and (gain is None or o["way"] > gain):
+                best, gain = o, o["way"]
+        return best
+    issued = []
+    while len(issued) < len(ops):
+        o = min((pick(q) for q in ready if ready[q]), key=lambda z: (max(z["at"], free[z["q"]]), z["k"]))
+        q = o["q"]
+        ready[q].remove(o)
+        free[q] = max(o["at"], free[q]) + o["cost"]
+        o["go"], o["end"] = free[q], free[q] + o["lat"]
+        issued.append(o)
+        for n in o["next"]:
+            n["left"] -= 1
+            if n["left"] == 0:
+                n["at"] = max([d["end"] for d in n["deps"]] + [d["end"] if n["q"] == "R" else d["go"] for d in n["order"]])
+                ready[n["q"]].append(n)
 
     qidx = {}
-    hist = {}
     known = {}
     need = set()
-    for k, o in enumerate(ops):
+    for k, o in enumerate(issued):
         q = o["q"]
         o["k"] = k
         if o["sem"] is None:
@@ -642,33 +771,10 @@ def rank_program(g, core, T, topo):
             qidx[q] = qidx.get(q, 0) + 1
         else:
             o["tok"] = ("*" + o["sem"], 0)
-        deps = []
-        for wr, lst in ((0, o["r"]), (1, o["w"])):
-            for x in lst:
-                name = x[0]
-                psum = name[0] == "b" and len(name) == 2
-                m = pm(x[1])
-                keep = []
-                for h in hist.get(name, []):
-                    ho, hw, hx = h
-                    over = (pm(hx[1]) & m) and hx[2] < x[3] and x[2] < hx[3]
-                    same = ho["q"] == q and o["sem"] is None and ho["sem"] is None
-                    if psum and not same:
-                        deps.append(ho)
-                    elif psum and q == "P":
-                        pass
-                    elif over and (wr or hw):
-                        deps.append(ho)
-                    if wr and not psum and hx[2] >= x[2] and hx[3] <= x[3] and (pm(hx[1]) & ~m) == 0 and x[4] == 1:
-                        continue
-                    keep.append(h)
-                if psum and len(keep) > 200:
-                    keep = keep[-200:]
-                hist[name] = keep
         kn = known.setdefault(q if q != "R" else ("R", k), {})
         waits = []
         best = {}
-        for ho in deps:
+        for ho in o["deps"]:
             tq, ti = ho["tok"]
             if tq not in best or best[tq]["tok"][1] < ti:
                 best[tq] = ho
@@ -684,13 +790,10 @@ def rank_program(g, core, T, topo):
             kn[tq] = max(kn.get(tq, -1), ti)
         o["waits"] = waits
         o["kn"] = dict(kn)
-        for wr, lst in ((0, o["r"]), (1, o["w"])):
-            for x in lst:
-                hist.setdefault(x[0], []).append((o, wr, x))
     cnt = {}
     eng_of = {"V": g.vector, "S": g.scalar, "P": g.tensor, "G": g, "Y": g.sync}
     sem_of = {"V": "sV", "S": "sS", "P": "sP", "G": "sG"}
-    for o in ops:
+    for o in issued:
         q = o["q"]
         if q == "R":
             o["val"] = o["n"]
@@ -698,7 +801,8 @@ def rank_program(g, core, T, topo):
         e = eng_of[q]
         for ho in o["waits"]:
             e.wait_ge(T.sem[ho["sem"] or sem_of[ho["q"]]], ho["val"])
-        r = o["call"]()
+        for call in o["calls"]:
+            r = call()
         if o["sem"] is not None:
             o["val"] = o["n"]
             if o["own"]:
@@ -710,6 +814,6 @@ def rank_program(g, core, T, topo):
     for q in ("V", "S", "P", "G"):
         if cnt.get(q, 0):
             g.wait_ge(T.sem[sem_of[q]], cnt[q])
-    for o in ops:
+    for o in issued:
         if o["sem"] is not None:
             g.wait_ge(T.sem[o["sem"]], o["n"])

@@ -7,14 +7,14 @@ RO = 3
 SL = 4224
 BIGW = 8192.0
 THIRD = 11184811 / 2 ** 25
-CUTS = (0, 48, 56, 64)
+CUTS = (0, 52, 58, 64)
 NS = (12, 12)
-ENDS1 = ((True, 0, 64), (False, 144, 208), (False, 208, 257), (True, 64, 144))
-ENDS2 = ((False, 0, 64), (False, 64, 128), (False, 128, 224), (True, 224, 256))
+ENDS1 = ((False, 144, 208), (True, 0, 64), (False, 208, 257), (True, 64, 144))
+ENDS2 = ((False, 0, 64), (False, 64, 128), (True, 208, 256), (False, 128, 208))
 RUNS = ((False, 3), (False, 2), (True, 1), (False, 0))
-COPY = ((False, 3072, 3584), (False, 2048, 3072), (False, 1024, 2048), (True, 0, 1024))
-NEWX = ((False, 2048, 3584), (True, 0, 1024), (False, 1536, 2048), (True, 1024, 1536))
-CYCLE, PE, WAKE, GATHER, SCATTER, SLACK = 0.00083, 0.00058, 0.18, 1.3, 2.5, 0.2
+SPLIT = 768
+NEWX = ((False, 2048, 3072), (True, 3072, 3584), (False, 1024, 2048), (True, 0, 1024))
+CYCLE, PE, WAKE, GATHER, SCATTER, SLACK, FAR = 0.00083, 0.00058, 0.18, 1.3, 2.5, 0.2, 4.0
 
 SCRATCH = {
     "BIG": ("sbuf", [128, 20736], "bfloat16"),
@@ -39,12 +39,10 @@ SCRATCH = {
     "OFF": ("sbuf", [128, 16], "uint16"),
     "PI": ("sbuf", [128, 4], "int32"),
     "COL": ("sbuf", [128, 48], "float32"),
-    "RC": ("sbuf", [128, 8], "float32"),
     "PW": ("sbuf", [128, 544], "float32"),
     "P0": ("sbuf", [128, 288], "float32"),
     "LB0": ("sbuf", [128, 144], "float32"),
     "HB": ("sbuf", [128, 512], "bfloat16"),
-    "KS": ("sbuf", [128, 64], "bfloat16"),
 }
 for _n in ("ML", "UL", "QL", "XL"):
     SCRATCH[_n] = ("sbuf", [128, 256], "uint16")
@@ -52,22 +50,26 @@ for _t in range(RO):
     SCRATCH["LZ%d" % _t] = ("sbuf", [128, 528], "bfloat16")
 for _n in ("LP", "LN", "L1", "LI", "LM1", "LM2", "LE", "LJ", "LD", "LS", "LV", "LZ"):
     SCRATCH[_n] = ("sbuf", [128, 144], "bfloat16")
-for _n in ("ID", "IDP", "TRI", "SHF", "ONE", "TY", "Y0", "Y1", "Y2", "Y3", "Y4"):
+for _n in ("ID", "IDH", "IDP", "TRI", "SHF", "ONE", "TY", "Y0", "Y1", "Y2", "Y3", "Y4"):
     SCRATCH[_n] = ("sbuf", [128, 128], "float32")
-for _n in ("IDM", "MISS", "IDB", "NIDB", "ID2B", "IDBIG", "IDN64", "IDA", "NIDA", "SHFB"):
+for _n in ("IDM", "MISS", "IDB", "NIDB", "ID2B", "IDBIG", "NIDBIG", "IDHB", "NIDH", "IDN64", "IDA", "NIDA", "SHFB"):
     SCRATCH[_n] = ("sbuf", [128, 128], "bfloat16")
-for _n in ("I16", "DM", "DO", "DG", "O16"):
+for _n in ("I16", "DM", "DO", "O16"):
     SCRATCH[_n] = ("sbuf", [128, 16], "float32")
-for _n in ("VC", "REM", "QW", "SZ", "HF", "TWE", "KDE", "HK", "OX", "OUT", "LQ", "T6", "SF", "T1", "T4", "T5"):
+SCRATCH["DG"] = ("sbuf", [128, 40], "float32")
+SCRATCH["U17"] = ("sbuf", [128, 17], "float32")
+SCRATCH["NB17"] = ("sbuf", [128, 17], "bfloat16")
+for _n in ("VC", "REM", "QW", "SZ", "HF", "TWE", "KDE", "HK", "OX", "OUT", "JL", "LQ", "T6", "SF", "T1", "T4", "T5"):
     SCRATCH[_n] = ("sbuf", [128, 256], "float32")
-for _n in ("HL", "RL", "RS", "JL"):
+for _n in ("HL", "RL", "RS"):
     SCRATCH[_n] = ("sbuf", [128, 264], "float32")
-for _n in ("CP", "ONEB", "KD", "TW", "HM", "KI", "CC", "M0", "M1", "H0", "H1", "J0", "J1", "U0", "U1", "Z0", "Z1", "V0", "V1", "Q0", "Q1"):
+SCRATCH["ONEB"] = ("sbuf", [128, 264], "bfloat16")
+for _n in ("CP", "KD", "TW", "HM", "KI", "CC", "M0", "M1", "H0", "H1", "J0", "J1", "U0", "U1", "Z0", "Z1", "V0", "V1", "Q0", "Q1"):
     SCRATCH[_n] = ("sbuf", [128, 256], "bfloat16")
 for _n in range(8):
     SCRATCH["b%d" % _n] = ("psum", [128, 512], "float32")
 
-SEMAPHORES = (["sV", "sS", "sP", "sG"] + ["d%d" % _k for _k in range(80)] + ["a%d" % _k for _k in range(2 * RO)]
+SEMAPHORES = (["sV", "sS", "sP", "sG"] + ["d%d" % _k for _k in range(80)] + ["a%d" % _k for _k in range(2 * RO + 2)]
               + ["%s%d" % (_a, _k) for _a in ("rx", "rz", "lx", "lz") for _k in range(RO)])
 
 ALL = (0, 128, 1)
@@ -108,6 +110,7 @@ def rank_program(g, core, T, topo):
     ops = []
     masks = {}
     row = [None]
+    KEPT = {"walk": "V", "rows": "Y", "blocks": "P", "end": "PS"}
 
     def pm(p):
         if p not in masks:
@@ -227,13 +230,18 @@ def rank_program(g, core, T, topo):
         nd[0] += 1
         add("Y", [i], [out], lambda: g.sync.dma_start(ap(out), ap(i)), 0.05, sem, 16, lat=1.6 + min(width(out), width(i)) / 1500)
 
-    def dma_add(out, i):
+    def dma_add(out, i, adds=True):
         sem = "a%d" % nd[1]
         nd[1] += 1
-        add("G", [i, out], [out], lambda: g.dma_start(ap(out), ap(i), accum_op=OP.add, max_dma_last_dim=4096), 0.5, sem, 16, lat=6.0)
+        if adds:
+            add("G", [i, out], [out], lambda: g.dma_start(ap(out), ap(i), accum_op=OP.add, max_dma_last_dim=4096), 0.5, sem, 16, lat=6.0)
+        else:
+            add("G", [i], [out], lambda: g.dma_start(ap(out), ap(i)), 0.5, sem, 16, lat=6.0)
 
     def rows(name, r, c0, src):
+        was, row[0] = row[0], "rows"
         dma(v(name, c0, c0 + 4096, 1, (r, 128, 16)), v(src))
+        row[0] = was
 
     def blk(lname, i):
         return v(lname, 15 - i, 143 - i)
@@ -297,7 +305,7 @@ def rank_program(g, core, T, topo):
         if not cut:
             mm(ps(6, 256, 257), v("SHF"), v("SZ", 0, 1), True, False)
             mm(ps(6, 1, 256), v("ID"), v("SZ", 1, 256), False, True)
-        act(v("KD"), v("SZ"), ACT.Sign, -1.0)
+        ts(v("KD"), v("SZ"), 1.0, OP.is_gt)
         tt(ps(5), v("SZ"), ps(6, 1, 257), OP.subtract)
         ts(v("TW"), ps(5), 1.0, OP.is_gt)
         tt(ps(5), ps(6, 1, 257), v("TW"), OP.mult)
@@ -325,7 +333,6 @@ def rank_program(g, core, T, topo):
             c = n
         act(v(name), v("LB0"), ACT.Copy, None, c)
     weight("LI", [(0, 1), (1, 1)])
-    fill(v("KS"), -1.0)
     for k in range(5):
         fill(xs(k, 4096, SL), 255.0)
     ts(v("AL"), v("STI", 0, 128), 1.0, OP.add)
@@ -333,7 +340,7 @@ def rank_program(g, core, T, topo):
     act(v("V0"), v("VC"), ACT.Copy)
     tt(v("V1"), v("VC"), v("V0"), OP.subtract)
     copy(ps(1, 256, 512), v("VC"))
-    for name in ("HL", "RL", "JL"):
+    for name in ("HL", "RL"):
         fill(v(name, 0, 1), 0.0)
     fill(v("P0"), 0.0)
     for t in range(RO - 1):
@@ -345,6 +352,7 @@ def rank_program(g, core, T, topo):
     iota(v("OX"), [[1, 16], [16, 16]], 0, 0)
     iota(v("T5"), [[0, 16], [1, 16]], 0, 0)
     iota(v("DM"), [[1, 16]], 12288, 16)
+    iota(v("U17"), [[1, 17]], 0, 0)
     ts(v("QW"), v("QW"), G16, OP.subtract)
 
     def growth_constants():
@@ -352,7 +360,10 @@ def rank_program(g, core, T, topo):
         ts(v("REM"), v("VC"), col(4), OP.subtract, -1.0, OP.mult)
         ts(v("REM"), v("REM"), 3584.0, OP.add)
         ts(col(6), G16, 16.0, OP.mult)
-        ts(v("DM"), v("DM"), col(6), OP.subtract)
+        ts(v("DM"), v("DM"), col(6), OP.subtract, 0.5, OP.mult)
+        ts(v("U17"), v("U17"), II, OP.is_ge)
+        ts(v("NB17", 0, 16), v("U17", 0, 16), -BIGW, OP.mult)
+        fill(v("NB17", 16, 17), 0.0)
         ts(COFF, AA, 272.0, OP.mult, -288.0, OP.add)
         ts(v("FI"), v("OX"), AA, OP.add)
         ts(v("FI"), v("FI"), 1, OP.arith_shift_right)
@@ -364,24 +375,27 @@ def rank_program(g, core, T, topo):
         tt(v("Q1"), v("QW"), v("Q0"), OP.subtract)
 
     def clear_windows():
-        iota(v("SEL"), [[0, 1024]], 1, 0)
-        asel(v("SEL"), v("SEL"), [[-1, 1024]], OP.is_equal, 0.0, 384, 1)
-        iota(v("GT"), [[0, 4128]], 0, 0)
+        for name in ("GT", "GH"):
+            dma_add(v(name, 0, 4096), xs(0), False)
+            fill(v(name, 4096, 4128), 0.0)
         rows("GT", 7, 16, "V0")
         rows("GT", 8, 16, "V1")
-        iota(v("GH"), [[0, 4128]], 0, 0)
-        iota(v("BIG", 0, 4096), [[0, 4096]], 0, 0)
-        iota(v("QB"), [[1, 4096]], 0, 0)
+        iota(v("SEL"), [[0, 1024]], 1, 0)
+        asel(v("SEL"), v("SEL"), [[-1, 1024]], OP.is_equal, 0.0, 384, 1)
+    iota(v("QB"), [[1, 4096]], 0, 0)
+    for a in range(0, 4096, 512):
+        act(v("QB", a, a + 512), v("QB", a, a + 512), ACT.Copy, None, 0.5)
 
     for name, src, k in (("NIDB", "ID", -1.0), ("ID2B", "ID", 2.0), ("IDBIG", "ID", BIGW), ("IDN64", "ID", -64.0), ("IDA", "ID", float(SL)),
-                         ("NIDA", "ID", -float(SL)), ("IDM", "IDP", 4096.0), ("SHFB", "SHF", 1.0), ("L1", "LB0", 1.0), ("Q0", "QW", 1.0)):
+                         ("NIDA", "ID", -float(SL)), ("IDM", "IDP", 4096.0), ("SHFB", "SHF", 1.0), ("L1", "LB0", 1.0), ("Q0", "QW", 1.0),
+                         ("IDH", "ID", 0.5), ("IDHB", "ID", 0.5), ("NIDH", "ID", -0.5), ("NIDBIG", "ID", -BIGW)):
         act(v(name), v(src), ACT.Copy, None, k)
     weight("LM1", [(0, 288), (1, -255), (2, -544)])
     weight("LM2", [(0, 16)])
-    weight("LE", [(0, 1)])
+    weight("LE", [(0, BIGW)])
     weight("LJ", [(3, 1), (4, 1)])
-    weight("LD", [(1, 1), (2, 1), (5, -1), (6, -1), (7, -1), (8, -1)])
-    weight("LS", [(1, 0.5), (2, 0.5), (3, 0.5), (4, 0.5), (5, -0.5), (6, -0.5), (7, -0.5), (8, -0.5)])
+    weight("LD", [(1, 1), (2, 1), (5, -2), (6, -2), (7, -1), (8, -1)])
+    weight("LS", [(1, 0.5), (2, 0.5), (3, 0.5), (4, 0.5), (5, -1), (6, -1), (7, -0.5), (8, -0.5)])
     weight("LV", [(7, 1), (8, 1)])
     weight("LZ", [(9, 1), (10, 1)])
 
@@ -394,19 +408,17 @@ def rank_program(g, core, T, topo):
         last = t == RO - 1
         for c in range(2):
             iota(xs(LESS[t][c]), [[0, 4096]], -1 - c, 0)
-        for c in range(2):
+            if t == 0 and c == 0:
+                clear_windows()
             dma_add(xs(LESS[t][c]), xs(XSLOT[t]))
-        if t == 0:
-            clear_windows()
-        else:
-            iota(v("BIG", 0, 4096), [[0, 4096]], 0, 0)
+        iota(v("BIG", 0, 4096), [[0, 4096]], 0, 0)
 
         def big(base, h):
             return bg(base[h], base[h] + 1024)
 
         def info(h, s):
             act(big(IG, h), ind(v("INFO", 0, 4112), w64("AL", h)), ACT.Copy)
-            mm(ps(h, 0, 64), v("IDB"), v("KS"), True, False)
+            mm(ps(h, 0, 64), v("NIDB"), v("ONEB", 0, 64), True, False)
             mm(ps(h, 0, 64), v("ID"), w64("Y%d" % s, h), False, False, True)
             bwd(ps(h, 0, 64), "LI", "BIG", BO + IG[h], 64, False, True)
 
@@ -450,8 +462,7 @@ def rank_program(g, core, T, topo):
             first(o, 2)
             if s < 3:
                 first_list(h, s)
-            second(o)
-            if s < 3:
+                second(o)
                 first(h, 0)
             if n == 4:
                 tt(v("MISS"), v("Y2"), v("Y1"), OP.is_lt)
@@ -494,25 +505,28 @@ def rank_program(g, core, T, topo):
             for cc in range(4):
                 a = 384 - 128 * gh + cc
                 mm(ps(7, 64 * cc, 64 * cc + 64), v("SEL", a, a + 512, 4), o, h + gh + cc == 0, h + gh + cc == 7, cc > 0)
+        if not last:
+            ts(v("Y0"), v("STI", 128 * t + 128, 128 * t + 256), 4.0, OP.add)
         digits(0)
+        second(1)
         one_hot_scalar(0)
+        a = NS[0]
+        one_hot(0, a, a + 15)
+        choose(1, 3)
+        one_hot(0, a + 15, a + 18)
+        enter(1, 3)
+        one_hot(0, a + 18, a + 29)
+        digits(1)
+        one_hot_scalar(1)
+        one_hot(0, a + 29, 64)
+        one_hot(1, NS[1], 64)
+        row[0] = None
         mm(ps(0), v("ID"), v("VC"), True, False)
         mm(ps(0), v("ID"), v("SZ"), False, False)
         mm(ps(0, 256, 257), v("SHF"), v("VC", 0, 1), False, False)
         mm(ps(0, 256, 257), v("SHF"), v("SZ", 0, 1), False, True)
-        if not last:
-            ts(v("Y0"), v("STI", 128 * t + 128, 128 * t + 256), 4.0, OP.add)
-        choose(1, 3)
-        one_hot(0, NS[0], NS[0] + 3)
-        enter(1, 3)
-        one_hot(0, NS[0] + 3, NS[0] + 14)
-        digits(1)
-        one_hot_scalar(1)
-        one_hot(0, NS[0] + 14, 64)
-        one_hot(1, NS[1], 64)
-        row[0] = None
         mm(ps(1), v("ID"), v("VC"), True, False)
-        mm(ps(2), v("ID"), v("VC"), True, False)
+        mm(ps(2), v("IDH"), v("VC"), True, False)
         ts(v("EL", 0, 257), ps(0, 0, 257), -1.0, OP.add)
         tt(v("TWE"), ps(0), v("TW"), OP.mult)
         tt(v("KDE"), ps(0), v("KD"), OP.mult)
@@ -532,72 +546,76 @@ def rank_program(g, core, T, topo):
         mm(ps(1), v("IDBIG"), v("HM"), False, True)
         tt(v("HK"), ps(3), v("KDE"), OP.mult)
         ts(ps(4), v("HL", 1, 257), ps(7, 256, 257), OP.add)
-        act(v("H0"), ps(4), ACT.Copy)
+        copy(v("H0"), ps(4))
         tt(v("DO"), v("HL", 16, 257, 16), v("HL", 0, 256, 16), OP.subtract)
         ts(v("DO"), v("DO"), 15.5, OP.is_gt)
         tt(v("DO"), v("DO"), v("DM"), OP.mult)
         tt(v("H1"), ps(4), v("H0"), OP.subtract)
         tt(v("T1"), v("VC"), ps(4), OP.subtract)
-        mm(ps(2), v("NIDB"), v("H0"), False, False)
-        mm(ps(2), v("NIDB"), v("H1"), False, False)
-        mm(ps(2), v("IDB"), v("HM"), False, True)
+        mm(ps(2), v("NIDH"), v("H0"), False, False)
+        mm(ps(2), v("NIDH"), v("H1"), False, False)
+        mm(ps(2), v("IDHB"), v("HM"), False, True)
         GHW, GTW = v("GH", 16, 4112), v("GT", 16, 4112)
-        for onv, a, b in ENDS1:
+        mm(ps(0, 0, 257), v("NIDBIG"), v("ONEB", 0, 257), True, False)
+        mm(ps(0, 1, 257), v("ID"), v("TWE"), False, False)
+        for n, (onv, a, b) in enumerate(ENDS1):
             gather(onv, bg(16 * a, 16 * b), GTW, v("EL", a, b))
-            bwd(ps(5, a, b), "LE", "BIG", BO + 16 * a, b - a)
+            bwd(ps(0, a, b), "LE", "BIG", BO + 16 * a, b - a, False, n == len(ENDS1) - 1)
         rows("GT", 1, 16, "H0")
         rows("GT", 2, 16, "H1")
-
-        def carry(src, k):
-            ts(v("DG"), v("I16"), src, OP.mult)
-            mm(ps(7, 272, 288), v("TRI"), v("DG"), True, True)
-            red(v("RC", k, k + 1), ps(7, 272, 288), OP.max)
-            return v("RC", k, k + 1)
-        tt(v("T4"), ps(5, 1, 257), v("TWE"), OP.mult)
-        scan(v("RL", 1, 257), v("T4"), v("HK"), 0.0, OP.max, OP.max)
-        ts(v("RS", 0, 257), v("RL", 0, 257), carry(v("RL", 256, 257), 0), OP.max)
+        scan(v("RL", 1, 257), ps(0, 1, 257), v("HK"), 0.0, OP.max, OP.max)
+        ts(v("DG", 0, 16), v("I16"), v("RL", 256, 257), OP.mult)
+        mm(ps(7, 272, 288), v("TRI"), v("DG", 0, 16), True, True)
+        red(col(40), ps(7, 272, 288), OP.max)
+        ts(v("RS", 0, 257), v("RL", 0, 257), col(40), OP.max)
         tt(v("KI"), v("RS", 1, 257), ps(1), OP.is_gt)
-        scan(v("JL", 1, 257), v("KI"), v("KI"), 0.0, OP.add, OP.add)
-        mm(ps(7, 257, 258), v("TRI"), v("JL", 256, 257), True, True)
+        tt(v("OX"), v("RS", 0, 256), ps(1, 256, 512), OP.is_gt)
+        scan(v("JL"), v("KI"), v("KI"), 0.0, OP.add, OP.max)
+        scan(v("LQ"), v("OX"), v("KI"), BIGW, OP.mult, OP.add)
         act(v("OUT"), v("KI"), ACT.Identity, 1.0, -1.0)
         act(v("OUT"), v("OUT"), ACT.Identity, THIRD, 1.0 - THIRD)
-        tt(v("OX"), v("RS", 0, 256), ps(1, 256, 512), OP.is_le)
-        ts(ps(4, 0, 257), v("JL", 0, 257), ps(7, 257, 258), OP.add)
-        tt(ps(3), ps(4, 1, 257), v("T1"), OP.add)
+        ts(v("DG", 0, 17), v("U17"), v("JL", 255, 256), OP.mult)
+        ts(v("DG", 24, 40), v("I16"), v("LQ", 255, 256), OP.mult, -1.0, OP.mult)
+        mm(ps(7, 272, 289), v("IDB"), v("NB17"), True, False)
+        mm(ps(7, 272, 289), v("TRI"), v("DG", 0, 17), False, False)
+        mm(ps(7, 272, 288), v("TRI"), v("DG", 24, 40), False, True)
+        base, above = ps(7, 288, 289), col(41)
+        red(above, ps(7, 272, 288), OP.max)
+        tt(v("T5"), v("JL"), v("LQ"), OP.subtract)
+        ts(ps(4), v("JL"), base, OP.add, 2.0, OP.mult)
+        tt(ps(3), ps(4), v("T1"), OP.add)
         act(v("J0"), ps(3), ACT.Copy)
         rows("GH", 3, 16, "J0")
-        tt(v("T5"), ps(4), v("OX"), OP.mult)
         tt(v("J1"), ps(3), v("J0"), OP.subtract)
         rows("GH", 4, 16, "J1")
         rows("GT", 3, 16, "J0")
         rows("GT", 4, 16, "J1")
-        scan(v("LQ"), v("T5"), v("T5"), 0.0, OP.max, OP.max)
-        above = carry(v("LQ", 255, 256), 1)
-        ts(v("T6"), v("LQ"), above, OP.max)
+        ts(v("T6"), v("T5"), base, OP.add, above, OP.max)
         tt(v("P0", 16, 272), ps(2), v("T6"), OP.add)
         act(v("U0"), v("T6"), ACT.Copy)
-        tt(v("O16"), ps(2, 0, 256, 16), v("LQ", 0, 256, 16), OP.add)
-        tt(v("O16"), v("O16"), v("DO"), OP.max)
-        ts(ps(7, 288, 304), ps(2, 0, 256, 16), above, OP.add)
-        tt(v("DO"), ps(7, 288, 304), v("O16"), OP.max)
-        copy(v("OFF"), v("DO"))
-        copy(ind(v("BIG", 0, VLS), v("OFF")), v("CP"))
-        mm(ps(1), v("IDB"), v("ONEB"), True, False)
+        tt(v("O16"), ps(2, 0, 256, 16), v("DO"), OP.max)
+        ts(ps(7, 304, 320), v("T5", 0, 256, 16), base, OP.add, above, OP.max)
+        tt(v("DO"), ps(7, 304, 320), v("O16"), OP.add)
+        ts(v("OFF"), v("DO"), 2.0, OP.mult)
+        copy(ind(v("BIG"), v("OFF")), v("CP"))
+        mm(ps(1), v("IDB"), v("ONEB", 0, 256), True, False)
         mm(ps(1), v("NIDB"), v("J0"), False, False)
         mm(ps(1), v("NIDB"), v("J1"), False, False)
         mm(ps(1), v("NIDB"), v("HM"), False, False)
         mm(ps(1), v("ID2B"), v("KI"), False, False)
+        row[0] = "blocks"
         for k in range(4):
             a = 1024 * k
             scan(v("BIG", VLS + a, VLS + a + 1024), v("BIG", a, a + 1024), v("BIG", a, a + 1024),
                  0.0 if k == 0 else v("BIG", VLS + a - 1, VLS + a), OP.max, OP.max)
-            bwd(ps(5, 64 * k, 64 * k + 64), "LM1", "BIG", VLS + a, 64)
+            bwd(ps(5 + k % 2, 0, 64), "LM1", "BIG", VLS + a, 64)
+            ts(w64("ML", k), ps(5 + k % 2, 0, 64), COFF, OP.add)
         vtr(v("PW", 0, 256), v("P0", 16, 272))
         vtr(v("PW", 256, 544), v("P0", 0, 288))
         for onv, a, b in ENDS2:
             gather(onv, v("G", 16 * a, 16 * b), GHW, v("EL", a, b))
-            bwd(ps(1, a, b), "LJ", "G", 16 * a, b - a, False, b == 256)
-        ts(v("ML"), ps(5), COFF, OP.add)
+            bwd(ps(1, a, b), "LJ", "G", 16 * a, b - a, False, (onv, a, b) == ENDS2[-1])
+        row[0] = None
         tt(v("U1"), v("T6"), v("U0"), OP.subtract)
         rows("GT", 5, 16, "U0")
         rows("GT", 6, 16, "U1")
@@ -612,13 +630,16 @@ def rank_program(g, core, T, topo):
             tt(v("BIG", CMP + a, CMP + a + 1024), ind(v("PW"), w64("ML", k)), v("QB", a, a + 1024), OP.is_le)
             bwd(ps(bank, 0, 64), "L1", "BIG", CMP + a, 64, False, True)
             ts(w64("UL", k), ps(bank, 0, 64), -17.0, OP.add)
+        for n, (onv, k) in enumerate(RUNS):
+            bd = ps((5, 7, 3, 4)[n], 0, 64)
+            mm(bd, v("IDB"), w64("Q0", k), True, False)
+            mm(bd, v("IDB"), w64("Q1", k), False, False, True)
+        row[0] = "end"
         for onv, k in RUNS:
             gather(onv, v("G", 1024 * k, 1024 * k + 1024), GTW, w64("UL", k))
         for n, (onv, k) in enumerate(RUNS):
-            bd, bs, one, cs = ps(4 + n % 2, 0, 64), ps(6 + n % 2, 0, 64), ps(4 + n % 2, 128, 192), ps(4 + n % 2, 256, 320)
-            mm(bd, v("IDB"), w64("Q0", k), True, False)
-            mm(bd, v("IDB"), w64("Q1", k), False, False, True)
-            bwd(bs, "LS", "G", 1024 * k, 64)
+            bd, bs, one, cs = (ps((5, 7, 3, 4)[n], 64 * c, 64 * c + 64) for c in range(4))
+            bwd(bs, "LS", "G", 1024 * k, 64, False, False)
             bwd(bd, "LD", "G", 1024 * k, 64, False, True)
             copy(w64("SF", k), bs)
             ts(one, bd, 1.0, OP.min)
@@ -633,7 +654,7 @@ def rank_program(g, core, T, topo):
         def send(frm, to, rsem, lsem):
             rid, pid, _se = topo.addr(dst)
             add("G", [frm], [], lambda: g.remote_dma(ap(to), ap(frm), T.sem[rsem], T.sem[lsem], pid, rid, topo.mask(core, dst)),
-                0.3, lsem, len(topo.engines(core, dst)), False, 3.0)
+                0.3, lsem, len(topo.engines(core, dst)), False, FAR)
             add("R", [], [to], None, 0.0, rsem, len(topo.engines(src, core)), lat=0.1)
 
         def copy0(onv, a, b):
@@ -657,23 +678,29 @@ def rank_program(g, core, T, topo):
             for i in range(lo, hi):
                 a = 256 * i
                 s = v("GQ", a, a + w) if i < 14 else v("LZ%d" % t, a - 3584, a - 3584 + w)
-                mm(ps(6, 0, w), blk("LZ", i), s, i == 8, i == 15)
+                mm(ps(6, 0, w), blk("LZ", i), s, i == 12, i == 15, i > lo)
         land = v("LX") if last else xs(XN, 3584, 4096)
         copy0(False, 3584, 4096)
         send(v("GQ", 3584, 4096), v("LZ%d" % t, 0, 512), "rz%d" % t, "lz%d" % t)
+        copy0(False, 3072, 3584)
+        copy0(False, 2048, 3072)
+        copy0(False, 1024, 2048)
         xlist(0, 3584, 4096)
         newx(False, 3584, 4096)
         send(v("XS"), land, "rx%d" % t, "lx%d" % t)
-        for onv, a, b in COPY:
-            copy0(onv, a, b)
-        size_sums(8, 14)
-        size_sums(0, 8)
-        size_sums(14, 16)
-        for bank, a, b in ((3, 2048, 3584), (0, 0, 1024), (2, 1024, 2048)):
-            xlist(bank, a, b)
-        tables(last)
+        copy0(False, SPLIT, 1024)
+        copy0(True, 0, SPLIT)
+        for sizes in (not last, last):
+            if sizes:
+                for lo, hi in ((12, 14), (8, 12), (4, 8), (0, 4), (14, 16)):
+                    size_sums(lo, hi)
+            else:
+                for bank, a, b in ((2, 2048, 3584), (0, 1024, 2048), (4, 0, 1024)):
+                    xlist(bank, a, b)
         for onv, a, b in NEWX:
             newx(onv, a, b)
+        row[0] = None
+        tables(last)
         if last:
             tt(v("T1"), ps(1, 256, 512), v("SZ"), OP.add)
             dma(v("ye", 0, 4096, 1, (0, 8, 1)), v("T1"))
@@ -706,7 +733,7 @@ def rank_program(g, core, T, topo):
                     keep.append(h)
                 hist[name] = keep
         key = q if q == "G" else (q, o["row"])
-        if key in lastq and (q == "G" or q == "V" and o["row"]):
+        if key in lastq and (q == "G" or o["row"] and q in KEPT[o["row"]]):
             order[lastq[key]["k"]] = lastq[key]
         if q == "R":
             order[k - 1] = ops[k - 1]

@@ -6,14 +6,24 @@ import comms_topo
 RO = 3
 SL = 4224
 BIGW = 8192.0
+BIGT = 4096
 THIRD = 11184811 / 2 ** 25
 CUTS = (0, 52, 58, 64)
-NS = (12, 12)
+HOT = ((2, 4, 3), (4, 4, 3))
+FILL = (8, 10, 15)
 ENDS1 = ((False, 144, 208), (True, 0, 64), (False, 208, 257), (True, 64, 144))
 ENDS2 = ((False, 0, 64), (False, 64, 128), (True, 208, 256), (False, 128, 208))
-RUNS = ((False, 3), (False, 2), (True, 1), (False, 0))
-SPLIT = 768
-NEWX = ((False, 2048, 3072), (True, 3072, 3584), (False, 1024, 2048), (True, 0, 1024))
+V, S = True, False
+TURN = ((192, 64, 5, 7), (64, 128, 0, 3), (0, 64, 6, 2))
+HEAD = (("run", S, 192, 256), ("run", S, 128, 192), ("run", V, 64, 128), ("sums", 0), ("steps", V, 0), ("run", S, 0, 32), ("run", V, 32, 64),
+        ("sums", 1), ("back", 0), ("sums", 2), ("steps", S, 1), ("copy0", S, 3584, 4096), ("send sizes",), ("steps", V, 2), ("copies", V, 0),
+        ("back", 1), ("back", 2), ("copy0", S, 3072, 3584), ("xlist", 4, 3584, 4096), ("copy0", V, 2048, 3072), ("copy0", S, 1024, 2048),
+        ("newx", S, 3584, 4096), ("send strengths",), ("copy0", V, 0, 1024), ("copies", S, 1), ("copies", S, 2))
+SIZES = (("sizes", 12, 14), ("sizes", 8, 12), ("sizes", 4, 8), ("sizes", 0, 4), ("sizes", 14, 16))
+XL = (("xlist", 7, 2048, 3584), ("xlist", 0, 1024, 2048), ("xlist", 4, 0, 1024))
+NEWX = (("newx", S, 2048, 3072), ("newx", V, 3072, 3584), ("newx", S, 1024, 2048), ("newx", V, 0, 1024))
+END = HEAD + SIZES + XL + (("tables",),) + NEWX
+END_LAST = HEAD + XL + SIZES + NEWX + (("tables",),)
 CYCLE, PE, WAKE, GATHER, SCATTER, SLACK, FAR = 0.00083, 0.00058, 0.18, 1.3, 2.5, 0.2, 4.0
 
 SCRATCH = {
@@ -24,7 +34,8 @@ SCRATCH = {
     "INFO": ("sbuf", [128, 4112], "bfloat16"),
     "GH": ("sbuf", [128, 4128], "bfloat16"),
     "GT": ("sbuf", [128, 4128], "bfloat16"),
-    "DI": ("sbuf", [128, 256], "bfloat16"),
+    "DI0": ("sbuf", [128, HOT[0][0], 128 * HOT[0][1] // HOT[0][0]], "bfloat16"),
+    "DI1": ("sbuf", [128, HOT[1][0], 128 * HOT[1][1] // HOT[1][0]], "bfloat16"),
     "G": ("sbuf", [128, 4096], "bfloat16"),
     "GQ": ("sbuf", [128, 4096], "bfloat16"),
     "XS": ("sbuf", [128, 512], "bfloat16"),
@@ -32,13 +43,17 @@ SCRATCH = {
     "SEL": ("sbuf", [128, 1024], "bfloat16"),
     "STI": ("sbuf", [128, 384], "int32"),
     "EI": ("sbuf", [128, 256], "int32"),
-    "FI": ("sbuf", [128, 256], "int32"),
+    "RR": ("sbuf", [128, 768], "float32"),
+    "AB": ("sbuf", [128, 768], "float32"),
+    "CT": ("sbuf", [128, 768], "bfloat16"),
+    "WT": ("sbuf", [128, 32], "bfloat16"),
+    "CQ": ("sbuf", [128, 768], "bfloat16"),
     "AL": ("sbuf", [128, 128], "uint16"),
     "BL": ("sbuf", [128, 128], "uint16"),
     "EL": ("sbuf", [128, 264], "uint16"),
     "OFF": ("sbuf", [128, 16], "uint16"),
     "PI": ("sbuf", [128, 4], "int32"),
-    "COL": ("sbuf", [128, 48], "float32"),
+    "COL": ("sbuf", [128, 52], "float32"),
     "PW": ("sbuf", [128, 544], "float32"),
     "P0": ("sbuf", [128, 288], "float32"),
     "LB0": ("sbuf", [128, 144], "float32"),
@@ -48,9 +63,9 @@ for _n in ("ML", "UL", "QL", "XL"):
     SCRATCH[_n] = ("sbuf", [128, 256], "uint16")
 for _t in range(RO):
     SCRATCH["LZ%d" % _t] = ("sbuf", [128, 528], "bfloat16")
-for _n in ("LP", "LN", "L1", "LI", "LM1", "LM2", "LE", "LJ", "LD", "LS", "LV", "LZ"):
+for _n in ("LP", "LN", "L1", "LI", "LM1", "LM2", "LE", "LJ", "LV", "LZ"):
     SCRATCH[_n] = ("sbuf", [128, 144], "bfloat16")
-for _n in ("ID", "IDH", "IDP", "TRI", "SHF", "ONE", "TY", "Y0", "Y1", "Y2", "Y3", "Y4"):
+for _n in ("ID", "NID", "IDP", "TRI", "SHF", "ONE", "TY", "Y0", "Y1", "Y2", "Y3", "Y4"):
     SCRATCH[_n] = ("sbuf", [128, 128], "float32")
 for _n in ("IDM", "MISS", "IDB", "NIDB", "ID2B", "IDBIG", "NIDBIG", "IDHB", "NIDH", "IDN64", "IDA", "NIDA", "SHFB"):
     SCRATCH[_n] = ("sbuf", [128, 128], "bfloat16")
@@ -59,12 +74,13 @@ for _n in ("I16", "DM", "DO", "O16"):
 SCRATCH["DG"] = ("sbuf", [128, 40], "float32")
 SCRATCH["U17"] = ("sbuf", [128, 17], "float32")
 SCRATCH["NB17"] = ("sbuf", [128, 17], "bfloat16")
-for _n in ("VC", "REM", "QW", "SZ", "HF", "TWE", "KDE", "HK", "OX", "OUT", "JL", "LQ", "T6", "SF", "T1", "T4", "T5"):
+for _n in ("QW", "HF", "TWE", "KDE", "HK", "OX", "OUT", "JL", "LQ", "T6", "T1", "T5"):
     SCRATCH[_n] = ("sbuf", [128, 256], "float32")
-for _n in ("HL", "RL", "RS"):
+for _n in ("HL", "RL", "RS", "VC", "EE"):
     SCRATCH[_n] = ("sbuf", [128, 264], "float32")
-SCRATCH["ONEB"] = ("sbuf", [128, 264], "bfloat16")
-for _n in ("CP", "KD", "TW", "HM", "KI", "CC", "M0", "M1", "H0", "H1", "J0", "J1", "U0", "U1", "Z0", "Z1", "V0", "V1", "Q0", "Q1"):
+for _n in ("ONEB", "V0", "V1"):
+    SCRATCH[_n] = ("sbuf", [128, 264], "bfloat16")
+for _n in ("CP", "KD", "TW", "HM", "KI", "IT", "M0", "M1", "H0", "H1", "J0", "J1", "U0", "U1", "Z0", "Z1"):
     SCRATCH[_n] = ("sbuf", [128, 256], "bfloat16")
 for _n in range(8):
     SCRATCH["b%d" % _n] = ("psum", [128, 512], "float32")
@@ -81,6 +97,10 @@ def v(name, c0=0, c1=None, cs=1, p=ALL):
     if c1 is None:
         c1 = 4096 if name in ("y", "ye", "x", "ends") else SCRATCH[name][1][1]
     return (name, p, c0, c1, cs)
+
+
+def v3(name, c0, c1, p=None):
+    return (name, ALL, c0, c1, 1, p)
 
 
 BO = 4096
@@ -122,14 +142,14 @@ def rank_program(g, core, T, topo):
             if x[0] == "@":
                 out.append(x[1])
                 out.append(x[2])
-            elif len(x) == 5:
+            else:
                 out.append(x)
         return out
 
     def width(x):
         if x[0] == "@":
             return 16 * width(x[2])
-        return len(range(x[2], x[3], x[4]))
+        return len(range(x[2], x[3], x[4])) * (SCRATCH[x[0]][1][1] if len(x) == 6 and x[5] is None else 1)
 
     def two(x):
         return SCRATCH.get(x[0], (0, 0, "x"))[2] in ("bfloat16", "uint16")
@@ -171,6 +191,8 @@ def rank_program(g, core, T, topo):
             return x
         if x[0] == "@":
             return ap(x[1]).indirect(ap(x[2]))
+        if len(x) == 6:
+            return T[x[0]][:, :, x[2]:x[3]] if x[5] is None else T[x[0]][:, x[5], x[2]:x[3]]
         name, p, c0, c1, cs = x
         return T[name][p[0]:p[1]:p[2], c0:c1:cs] if (p[2] != 1 or cs != 1) else T[name][p[0]:p[1], c0:c1]
 
@@ -240,7 +262,7 @@ def rank_program(g, core, T, topo):
 
     def rows(name, r, c0, src):
         was, row[0] = row[0], "rows"
-        dma(v(name, c0, c0 + 4096, 1, (r, 128, 16)), v(src))
+        dma(v(name, c0, c0 + 4096, 1, (r, 128, 16)), v(src, 0, 256))
         row[0] = was
 
     def blk(lname, i):
@@ -276,45 +298,48 @@ def rank_program(g, core, T, topo):
     dma(v("WP", 0, 1024), v("w", 0, 1024))
     PIc = v("PI", 0, 1)
     iota(PIc, [[0, 1]], 0, 1, False)
-    iota(v("VC"), [[1, 256]], 0, 256)
+    VC, VN, NEXT = v("VC", 0, 256), v("VC", 1, 257), ps(1, 256, 512)
+    iota(v("VC", 0, 257), [[1, 257]], 0, 256)
     fill(v("ONE"), 1.0)
-    asel(v("ID"), v("ONE"), [[-1, 128]], OP.is_equal, 0.0, 0, 1)
     asel(v("SHF"), v("ONE"), [[-1, 128]], OP.is_equal, 0.0, -1, 1)
+    asel(v("ID"), v("ONE"), [[-1, 128]], OP.is_equal, 0.0, 0, 1)
     iota(v("LB0"), [[1, 144]], -15, 0)
     iota(v("I16"), [[1, 16]], 0, 0)
-    fill(v("ONEB"), 1.0)
     ts(v("PI", 1, 2), PIc, 4, OP.arith_shift_right)
     ts(v("PI", 2, 3), PIc, 15, OP.bitwise_and)
     ts(v("PI", 3, 4), v("PI", 1, 2), 1, OP.bitwise_and)
-    G16, GB, II, AA, COFF = col(0), col(1), col(2), col(3), col(5)
-    ts(GB, v("PI", 1, 2), 4096.0, OP.mult)
-    ts(v("VC"), v("VC"), GB, OP.subtract)
-    fill(v("INFO"), 0.0)
-    ts(G16, v("PI", 1, 2), 16.0, OP.mult)
+    G16, GB, II, AA, LIM, COFF = col(0), col(1), col(2), col(3), col(4), col(5)
+    ts(GB, v("PI", 1, 2), -4096.0, OP.mult)
     copy(II, v("PI", 2, 3))
+    ts(col(42), v("PI", 2, 3), 15.0, OP.is_ge, 4096.0, OP.mult)
+    fill(v("INFO"), 0.0)
+    act(v("VC", 0, 257), v("VC", 0, 257), ACT.Identity, GB)
+    act(NEXT, VN, ACT.Copy)
+    fill(v("ONEB"), 1.0)
+    ts(G16, v("PI", 1, 2), 16.0, OP.mult)
     copy(AA, v("PI", 3, 4))
     act(v("IDB"), v("ID"), ACT.Copy)
 
     def tables(last, cut=True):
-        if cut:
-            tt(v("SZ"), ps(6), v("REM"), OP.min)
-        else:
-            tt(v("SZ"), v("EI"), v("VC"), OP.subtract)
+        if not cut:
+            copy(col(7), v("EI", 0, 1))
+            copy(ps(6), v("EI"))
+            mm(ps(6, 256, 257), v("SHF"), col(7), True, False)
+            mm(ps(6, 256, 257), v("ID"), col(42), False, True)
+        w = 256 if last else 257
+        ts(v("EE", 0, w), ps(6, 0, w), LIM if cut else 4096.0, OP.min)
         if last:
             return
-        if not cut:
-            mm(ps(6, 256, 257), v("SHF"), v("SZ", 0, 1), True, False)
-            mm(ps(6, 1, 256), v("ID"), v("SZ", 1, 256), False, True)
-        ts(v("KD"), v("SZ"), 1.0, OP.is_gt)
-        tt(ps(5), v("SZ"), ps(6, 1, 257), OP.subtract)
-        ts(v("TW"), ps(5), 1.0, OP.is_gt)
-        tt(ps(5), ps(6, 1, 257), v("TW"), OP.mult)
+        tt(ps(5, 256, 512), ps(6, 1, 257), VN, OP.subtract)
+        tt(v("TW"), ps(6, 1, 257), v("EE", 0, 256), OP.is_lt)
+        tt(v("KD"), NEXT, v("EE", 0, 256), OP.is_lt)
+        rows("INFO", 2, 1, "KD")
+        tt(ps(5), ps(5, 256, 512), v("TW"), OP.mult)
         copy(v("M0"), ps(5))
         rows("INFO", 0, 1, "M0")
-        tt(ps(5, 256, 512), ps(5), v("KD"), OP.add)
-        tt(v("M1"), ps(5, 256, 512), v("M0"), OP.subtract)
+        tt(v("M1"), ps(5), v("M0"), OP.subtract)
         rows("INFO", 1, 1, "M1")
-        act(v("HF"), v("SZ"), ACT.Relu, 2.0, -1.0)
+        act(v("HF"), v("KD"), ACT.Identity, 1.0, -1.0)
     tables(False, False)
     dma(v("WP", 1024, 2048), v("w", 1024, 2048))
     dma(v("STI", 128, 384), v("start", 128, 384))
@@ -324,22 +349,25 @@ def rank_program(g, core, T, topo):
     ts(v("LN"), v("LB0"), -BIGW, OP.mult)
     nw = [8]
 
-    def weight(name, terms):
+    def weights(terms):
         c = None
         for r, wgt in terms:
             n = col(nw[0])
             nw[0] += 1
             act(n, v("I16", r, r + 1), ACT.Identity, c, float(wgt))
             c = n
-        act(v(name), v("LB0"), ACT.Copy, None, c)
-    weight("LI", [(0, 1), (1, 1)])
+        return c
+
+    def weight(name, terms):
+        act(v(name), v("LB0"), ACT.Copy, None, weights(terms))
+    weight("LI", [(0, 1), (1, 1), (2, 1)])
     for k in range(5):
         fill(xs(k, 4096, SL), 255.0)
     ts(v("AL"), v("STI", 0, 128), 1.0, OP.add)
     ts(v("Y0"), v("STI", 0, 128), 4.0, OP.add)
-    act(v("V0"), v("VC"), ACT.Copy)
-    tt(v("V1"), v("VC"), v("V0"), OP.subtract)
-    copy(ps(1, 256, 512), v("VC"))
+    act(col(43), II, ACT.Copy, None, 256.0)
+    act(v("V0", 0, 257), v("ONEB", 0, 257), ACT.Copy, None, col(43))
+    iota(v("V1", 0, 257), [[1, 257]], 0, 0)
     for name in ("HL", "RL"):
         fill(v(name, 0, 1), 0.0)
     fill(v("P0"), 0.0)
@@ -349,30 +377,29 @@ def rank_program(g, core, T, topo):
     asel(v("TRI"), v("TRI"), [[-16, 8], [0, 16]], OP.is_ge, 0.0, 0, 1)
     asel(v("IDP"), v("ONE"), [[-8, 2], [-16, 8], [-1, 8]], OP.is_equal, 0.0, 0, 1)
     iota(v("QW"), [[16, 256]], 0, 1)
-    iota(v("OX"), [[1, 16], [16, 16]], 0, 0)
-    iota(v("T5"), [[0, 16], [1, 16]], 0, 0)
+    iota(v("CP"), [[1, 16], [16, 16]], 1, 0)
+    iota(v("CQ", 0, 256), [[0, 16], [1, 16]], 0, 0)
+    dma(v("CP", 0, 256, 1, (1, 128, 16)), v("CQ", 0, 256, 1, (1, 128, 16)))
+    for a in range(2):
+        iota(v("CQ", 256 * a + 256, 256 * a + 512), [[1, 8], [a, 2], [8, 16]], 0, 0)
+        dma(v("CP", 0, 256, 1, (16 * a + 2, 128, 32)), v("CQ", 256 * a + 256, 256 * a + 512, 1, (16 * a + 2, 128, 32)))
+    iota(v("IT"), [[0, 16], [BIGT, 16]], 0, 0)
+    for k, piece in enumerate(TURN):
+        iota(col(48 + k), [[0, 1]], 16 * piece[0] * BIGT, 16 * BIGT)
     iota(v("DM"), [[1, 16]], 12288, 16)
     iota(v("U17"), [[1, 17]], 0, 0)
-    ts(v("QW"), v("QW"), G16, OP.subtract)
+    act(col(46), G16, ACT.Copy, None, -1.0)
+    act(v("QW"), v("QW"), ACT.Identity, col(46))
 
     def growth_constants():
-        ts(col(4), II, 14.0, OP.is_ge, 512.0, OP.mult)
-        ts(v("REM"), v("VC"), col(4), OP.subtract, -1.0, OP.mult)
-        ts(v("REM"), v("REM"), 3584.0, OP.add)
+        ts(LIM, II, 14.0, OP.is_ge, 512.0, OP.mult)
+        act(LIM, LIM, ACT.Identity, 3584.0)
         ts(col(6), G16, 16.0, OP.mult)
         ts(v("DM"), v("DM"), col(6), OP.subtract, 0.5, OP.mult)
         ts(v("U17"), v("U17"), II, OP.is_ge)
         ts(v("NB17", 0, 16), v("U17", 0, 16), -BIGW, OP.mult)
         fill(v("NB17", 16, 17), 0.0)
         ts(COFF, AA, 272.0, OP.mult, -288.0, OP.add)
-        ts(v("FI"), v("OX"), AA, OP.add)
-        ts(v("FI"), v("FI"), 1, OP.arith_shift_right)
-        ts(v("OX"), v("OX"), 1.0, OP.add, v("I16", 0, 1), OP.mult)
-        ts(v("T5"), v("T5"), v("I16", 1, 2), OP.mult)
-        tt(v("OX"), v("OX"), v("T5"), OP.add)
-        ts(v("T5"), v("FI"), v("I16", 2, 3), OP.mult)
-        tt(v("CP"), v("OX"), v("T5"), OP.add)
-        tt(v("Q1"), v("QW"), v("Q0"), OP.subtract)
 
     def clear_windows():
         for name in ("GT", "GH"):
@@ -387,15 +414,18 @@ def rank_program(g, core, T, topo):
         act(v("QB", a, a + 512), v("QB", a, a + 512), ACT.Copy, None, 0.5)
 
     for name, src, k in (("NIDB", "ID", -1.0), ("ID2B", "ID", 2.0), ("IDBIG", "ID", BIGW), ("IDN64", "ID", -64.0), ("IDA", "ID", float(SL)),
-                         ("NIDA", "ID", -float(SL)), ("IDM", "IDP", 4096.0), ("SHFB", "SHF", 1.0), ("L1", "LB0", 1.0), ("Q0", "QW", 1.0),
-                         ("IDH", "ID", 0.5), ("IDHB", "ID", 0.5), ("NIDH", "ID", -0.5), ("NIDBIG", "ID", -BIGW)):
+                         ("NIDA", "ID", -float(SL)), ("IDM", "IDP", 4096.0), ("SHFB", "SHF", 1.0), ("L1", "LB0", 1.0), ("NID", "ID", -1.0),
+                         ("IDHB", "ID", 0.5), ("NIDH", "ID", -0.5), ("NIDBIG", "ID", -BIGW)):
         act(v(name), v(src), ACT.Copy, None, k)
     weight("LM1", [(0, 288), (1, -255), (2, -544)])
     weight("LM2", [(0, 16)])
     weight("LE", [(0, BIGW)])
     weight("LJ", [(3, 1), (4, 1)])
-    weight("LD", [(1, 1), (2, 1), (5, -2), (6, -2), (7, -1), (8, -1)])
-    weight("LS", [(1, 0.5), (2, 0.5), (3, 0.5), (4, 0.5), (5, -1), (6, -1), (7, -0.5), (8, -0.5)])
+    behind = weights([(1, BIGT), (2, BIGT), (5, -2 * BIGT), (6, -2 * BIGT), (7, -BIGT), (8, -BIGT)])
+    size = weights([(1, 0.5), (2, 0.5), (3, 0.5), (4, 0.5), (5, -1), (6, -1), (7, -0.5), (8, -0.5)])
+    act(col(47), size, ACT.Identity, behind, -float(BIGT))
+    for k, c in enumerate((behind, col(47), size, size)):
+        act(v("WT", 8 * k, 8 * k + 8), v("LB0", 15, 143, 16), ACT.Copy, None, c)
     weight("LV", [(7, 1), (8, 1)])
     weight("LZ", [(9, 1), (10, 1)])
 
@@ -468,66 +498,86 @@ def rank_program(g, core, T, topo):
                 tt(v("MISS"), v("Y2"), v("Y1"), OP.is_lt)
 
         def digits(h):
-            HI, LO = v("DI", 128 * h, 128 * h + 64), v("DI", 128 * h + 64, 128 * h + 128)
+            pieces, reps, _ = HOT[h]
+            n = 64 // pieces
+
+            def digit(r, low):
+                return v3("DI%d" % h, n * (2 * r + low), n * (2 * r + low + 1))
             for a in (0, 64):
                 o = v("b%d" % (4 + h), 0, 64, 1, (a, a + 64, 1))
                 mm(o, w64("MISS", h), v("IDM", a, a + 64), True, False)
                 mm(o, w64("Y4", h), v("IDP", a, a + 64), False, True, True)
-            ts(HI, ps(4 + h, 0, 64), 1.0 / 64, OP.mult, 129 - 31.5 / 64, OP.add)
+            for r in range(reps):
+                ts(digit(r, 0), ps(4 + h, 0, 64), 1.0 / 64, OP.mult, 129 + reps - r - 31.5 / 64, OP.add)
             for a in (0, 64):
-                o = v("b%d" % (4 + h), 64, 128, 1, (a, a + 64, 1))
+                o = v("b%d" % (6 + h), 0, 64, 1, (a, a + 64, 1))
                 mm(o, w64("Y4", h), v("IDP", a, a + 64), True, False)
-                mm(o, v("IDN64", a, a + 64), HI, False, True, True)
-            act(LO, ps(4 + h, 64, 128), ACT.Identity, 65.0 * 129)
+                mm(o, v("IDN64", a, a + 64), digit(0, 0), False, True, True)
+            for r in range(reps):
+                act(digit(r, 1), ps(6 + h, 0, 64), ACT.Identity, 65.0 * (129 + reps) - r)
+
+        def hot(h, j):
+            pieces, reps, _ = HOT[h]
+            p, k = divmod(j, 64 // reps)
+            w = 128 * reps // pieces
+            return v3("DI%d" % h, 0, w, p), bg(OH[h] + w * j, OH[h] + w * j + w), 129.0 + reps + reps * k
+
+        def mine(h, onv):
+            pieces, reps, ns = HOT[h]
+            return [j for j in range(64 * pieces // reps) if (j % (64 // reps) >= ns) == onv]
 
         def one_hot(h, a, b):
-            for k in range(a, b):
-                ts(bg(OH[h] + 128 * k, OH[h] + 128 * k + 128), v("DI", 128 * h, 128 * h + 128), 129.0 + k, OP.is_equal)
+            for j in mine(h, V)[a:b]:
+                d, o, c = hot(h, j)
+                ts(o, d, c, OP.is_equal)
 
         def one_hot_scalar(h):
-            for k in range(NS[h]):
-                o = bg(OH[h] + 128 * k, OH[h] + 128 * k + 128)
-                act(o, v("DI", 128 * h, 128 * h + 128), ACT.Abs, -129.0 - k)
+            for j in mine(h, S):
+                d, o, c = hot(h, j)
+                act(o, d, ACT.Abs, -c)
                 act(o, o, ACT.Relu, 1.0, -1.0)
 
         def counts(h, gh):
-            bank = (3, 4, 5, 6)[gh] if h else (6, 3)[gh % 2]
-            for gg in (2 * gh, 2 * gh + 1):
-                for i in range(8):
-                    c = OH[h] + 8 * gg + i
-                    mm(v("b%d" % bank, 0, 64, 1, (64 * (gg % 2), 64 * (gg % 2) + 64, 1)), bg(c, OH[h] + 8192, 128), bg(c + 64, OH[h] + 8192, 128),
-                       i == 0, i == 7, i > 0)
-            o = v("HB", 256 * h + 64 * gh, 256 * h + 64 * gh + 64)
-            if h == 1 and gh >= 2:
+            bank = (4, 6, 3, 2)[gh]
+            n = 64 // HOT[h][0]
+            if h == 0:
+                mm(ps(bank, 0, 64), v("SEL", 0, 128), v("ONEB", 0, 64), True, False)
+            for x0 in range(16):
+                gg = x0 // 8
+                p, x = divmod(16 * gh + x0, n)
+                c, end = OH[h] + 128 * n * p + x, OH[h] + 128 * n * (p + 1)
+                mm(v("b%d" % bank, 0, 64, 1, (64 * gg, 64 * gg + 64, 1)), bg(c, end, 2 * n), bg(c + n, end, 2 * n),
+                   False, False, x0 > 0)
+            if h == 0:
+                return
+            mm(ps(bank, 0, 64), v("SEL", 0, 128), v("ONEB", 0, 64), False, True, True)
+            o = v("HB", 64 * gh, 64 * gh + 64)
+            if gh >= 3:
                 copy(o, ps(bank, 0, 64))
             else:
                 act(o, ps(bank, 0, 64), ACT.Copy)
             for cc in range(4):
                 a = 384 - 128 * gh + cc
-                mm(ps(7, 64 * cc, 64 * cc + 64), v("SEL", a, a + 512, 4), o, h + gh + cc == 0, h + gh + cc == 7, cc > 0)
+                mm(ps(7, 64 * cc, 64 * cc + 64), v("SEL", a, a + 512, 4), o, gh + cc == 0, gh + cc == 6, cc > 0)
         if not last:
             ts(v("Y0"), v("STI", 128 * t + 128, 128 * t + 256), 4.0, OP.add)
         digits(0)
         second(1)
         one_hot_scalar(0)
-        a = NS[0]
-        one_hot(0, a, a + 15)
+        one_hot(0, 0, FILL[0])
         choose(1, 3)
-        one_hot(0, a + 15, a + 18)
+        one_hot(0, FILL[0], FILL[1])
         enter(1, 3)
-        one_hot(0, a + 18, a + 29)
+        one_hot(0, FILL[1], FILL[2])
         digits(1)
         one_hot_scalar(1)
-        one_hot(0, a + 29, 64)
-        one_hot(1, NS[1], 64)
+        one_hot(0, FILL[2], 64)
+        one_hot(1, 0, 64)
         row[0] = None
-        mm(ps(0), v("ID"), v("VC"), True, False)
-        mm(ps(0), v("ID"), v("SZ"), False, False)
-        mm(ps(0, 256, 257), v("SHF"), v("VC", 0, 1), False, False)
-        mm(ps(0, 256, 257), v("SHF"), v("SZ", 0, 1), False, True)
-        mm(ps(1), v("ID"), v("VC"), True, False)
-        mm(ps(2), v("IDH"), v("VC"), True, False)
-        ts(v("EL", 0, 257), ps(0, 0, 257), -1.0, OP.add)
+        mm(ps(0), v("ID"), v("EE", 0, 256), True, True)
+        mm(ps(1), v("IDB"), v("V0", 0, 256), True, False)
+        mm(ps(1), v("IDB"), v("V1", 0, 256), False, False)
+        ts(v("EL", 0, 257), v("EE", 0, 257), -1.0, OP.add)
         tt(v("TWE"), ps(0), v("TW"), OP.mult)
         tt(v("KDE"), ps(0), v("KD"), OP.mult)
         if not last:
@@ -551,10 +601,12 @@ def rank_program(g, core, T, topo):
         ts(v("DO"), v("DO"), 15.5, OP.is_gt)
         tt(v("DO"), v("DO"), v("DM"), OP.mult)
         tt(v("H1"), ps(4), v("H0"), OP.subtract)
-        tt(v("T1"), v("VC"), ps(4), OP.subtract)
+        tt(v("T1"), VC, ps(4), OP.subtract)
+        mm(ps(2), v("IDHB"), v("V0", 0, 256), True, False)
+        mm(ps(2), v("IDHB"), v("V1", 0, 256), False, False)
+        mm(ps(2), v("IDHB"), v("HM"), False, False)
         mm(ps(2), v("NIDH"), v("H0"), False, False)
-        mm(ps(2), v("NIDH"), v("H1"), False, False)
-        mm(ps(2), v("IDHB"), v("HM"), False, True)
+        mm(ps(2), v("NIDH"), v("H1"), False, True)
         GHW, GTW = v("GH", 16, 4112), v("GT", 16, 4112)
         mm(ps(0, 0, 257), v("NIDBIG"), v("ONEB", 0, 257), True, False)
         mm(ps(0, 1, 257), v("ID"), v("TWE"), False, False)
@@ -569,7 +621,7 @@ def rank_program(g, core, T, topo):
         red(col(40), ps(7, 272, 288), OP.max)
         ts(v("RS", 0, 257), v("RL", 0, 257), col(40), OP.max)
         tt(v("KI"), v("RS", 1, 257), ps(1), OP.is_gt)
-        tt(v("OX"), v("RS", 0, 256), ps(1, 256, 512), OP.is_gt)
+        tt(v("OX"), v("RS", 0, 256), NEXT, OP.is_ge)
         scan(v("JL"), v("KI"), v("KI"), 0.0, OP.add, OP.max)
         scan(v("LQ"), v("OX"), v("KI"), BIGW, OP.mult, OP.add)
         act(v("OUT"), v("KI"), ACT.Identity, 1.0, -1.0)
@@ -630,24 +682,43 @@ def rank_program(g, core, T, topo):
             tt(v("BIG", CMP + a, CMP + a + 1024), ind(v("PW"), w64("ML", k)), v("QB", a, a + 1024), OP.is_le)
             bwd(ps(bank, 0, 64), "L1", "BIG", CMP + a, 64, False, True)
             ts(w64("UL", k), ps(bank, 0, 64), -17.0, OP.add)
-        for n, (onv, k) in enumerate(RUNS):
-            bd = ps((5, 7, 3, 4)[n], 0, 64)
-            mm(bd, v("IDB"), w64("Q0", k), True, False)
-            mm(bd, v("IDB"), w64("Q1", k), False, False, True)
+        for a, n, tb, wb in TURN:
+            mm(v("b%d" % tb, 0, 256, 1, (0, n, 1)), v("IDB", 0, n), v("IT"), True, False)
+            mm(v("b%d" % tb, 256, 512, 1, (0, n, 1)), v("SEL", 0, n), v("IT"), False, False, True)
+            mm(ps(wb, 0, n), v("ID"), v("QW", a, a + n), True, False)
         row[0] = "end"
-        for onv, k in RUNS:
-            gather(onv, v("G", 1024 * k, 1024 * k + 1024), GTW, w64("UL", k))
-        for n, (onv, k) in enumerate(RUNS):
-            bd, bs, one, cs = (ps((5, 7, 3, 4)[n], 64 * c, 64 * c + 64) for c in range(4))
-            bwd(bs, "LS", "G", 1024 * k, 64, False, False)
-            bwd(bd, "LD", "G", 1024 * k, 64, False, True)
-            copy(w64("SF", k), bs)
-            ts(one, bd, 1.0, OP.min)
-            tt(w64("T4", k), bd, w64("SF", k), OP.is_gt)
-            tt(w64("CC", k), one, w64("T4", k), OP.add)
-            tt(cs, bs, w64("CC", k), OP.mult)
-            tt(w64("T5", k), w64("QW", k), cs, OP.subtract)
-            copy(w64("QL", k), w64("T5", k))
+
+        def part(name, k, a=0, b=256):
+            return v(name, 256 * k + a, 256 * k + b, 1, (0, TURN[k][1], 1))
+
+        def run(onv, a, b):
+            gather(onv, v("G", 16 * a, 16 * b), GTW, v("UL", a, b))
+
+        def sums(k):
+            a, n, tb, wb = TURN[k]
+            for i in range(16):
+                mm(v("b%d" % tb, i, 512, 16, (0, n, 1)), v("G", 16 * a + i, 16 * (a + n), 16), v("WT"), False, i == 15, i > 0)
+
+        def steps(onv, k):
+            a, n, tb, wb = TURN[k]
+            p = (0, n, 1)
+            if onv:
+                ts(part("RR", k), v("b%d" % tb, 0, 256, 1, p), v("COL", 48 + k, 49 + k, 1, p), OP.add, 0.0, OP.max)
+            else:
+                act(part("RR", k), v("b%d" % tb, 0, 256, 1, p), ACT.Relu, v("COL", 48 + k, 49 + k, 1, p))
+            tt(part("AB", k), v("b%d" % tb, 256, 512, 1, p), part("RR", k), OP.min)
+
+        def back(k):
+            a, n, tb, wb = TURN[k]
+            for c in range(2):
+                mm(ps(wb, 0, n), part("AB", k, 128 * c, 128 * c + 128), v("NID", 0, n, 1, (0, n, 1)), False, c == 1, c > 0)
+            copy(v("QL", a, a + n), ps(wb, 0, n))
+
+        def copies(onv, k):
+            if onv:
+                ts(part("CT", k), part("RR", k), 1.0, OP.min)
+            else:
+                act(part("CT", k), part("RR", k), ACT.Sign)
         dst = T.cores[(rank + 1) % len(T.cores)]
         src = T.cores[(rank - 1) % len(T.cores)]
 
@@ -662,7 +733,13 @@ def rank_program(g, core, T, topo):
 
         def xlist(bank, a, b):
             o = ps(bank, 0, (b - a) // 16)
-            mm(o, v("IDA" if t == 0 else "NIDA"), v("CC", a // 16, b // 16), True, False)
+            lo, hi, start = a // 16, b // 16, True
+            for k, (a0, n, tb, wb) in enumerate(TURN):
+                c0, c1 = max(a0, lo), min(a0 + n, hi)
+                for c in range(2 if c0 < c1 else 0):
+                    mm(ps(bank, c0 - lo, c1 - lo), part("CT", k, 128 * c, 128 * c + 128),
+                       v("IDA" if t == 0 else "NIDA", c0 - a0, c1 - a0, 1, (0, n, 1)), start, False, not start)
+                    start = False
             bwd(o, "LV", "GQ", a, (b - a) // 16, False, True)
             ts(v("XL", a // 16, b // 16), o, 0.0 if t == 0 else 2.0 * SL, OP.add)
         XW = v("XX", SL * min(LESS[t] + (XSLOT[t],)), SL * (min(LESS[t] + (XSLOT[t],)) + 3))
@@ -675,35 +752,23 @@ def rank_program(g, core, T, topo):
 
         def size_sums(lo, hi):
             w = 256 if last else 257
+            if lo == 12:
+                mm(ps(6, 0, w), v("IDB"), v("V0", 0, w), True, False)
+                mm(ps(6, 0, w), v("IDB"), v("V1", 0, w), False, False, True)
             for i in range(lo, hi):
                 a = 256 * i
                 s = v("GQ", a, a + w) if i < 14 else v("LZ%d" % t, a - 3584, a - 3584 + w)
-                mm(ps(6, 0, w), blk("LZ", i), s, i == 12, i == 15, i > lo)
+                mm(ps(6, 0, w), blk("LZ", i), s, False, i == 15, i > lo)
         land = v("LX") if last else xs(XN, 3584, 4096)
-        copy0(False, 3584, 4096)
-        send(v("GQ", 3584, 4096), v("LZ%d" % t, 0, 512), "rz%d" % t, "lz%d" % t)
-        copy0(False, 3072, 3584)
-        copy0(False, 2048, 3072)
-        copy0(False, 1024, 2048)
-        xlist(0, 3584, 4096)
-        newx(False, 3584, 4096)
-        send(v("XS"), land, "rx%d" % t, "lx%d" % t)
-        copy0(False, SPLIT, 1024)
-        copy0(True, 0, SPLIT)
-        for sizes in (not last, last):
-            if sizes:
-                for lo, hi in ((12, 14), (8, 12), (4, 8), (0, 4), (14, 16)):
-                    size_sums(lo, hi)
-            else:
-                for bank, a, b in ((2, 2048, 3584), (0, 1024, 2048), (4, 0, 1024)):
-                    xlist(bank, a, b)
-        for onv, a, b in NEWX:
-            newx(onv, a, b)
+        calls = {"run": run, "sums": sums, "steps": steps, "back": back, "copies": copies, "copy0": copy0, "xlist": xlist, "newx": newx,
+                 "sizes": size_sums, "tables": lambda: tables(last),
+                 "send sizes": lambda: send(v("GQ", 3584, 4096), v("LZ%d" % t, 0, 512), "rz%d" % t, "lz%d" % t),
+                 "send strengths": lambda: send(v("XS"), land, "rx%d" % t, "lx%d" % t)}
+        for c in (END_LAST if last else END):
+            calls[c[0]](*c[1:])
         row[0] = None
-        tables(last)
         if last:
-            tt(v("T1"), ps(1, 256, 512), v("SZ"), OP.add)
-            dma(v("ye", 0, 4096, 1, (0, 8, 1)), v("T1"))
+            dma(v("ye", 0, 4096, 1, (0, 8, 1)), v("EE", 0, 256))
             dma(v("y", 3584, 4096), land)
 
     hist = {}
@@ -728,7 +793,7 @@ def rank_program(g, core, T, topo):
                         continue
                     elif over and (wr or hw):
                         deps[ho["k"]] = ho
-                    if wr and not psum and hx[2] >= x[2] and hx[3] <= x[3] and (pm(hx[1]) & ~m) == 0 and x[4] == 1:
+                    if wr and not psum and hx[2] >= x[2] and hx[3] <= x[3] and (pm(hx[1]) & ~m) == 0 and x[4] == 1 and x[5:] in ((), (None,)):
                         continue
                     keep.append(h)
                 hist[name] = keep

@@ -8,23 +8,32 @@ SL = 4224
 BIGW = 8192.0
 BIGT = 4096
 THIRD = 11184811 / 2 ** 25
-CUTS = (0, 52, 58, 64)
+CUTS = (0, 48, 56, 64)
 HOT = ((2, 4, 3), (4, 4, 3))
-FILL = (8, 10, 15)
-ENDS1 = ((False, 144, 208), (True, 0, 64), (False, 208, 257), (True, 64, 144))
-ENDS2 = ((False, 0, 64), (False, 64, 128), (True, 208, 256), (False, 128, 208))
+FILL = (7, 13)
+ENDS1 = ((False, 134, 198), (True, 0, 64), (False, 198, 257), (True, 64, 134))
+ENDS2 = ((False, 0, 64), (False, 64, 128), (False, 128, 192), (False, 192, 256))
+SEARCH = (("compare", 64, 128), ("compare", 192, 256), ("compare", 128, 152), ("sizes", 0), ("compare", 152, 164), ("sizes", 1), ("count", 3),
+          ("count", 1), ("compare", 164, 192), ("count", 2), ("found", 3), ("compare", 0, 64), ("count", 0), ("found", 1), ("found", 2))
 V, S = True, False
-TURN = ((192, 64, 5, 7), (64, 128, 0, 3), (0, 64, 6, 2))
-HEAD = (("run", S, 192, 256), ("run", S, 128, 192), ("run", V, 64, 128), ("sums", 0), ("steps", V, 0), ("run", S, 0, 32), ("run", V, 32, 64),
-        ("sums", 1), ("back", 0), ("sums", 2), ("steps", S, 1), ("copy0", S, 3584, 4096), ("send sizes",), ("steps", V, 2), ("copies", V, 0),
-        ("back", 1), ("back", 2), ("copy0", S, 3072, 3584), ("xlist", 4, 3584, 4096), ("copy0", V, 2048, 3072), ("copy0", S, 1024, 2048),
-        ("newx", S, 3584, 4096), ("send strengths",), ("copy0", V, 0, 1024), ("copies", S, 1), ("copies", S, 2))
-SIZES = (("sizes", 12, 14), ("sizes", 8, 12), ("sizes", 4, 8), ("sizes", 0, 4), ("sizes", 14, 16))
-XL = (("xlist", 7, 2048, 3584), ("xlist", 0, 1024, 2048), ("xlist", 4, 0, 1024))
-NEWX = (("newx", S, 2048, 3072), ("newx", V, 3072, 3584), ("newx", S, 1024, 2048), ("newx", V, 0, 1024))
-END = HEAD + SIZES + XL + (("tables",),) + NEWX
-END_LAST = HEAD + XL + SIZES + NEWX + (("tables",),)
-CYCLE, PE, WAKE, GATHER, SCATTER, SLACK, FAR = 0.00083, 0.00058, 0.18, 1.3, 2.5, 0.2, 4.0
+TURN = ((192, 64, 4, 7), (64, 128, 6, 3), (0, 64, 0, 5))
+XA, XB, XC, XD = (4, 3072, 4096), (7, 2048, 3072), (0, 1024, 2048), (4, 0, 1024)
+XE, XF = (4, 3584, 4096), (7, 2048, 3584)
+HEAD = (("run", S, 224, 256), ("run", V, 192, 224), ("sums", 0), ("run", S, 128, 192), ("run", V, 64, 96), ("found", 0), ("run", V, 96, 128),
+        ("sums", 1), ("steps", V, 0), ("run", S, 0, 44), ("run", V, 44, 54), ("back", 0), ("run", V, 54, 64), ("sums", 2), ("steps", S, 1),
+        ("copies", V, 0), ("home", 0), ("back", 1), ("copy0", S, 3584, 3840), ("copy0", V, 3840, 4096), ("send sizes",), ("steps", V, 2),
+        ("copy0", S, 3072, 3584), ("copies", S, 1))
+END = HEAD + (
+    ("back", 2), ("home", 1), ("xlist",) + XA, ("copy0", V, 2048, 2560), ("copy0", S, 1024, 2048), ("home", 2), ("copy0", V, 2560, 3072), ("xl",) + XA,
+    ("sizes", 12, 14), ("newx", S, 3584, 4096), ("send strengths",), ("copy0", V, 0, 768), ("copy0", S, 768, 1024), ("copies", S, 2),
+    ("newx", V, 3072, 3584), ("sizes", 4, 12), ("sizes", 0, 4), ("xlist",) + XB, ("sizes", 14, 16), ("xlist",) + XC, ("xlist",) + XD, ("xl",) + XB,
+    ("newx", S, 2048, 3072), ("tables",), ("xl",) + XC, ("xl",) + XD, ("newx", S, 1024, 2048), ("newx", V, 0, 1024))
+END_LAST = HEAD + (
+    ("xlist",) + XE, ("back", 2), ("home", 1), ("copy0", V, 2048, 2304), ("xl",) + XE, ("home", 2), ("newx", S, 3584, 4096), ("send strengths",),
+    ("copy0", V, 2304, 3072), ("sizes", 12, 14), ("copy0", S, 1024, 2048), ("copy0", V, 0, 1024), ("copies", S, 2), ("xlist",) + XF, ("sizes", 8, 12),
+    ("xlist",) + XC, ("xlist",) + XD, ("sizes", 0, 8), ("sizes", 14, 16), ("xl",) + XF, ("newx", V, 3072, 3584), ("newx", S, 2048, 3072), ("xl",) + XC,
+    ("newx", V, 1024, 1536), ("newx", S, 1536, 2048), ("xl",) + XD, ("newx", V, 0, 512), ("newx", S, 512, 1024), ("tables",))
+CYCLE, PE, WAKE, GATHER, SCATTER, SLACK, FAR = 0.00083, 0.00055, 0.18, 1.3, 2.5, 0.2, 4.0
 
 SCRATCH = {
     "BIG": ("sbuf", [128, 20736], "bfloat16"),
@@ -38,6 +47,7 @@ SCRATCH = {
     "DI1": ("sbuf", [128, HOT[1][0], 128 * HOT[1][1] // HOT[1][0]], "bfloat16"),
     "G": ("sbuf", [128, 4096], "bfloat16"),
     "GQ": ("sbuf", [128, 4096], "bfloat16"),
+    "TH": ("sbuf", [128, 4096], "bfloat16"),
     "XS": ("sbuf", [128, 512], "bfloat16"),
     "LX": ("sbuf", [128, 512], "bfloat16"),
     "SEL": ("sbuf", [128, 1024], "bfloat16"),
@@ -46,8 +56,8 @@ SCRATCH = {
     "RR": ("sbuf", [128, 768], "float32"),
     "AB": ("sbuf", [128, 768], "float32"),
     "CT": ("sbuf", [128, 768], "bfloat16"),
-    "WT": ("sbuf", [128, 32], "bfloat16"),
-    "CQ": ("sbuf", [128, 768], "bfloat16"),
+    "WT": ("sbuf", [128, 512], "bfloat16"),
+    "CQ": ("sbuf", [128, 384], "bfloat16"),
     "AL": ("sbuf", [128, 128], "uint16"),
     "BL": ("sbuf", [128, 128], "uint16"),
     "EL": ("sbuf", [128, 264], "uint16"),
@@ -55,7 +65,7 @@ SCRATCH = {
     "PI": ("sbuf", [128, 4], "int32"),
     "COL": ("sbuf", [128, 52], "float32"),
     "PW": ("sbuf", [128, 544], "float32"),
-    "P0": ("sbuf", [128, 288], "float32"),
+    "P0": ("sbuf", [128, 17, 32], "float32"),
     "LB0": ("sbuf", [128, 144], "float32"),
     "HB": ("sbuf", [128, 512], "bfloat16"),
 }
@@ -63,24 +73,24 @@ for _n in ("ML", "UL", "QL", "XL"):
     SCRATCH[_n] = ("sbuf", [128, 256], "uint16")
 for _t in range(RO):
     SCRATCH["LZ%d" % _t] = ("sbuf", [128, 528], "bfloat16")
-for _n in ("LP", "LN", "L1", "LI", "LM1", "LM2", "LE", "LJ", "LV", "LZ"):
+for _n in ("LP", "LN", "L1", "LI", "LM1", "LE", "LJ", "LV", "LZ", "LT"):
     SCRATCH[_n] = ("sbuf", [128, 144], "bfloat16")
-for _n in ("ID", "NID", "IDP", "TRI", "SHF", "ONE", "TY", "Y0", "Y1", "Y2", "Y3", "Y4"):
+for _n in ("ID", "NID", "BLK", "IDP", "TRI", "TRI2", "SHF", "ONE"):
     SCRATCH[_n] = ("sbuf", [128, 128], "float32")
-for _n in ("IDM", "MISS", "IDB", "NIDB", "ID2B", "IDBIG", "NIDBIG", "IDHB", "NIDH", "IDN64", "IDA", "NIDA", "SHFB"):
+for _n in ("IDM", "MISS", "IDB", "NIDB", "ID2B", "IDBIG", "NIDBIG", "IDHB", "NIDH", "IDN64", "IDA", "NIDA", "SHFB", "BT", "ID16", "TRIB"):
     SCRATCH[_n] = ("sbuf", [128, 128], "bfloat16")
 for _n in ("I16", "DM", "DO", "O16"):
     SCRATCH[_n] = ("sbuf", [128, 16], "float32")
 SCRATCH["DG"] = ("sbuf", [128, 40], "float32")
 SCRATCH["U17"] = ("sbuf", [128, 17], "float32")
 SCRATCH["NB17"] = ("sbuf", [128, 17], "bfloat16")
-for _n in ("QW", "HF", "TWE", "KDE", "HK", "OX", "OUT", "JL", "LQ", "T6", "T1", "T5"):
+for _n in ("HF", "TWE", "KDE", "HK", "OX", "OUT", "LQ", "HV", "T5"):
     SCRATCH[_n] = ("sbuf", [128, 256], "float32")
-for _n in ("HL", "RL", "RS", "VC", "EE"):
+for _n in ("HL", "RL", "RS", "VC", "EE", "Y0", "Y1", "Y2", "Y3", "Y4"):
     SCRATCH[_n] = ("sbuf", [128, 264], "float32")
 for _n in ("ONEB", "V0", "V1"):
     SCRATCH[_n] = ("sbuf", [128, 264], "bfloat16")
-for _n in ("CP", "KD", "TW", "HM", "KI", "IT", "M0", "M1", "H0", "H1", "J0", "J1", "U0", "U1", "Z0", "Z1"):
+for _n in ("CP", "KD", "TW", "HM", "KI", "JL", "QC", "C1", "M0", "M1", "H0", "H1", "J0", "J1", "U0", "U1", "Z0", "Z1"):
     SCRATCH[_n] = ("sbuf", [128, 256], "bfloat16")
 for _n in range(8):
     SCRATCH["b%d" % _n] = ("psum", [128, 512], "float32")
@@ -130,7 +140,7 @@ def rank_program(g, core, T, topo):
     ops = []
     masks = {}
     row = [None]
-    KEPT = {"walk": "V", "rows": "Y", "blocks": "P", "end": "PS"}
+    KEPT = {"walk": "VS", "rows": "Y", "blocks": "VPS", "search": "VP", "end": "VPS"}
 
     def pm(p):
         if p not in masks:
@@ -149,7 +159,10 @@ def rank_program(g, core, T, topo):
     def width(x):
         if x[0] == "@":
             return 16 * width(x[2])
-        return len(range(x[2], x[3], x[4])) * (SCRATCH[x[0]][1][1] if len(x) == 6 and x[5] is None else 1)
+        blocks = 1
+        if len(x) == 6 and not isinstance(x[5], int):
+            blocks = SCRATCH[x[0]][1][1] if x[5] is None else x[5][1] - x[5][0]
+        return len(range(x[2], x[3], x[4])) * blocks
 
     def two(x):
         return SCRATCH.get(x[0], (0, 0, "x"))[2] in ("bfloat16", "uint16")
@@ -192,6 +205,8 @@ def rank_program(g, core, T, topo):
         if x[0] == "@":
             return ap(x[1]).indirect(ap(x[2]))
         if len(x) == 6:
+            if isinstance(x[5], tuple):
+                return T[x[0]][:, x[5][0]:x[5][1], x[2]:x[3]]
             return T[x[0]][:, :, x[2]:x[3]] if x[5] is None else T[x[0]][:, x[5], x[2]:x[3]]
         name, p, c0, c1, cs = x
         return T[name][p[0]:p[1]:p[2], c0:c1:cs] if (p[2] != 1 or cs != 1) else T[name][p[0]:p[1], c0:c1]
@@ -292,6 +307,9 @@ def rank_program(g, core, T, topo):
     def w64(name, h):
         return v(name, 64 * h, 64 * h + 64)
 
+    def yy(s, h, c=2, step=2):
+        return v("Y%d" % s, 132 * h + c, 132 * h + c + 128, step)
+
     dma(v("EI"), v("ends", 0, 4096, 1, (0, 8, 1)))
     dma(v("STI", 0, 128), v("start", 0, 128))
     dma(xs(0), v("x"))
@@ -312,7 +330,8 @@ def rank_program(g, core, T, topo):
     ts(GB, v("PI", 1, 2), -4096.0, OP.mult)
     copy(II, v("PI", 2, 3))
     ts(col(42), v("PI", 2, 3), 15.0, OP.is_ge, 4096.0, OP.mult)
-    fill(v("INFO"), 0.0)
+    for a in range(0, 4112, 514):
+        fill(v("INFO", a, a + 514), 0.0)
     act(v("VC", 0, 257), v("VC", 0, 257), ACT.Identity, GB)
     act(NEXT, VN, ACT.Copy)
     fill(v("ONEB"), 1.0)
@@ -334,9 +353,9 @@ def rank_program(g, core, T, topo):
         tt(v("TW"), ps(6, 1, 257), v("EE", 0, 256), OP.is_lt)
         tt(v("KD"), NEXT, v("EE", 0, 256), OP.is_lt)
         rows("INFO", 2, 1, "KD")
-        tt(ps(5), ps(5, 256, 512), v("TW"), OP.mult)
-        copy(v("M0"), ps(5))
+        tt(v("M0"), ps(5, 256, 512), v("TW"), OP.mult)
         rows("INFO", 0, 1, "M0")
+        tt(ps(5), ps(5, 256, 512), v("TW"), OP.mult)
         tt(v("M1"), ps(5), v("M0"), OP.subtract)
         rows("INFO", 1, 1, "M1")
         act(v("HF"), v("KD"), ACT.Identity, 1.0, -1.0)
@@ -364,32 +383,30 @@ def rank_program(g, core, T, topo):
     for k in range(5):
         fill(xs(k, 4096, SL), 255.0)
     ts(v("AL"), v("STI", 0, 128), 1.0, OP.add)
-    ts(v("Y0"), v("STI", 0, 128), 4.0, OP.add)
+    for h in range(2):
+        ts(yy(0, h), w64("STI", h), 4.0, OP.add)
+        fill(ps(2 + h, 384, 512), BIGW)
     act(col(43), II, ACT.Copy, None, 256.0)
     act(v("V0", 0, 257), v("ONEB", 0, 257), ACT.Copy, None, col(43))
     iota(v("V1", 0, 257), [[1, 257]], 0, 0)
     for name in ("HL", "RL"):
         fill(v(name, 0, 1), 0.0)
-    fill(v("P0"), 0.0)
+    fill(v3("P0", 0, 32), 0.0)
     for t in range(RO - 1):
         fill(v("LZ%d" % t, 512, 528), 0.0)
     asel(v("TRI"), v("ONE"), [[1, 128]], OP.is_gt, 0.0, 0, -1)
     asel(v("TRI"), v("TRI"), [[-16, 8], [0, 16]], OP.is_ge, 0.0, 0, 1)
     asel(v("IDP"), v("ONE"), [[-8, 2], [-16, 8], [-1, 8]], OP.is_equal, 0.0, 0, 1)
-    iota(v("QW"), [[16, 256]], 0, 1)
+    iota(v("QC"), [[16, 256]], 0, 0)
     iota(v("CP"), [[1, 16], [16, 16]], 1, 0)
     iota(v("CQ", 0, 256), [[0, 16], [1, 16]], 0, 0)
-    dma(v("CP", 0, 256, 1, (1, 128, 16)), v("CQ", 0, 256, 1, (1, 128, 16)))
-    for a in range(2):
-        iota(v("CQ", 256 * a + 256, 256 * a + 512), [[1, 8], [a, 2], [8, 16]], 0, 0)
-        dma(v("CP", 0, 256, 1, (16 * a + 2, 128, 32)), v("CQ", 256 * a + 256, 256 * a + 512, 1, (16 * a + 2, 128, 32)))
-    iota(v("IT"), [[0, 16], [BIGT, 16]], 0, 0)
+    for r in (1, 2):
+        dma(v("CP", 0, 256, 1, (r, 128, 16)), v("CQ", 0, 256, 1, (r, 128, 16)))
+    iota(v("CQ", 256, 384), [[0, 8], [BIGT, 16]], 0, 0)
     for k, piece in enumerate(TURN):
         iota(col(48 + k), [[0, 1]], 16 * piece[0] * BIGT, 16 * BIGT)
     iota(v("DM"), [[1, 16]], 12288, 16)
     iota(v("U17"), [[1, 17]], 0, 0)
-    act(col(46), G16, ACT.Copy, None, -1.0)
-    act(v("QW"), v("QW"), ACT.Identity, col(46))
 
     def growth_constants():
         ts(LIM, II, 14.0, OP.is_ge, 512.0, OP.mult)
@@ -399,33 +416,41 @@ def rank_program(g, core, T, topo):
         ts(v("U17"), v("U17"), II, OP.is_ge)
         ts(v("NB17", 0, 16), v("U17", 0, 16), -BIGW, OP.mult)
         fill(v("NB17", 16, 17), 0.0)
-        ts(COFF, AA, 272.0, OP.mult, -288.0, OP.add)
+        act(COFF, AA, ACT.Copy, None, -16.0)
 
-    def clear_windows():
-        for name in ("GT", "GH"):
-            dma_add(v(name, 0, 4096), xs(0), False)
-            fill(v(name, 4096, 4128), 0.0)
-        rows("GT", 7, 16, "V0")
-        rows("GT", 8, 16, "V1")
-        iota(v("SEL"), [[0, 1024]], 1, 0)
-        asel(v("SEL"), v("SEL"), [[-1, 1024]], OP.is_equal, 0.0, 384, 1)
-    iota(v("QB"), [[1, 4096]], 0, 0)
-    for a in range(0, 4096, 512):
-        act(v("QB", a, a + 512), v("QB", a, a + 512), ACT.Copy, None, 0.5)
+    iota(v("TH"), [[1, 16], [0, 256]], 0, -1)
+    act(col(44), G16, ACT.Identity, -0.5)
+    for name in ("GT", "GH"):
+        dma_add(v(name, 0, 4096), xs(0), False)
+        fill(v(name, 4096, 4128), 0.0)
+        rows(name, 7, 16, "V0")
+        rows(name, 8, 16, "V1")
+    rows("GT", 11, 16, "ONEB")
+    iota(v("SEL"), [[0, 1024]], 1, 0)
+    asel(v("SEL"), v("SEL"), [[-1, 1024]], OP.is_equal, 0.0, 384, 1)
+    asel(v("BLK"), v("ONE"), [[-16, 8], [0, 16]], OP.is_ge, 0.0, 0, 1)
+    asel(v("BLK"), v("BLK"), [[16, 8], [0, 16]], OP.is_ge, 0.0, 15, -1)
+
+    def late_constants():
+        iota(v("QB"), [[1, 4096]], 0, 0)
+        for a in range(0, 4096, 512):
+            act(v("QB", a, a + 512), v("QB", a, a + 512), ACT.Copy, None, 0.5)
+        asel(v("WT"), v("WT"), [[0, 4], [-16, 8], [0, 16]], OP.is_ge, 0.0, 0, 1)
+        asel(v("WT"), v("WT"), [[0, 4], [16, 8], [0, 16]], OP.is_ge, 0.0, 15, -1)
 
     for name, src, k in (("NIDB", "ID", -1.0), ("ID2B", "ID", 2.0), ("IDBIG", "ID", BIGW), ("IDN64", "ID", -64.0), ("IDA", "ID", float(SL)),
                          ("NIDA", "ID", -float(SL)), ("IDM", "IDP", 4096.0), ("SHFB", "SHF", 1.0), ("L1", "LB0", 1.0), ("NID", "ID", -1.0),
-                         ("IDHB", "ID", 0.5), ("NIDH", "ID", -0.5), ("NIDBIG", "ID", -BIGW)):
+                         ("ID16", "ID", 16.0), ("TRI2", "TRI", 2.0), ("TRIB", "TRI", 1.0), ("IDHB", "ID", 0.5), ("NIDH", "ID", -0.5), ("NIDBIG", "ID", -BIGW)):
         act(v(name), v(src), ACT.Copy, None, k)
-    weight("LM1", [(0, 288), (1, -255), (2, -544)])
-    weight("LM2", [(0, 16)])
+    weight("LM1", [(0, 32), (1, -256), (2, -255)])
     weight("LE", [(0, BIGW)])
-    weight("LJ", [(3, 1), (4, 1)])
+    weight("LJ", [(1, -1), (2, -1), (3, 2), (7, 1), (8, 1)])
     behind = weights([(1, BIGT), (2, BIGT), (5, -2 * BIGT), (6, -2 * BIGT), (7, -BIGT), (8, -BIGT)])
     size = weights([(1, 0.5), (2, 0.5), (3, 0.5), (4, 0.5), (5, -1), (6, -1), (7, -0.5), (8, -0.5)])
     act(col(47), size, ACT.Identity, behind, -float(BIGT))
-    for k, c in enumerate((behind, col(47), size, size)):
-        act(v("WT", 8 * k, 8 * k + 8), v("LB0", 15, 143, 16), ACT.Copy, None, c)
+    for k, c in enumerate((behind, col(47))):
+        act(v("WT", 128 * k, 128 * k + 128), v("CQ", 256, 384), ACT.Identity, c, v("I16", 11, 12))
+    act(v("WT", 256, 512), v("ONEB", 0, 256), ACT.Copy, None, size)
     weight("LV", [(7, 1), (8, 1)])
     weight("LZ", [(9, 1), (10, 1)])
 
@@ -436,66 +461,71 @@ def rank_program(g, core, T, topo):
     for t in range(RO):
         X = xs(XSLOT[t], 0, 4112)
         last = t == RO - 1
+        iota(v("BIG", 0, 4096), [[0, 4096]], 0, 0)
+        if t == 0:
+            late_constants()
         for c in range(2):
             iota(xs(LESS[t][c]), [[0, 4096]], -1 - c, 0)
-            if t == 0 and c == 0:
-                clear_windows()
             dma_add(xs(LESS[t][c]), xs(XSLOT[t]))
-        iota(v("BIG", 0, 4096), [[0, 4096]], 0, 0)
 
         def big(base, h):
             return bg(base[h], base[h] + 1024)
 
         def info(h, s):
-            act(big(IG, h), ind(v("INFO", 0, 4112), w64("AL", h)), ACT.Copy)
+            for onv, a, b in (((S, 0, 32), (V, 32, 64)) if h + s == 0 else ((S, 0, 64),)):
+                gather(onv, bg(IG[h] + 16 * a, IG[h] + 16 * b), v("INFO", 0, 4112), v("AL", 64 * h + a, 64 * h + b))
             mm(ps(h, 0, 64), v("NIDB"), v("ONEB", 0, 64), True, False)
-            mm(ps(h, 0, 64), v("ID"), w64("Y%d" % s, h), False, False, True)
+            mm(ps(h, 0, 64), v("ID"), yy(s, h), False, False, True)
             bwd(ps(h, 0, 64), "LI", "BIG", BO + IG[h], 64, False, True)
 
         def first(h, k):
             a, b = CUTS[k], CUTS[k + 1]
             tt(bg(MA[h] + 16 * a, MA[h] + 16 * b), ind(X, v("AL", 64 * h + a, 64 * h + b)), v("WP", 1024 * h + 16 * a, 1024 * h + 16 * b), OP.min)
             if b == 64:
-                bwd(ps(2 + h, 0, 64), "LP", "BIG", BO + MA[h], 64, True, False)
+                bwd(ps(2 + h, 385, 512, 2), "LP", "BIG", BO + MA[h], 64, True, False)
 
         def second_list(h, s):
             ts(w64("BL", h), ps(h, 0, 64), s - 3.0, OP.add)
+            act(yy(s, h, 3), ps(h, 0, 64), ACT.Copy)
 
         def second(h):
             tt(big(MB, h), ind(X, w64("BL", h)), v("WP", 1024 * h, 1024 * h + 1024), OP.min)
-            bwd(ps(2 + h, 0, 64), "LN", "BIG", BO + MB[h], 64, False, True)
+            bwd(ps(2 + h, 385, 512, 2), "LN", "BIG", BO + MB[h], 64, False, True)
 
-        def choose(h, s):
-            tt(w64("TY", h), ps(2 + h, 0, 64), w64("Y%d" % s, h), OP.max)
-
-        def enter(h, s):
-            tt(w64("Y%d" % (s + 1), h), ps(h, 0, 64), w64("TY", h), OP.min)
+        def decide(h, s):
+            scan(yy(s + 1, h, 1, 1), ps(2 + h, 384, 512), yy(s, h, 2, 1), 0.0, OP.max, OP.min)
 
         def first_list(h, s):
-            ts(w64("AL", h), w64("Y%d" % (s + 1), h), s - 2.0, OP.add)
+            ts(w64("AL", h), yy(s + 1, h), s - 2.0, OP.add)
             info(h, s + 1)
+
+        def end_rows(a, b):
+            act(v("GQ", 16 * a, 16 * b), ind(v("TH"), v("EL", a, b)), ACT.Sign, col(44))
         info(0, 0)
         info(1, 0)
-        for k in range(3):
+        for k in range(len(CUTS) - 1):
             first(0, k)
         second_list(0, 0)
         second(0)
         first(1, 0)
+        ts(v("EL", 0, 257), v("EE", 0, 257), -1.0, OP.add)
         row[0] = "walk"
         for n in range(7):
             h, s = n % 2, n // 2
             o, so = 1 - h, (n + 1) // 2
-            choose(h, s)
+            decide(h, s)
             first(o, 1)
-            enter(h, s)
+            if s < 3:
+                first_list(h, s)
             second_list(o, so)
             first(o, 2)
             if s < 3:
-                first_list(h, s)
+                if n > 1:
+                    end_rows(64 * n - 128, 64 * n - 64)
                 second(o)
                 first(h, 0)
-            if n == 4:
-                tt(v("MISS"), v("Y2"), v("Y1"), OP.is_lt)
+            if s == 2:
+                tt(w64("MISS", h), yy(2, h), yy(1, h), OP.is_lt)
 
         def digits(h):
             pieces, reps, _ = HOT[h]
@@ -506,12 +536,13 @@ def rank_program(g, core, T, topo):
             for a in (0, 64):
                 o = v("b%d" % (4 + h), 0, 64, 1, (a, a + 64, 1))
                 mm(o, w64("MISS", h), v("IDM", a, a + 64), True, False)
-                mm(o, w64("Y4", h), v("IDP", a, a + 64), False, True, True)
-            for r in range(reps):
-                ts(digit(r, 0), ps(4 + h, 0, 64), 1.0 / 64, OP.mult, 129 + reps - r - 31.5 / 64, OP.add)
+                mm(o, yy(4, h), v("IDP", a, a + 64), False, True, True)
+            ts(digit(0, 0), ps(4 + h, 0, 64), 1.0 / 64, OP.mult, 129 + reps - 31.5 / 64, OP.add)
+            for r in range(1, reps):
+                act(digit(r, 0), digit(0, 0), ACT.Identity, -float(r))
             for a in (0, 64):
                 o = v("b%d" % (6 + h), 0, 64, 1, (a, a + 64, 1))
-                mm(o, w64("Y4", h), v("IDP", a, a + 64), True, False)
+                mm(o, yy(4, h), v("IDP", a, a + 64), True, False)
                 mm(o, v("IDN64", a, a + 64), digit(0, 0), False, True, True)
             for r in range(reps):
                 act(digit(r, 1), ps(6 + h, 0, 64), ACT.Identity, 65.0 * (129 + reps) - r)
@@ -532,10 +563,12 @@ def rank_program(g, core, T, topo):
                 ts(o, d, c, OP.is_equal)
 
         def one_hot_scalar(h):
+            row[0] = None
             for j in mine(h, S):
                 d, o, c = hot(h, j)
                 act(o, d, ACT.Abs, -c)
                 act(o, o, ACT.Relu, 1.0, -1.0)
+            row[0] = "walk"
 
         def counts(h, gh):
             bank = (4, 6, 3, 2)[gh]
@@ -560,26 +593,24 @@ def rank_program(g, core, T, topo):
                 a = 384 - 128 * gh + cc
                 mm(ps(7, 64 * cc, 64 * cc + 64), v("SEL", a, a + 512, 4), o, gh + cc == 0, gh + cc == 6, cc > 0)
         if not last:
-            ts(v("Y0"), v("STI", 128 * t + 128, 128 * t + 256), 4.0, OP.add)
+            for h in range(2):
+                ts(yy(0, h), w64("STI", 2 * t + 2 + h), 4.0, OP.add)
         digits(0)
         second(1)
         one_hot_scalar(0)
         one_hot(0, 0, FILL[0])
-        choose(1, 3)
+        decide(1, 3)
         one_hot(0, FILL[0], FILL[1])
-        enter(1, 3)
-        one_hot(0, FILL[1], FILL[2])
         digits(1)
         one_hot_scalar(1)
-        one_hot(0, FILL[2], 64)
+        one_hot(0, FILL[1], 64)
         one_hot(1, 0, 64)
-        row[0] = None
         mm(ps(0), v("ID"), v("EE", 0, 256), True, True)
-        mm(ps(1), v("IDB"), v("V0", 0, 256), True, False)
-        mm(ps(1), v("IDB"), v("V1", 0, 256), False, False)
-        ts(v("EL", 0, 257), v("EE", 0, 257), -1.0, OP.add)
         tt(v("TWE"), ps(0), v("TW"), OP.mult)
         tt(v("KDE"), ps(0), v("KD"), OP.mult)
+        row[0] = None
+        mm(ps(1), v("IDB"), v("V0", 0, 256), True, False)
+        mm(ps(1), v("IDB"), v("V1", 0, 256), False, False)
         if not last:
             ts(v("AL"), v("STI", 128 * t + 128, 128 * t + 256), 1.0, OP.add)
         if t == 0:
@@ -601,12 +632,17 @@ def rank_program(g, core, T, topo):
         ts(v("DO"), v("DO"), 15.5, OP.is_gt)
         tt(v("DO"), v("DO"), v("DM"), OP.mult)
         tt(v("H1"), ps(4), v("H0"), OP.subtract)
-        tt(v("T1"), VC, ps(4), OP.subtract)
+        rows("GH", 1, 16, "H0")
+        rows("GH", 2, 16, "H1")
+        for k, (lname, name) in enumerate((("IDB", "V0"), ("IDB", "V1"), ("NIDB", "H0"), ("NIDB", "H1"))):
+            mm(ps(3), v(lname), v(name, 0, 256), k == 0, False)
         mm(ps(2), v("IDHB"), v("V0", 0, 256), True, False)
         mm(ps(2), v("IDHB"), v("V1", 0, 256), False, False)
         mm(ps(2), v("IDHB"), v("HM"), False, False)
         mm(ps(2), v("NIDH"), v("H0"), False, False)
         mm(ps(2), v("NIDH"), v("H1"), False, True)
+        tt(v("O16"), ps(2, 0, 256, 16), v("DO"), OP.max)
+        act(v("HV"), ps(2), ACT.Copy)
         GHW, GTW = v("GH", 16, 4112), v("GT", 16, 4112)
         mm(ps(0, 0, 257), v("NIDBIG"), v("ONEB", 0, 257), True, False)
         mm(ps(0, 1, 257), v("ID"), v("TWE"), False, False)
@@ -623,69 +659,101 @@ def rank_program(g, core, T, topo):
         tt(v("KI"), v("RS", 1, 257), ps(1), OP.is_gt)
         tt(v("OX"), v("RS", 0, 256), NEXT, OP.is_ge)
         scan(v("JL"), v("KI"), v("KI"), 0.0, OP.add, OP.max)
+        rows("GH", 3, 16, "JL")
         scan(v("LQ"), v("OX"), v("KI"), BIGW, OP.mult, OP.add)
         act(v("OUT"), v("KI"), ACT.Identity, 1.0, -1.0)
         act(v("OUT"), v("OUT"), ACT.Identity, THIRD, 1.0 - THIRD)
-        ts(v("DG", 0, 17), v("U17"), v("JL", 255, 256), OP.mult)
-        ts(v("DG", 24, 40), v("I16"), v("LQ", 255, 256), OP.mult, -1.0, OP.mult)
+        ts(v("C1", 0, 17), v("U17"), v("JL", 255, 256), OP.mult)
+        ts(v("C1", 24, 40), v("I16"), v("LQ", 255, 256), OP.mult, -1.0, OP.mult)
         mm(ps(7, 272, 289), v("IDB"), v("NB17"), True, False)
-        mm(ps(7, 272, 289), v("TRI"), v("DG", 0, 17), False, False)
-        mm(ps(7, 272, 288), v("TRI"), v("DG", 24, 40), False, True)
+        mm(ps(7, 272, 289), v("TRIB"), v("C1", 0, 17), False, False)
+        mm(ps(7, 272, 288), v("TRIB"), v("C1", 24, 40), False, True)
         base, above = ps(7, 288, 289), col(41)
-        red(above, ps(7, 272, 288), OP.max)
         tt(v("T5"), v("JL"), v("LQ"), OP.subtract)
-        ts(ps(4), v("JL"), base, OP.add, 2.0, OP.mult)
-        tt(ps(3), ps(4), v("T1"), OP.add)
-        act(v("J0"), ps(3), ACT.Copy)
-        rows("GH", 3, 16, "J0")
-        tt(v("J1"), ps(3), v("J0"), OP.subtract)
-        rows("GH", 4, 16, "J1")
-        rows("GT", 3, 16, "J0")
-        rows("GT", 4, 16, "J1")
-        ts(v("T6"), v("T5"), base, OP.add, above, OP.max)
-        tt(v("P0", 16, 272), ps(2), v("T6"), OP.add)
-        act(v("U0"), v("T6"), ACT.Copy)
-        tt(v("O16"), ps(2, 0, 256, 16), v("DO"), OP.max)
-        ts(ps(7, 304, 320), v("T5", 0, 256, 16), base, OP.add, above, OP.max)
-        tt(v("DO"), ps(7, 304, 320), v("O16"), OP.add)
-        ts(v("OFF"), v("DO"), 2.0, OP.mult)
-        copy(ind(v("BIG"), v("OFF")), v("CP"))
         mm(ps(1), v("IDB"), v("ONEB", 0, 256), True, False)
-        mm(ps(1), v("NIDB"), v("J0"), False, False)
-        mm(ps(1), v("NIDB"), v("J1"), False, False)
         mm(ps(1), v("NIDB"), v("HM"), False, False)
         mm(ps(1), v("ID2B"), v("KI"), False, False)
+        total = col(45)
         row[0] = "blocks"
+        red(above, ps(7, 272, 288), OP.max)
+        act(total, v("JL", 255, 256), ACT.Copy)
+        act(v("HB", 256, 384), v("TRI2"), ACT.Copy, None, total)
+        act(v("LT"), v("LB0"), ACT.Copy, None, total)
+        act(v("BT"), v("BLK"), ACT.Copy, None, total)
+        mm(ps(3), v("ID2B"), v("JL"), False, False)
+        mm(ps(3), v("HB", 256, 384), v("ONEB", 0, 256), False, True)
+        act(v("J0"), ps(3), ACT.Copy)
+        rows("GT", 3, 16, "J0")
+        T6 = ps(4, 256, 512)
+        ts(ps(7, 304, 320), v("T5", 0, 256, 16), base, OP.add, above, OP.max)
+        ts(T6, v("T5"), base, OP.add, above, OP.max)
+        tt(v("DO"), ps(7, 304, 320), v("O16"), OP.add)
+        tt(v3("P0", 0, 16, (1, 17)), T6, v("HV"), OP.add)
+        ts(v("OFF"), v("DO"), 2.0, OP.mult)
+        tt(v3("P0", 16, 32, (0, 16)), T6, v("HV"), OP.add)
+        copy(ind(v("BIG"), v("OFF")), v("CP"))
+        tt(v("J1"), ps(3), v("J0"), OP.subtract)
+        rows("GT", 4, 16, "J1")
+        for i in range(16):
+            mm(ps(1), blk("LT", i), v("GQ", i, 4096, 16), False, False, i % 2 > 0)
+        mm(ps(1), v("BT"), v("ONEB", 0, 256), False, False)
+        BLOCKS = (0, 2, 5, 6)
+
+        def at_ends(k):
+            onv, a, b = ENDS2[k]
+            gather(onv, v("G", 16 * a, 16 * b), GHW, v("EL", a, b))
+            bwd(ps(1, a, b), "LJ", "G", 16 * a, b - a, False, k == len(ENDS2) - 1)
+        at_ends(0)
+        act(v("U0"), T6, ACT.Copy)
+        rows("GT", 5, 16, "U0")
         for k in range(4):
             a = 1024 * k
             scan(v("BIG", VLS + a, VLS + a + 1024), v("BIG", a, a + 1024), v("BIG", a, a + 1024),
                  0.0 if k == 0 else v("BIG", VLS + a - 1, VLS + a), OP.max, OP.max)
-            bwd(ps(5 + k % 2, 0, 64), "LM1", "BIG", VLS + a, 64)
-            ts(w64("ML", k), ps(5 + k % 2, 0, 64), COFF, OP.add)
-        vtr(v("PW", 0, 256), v("P0", 16, 272))
-        vtr(v("PW", 256, 544), v("P0", 0, 288))
-        for onv, a, b in ENDS2:
-            gather(onv, v("G", 16 * a, 16 * b), GHW, v("EL", a, b))
-            bwd(ps(1, a, b), "LJ", "G", 16 * a, b - a, False, (onv, a, b) == ENDS2[-1])
-        row[0] = None
-        tt(v("U1"), v("T6"), v("U0"), OP.subtract)
-        rows("GT", 5, 16, "U0")
+            bwd(ps(BLOCKS[k], 0, 64), "LM1", "BIG", VLS + a, 64)
+            if k < 3:
+                a, b = 6 * k, min(17, 6 * k + 6)
+                vtr(v("PW", 32 * a, 32 * b), v3("P0", 0, 32, (a, b)))
+        mm(ps(1), v("NIDB"), v("J0"), False, False)
+        mm(ps(1), v("NIDB"), v("J1"), False, False)
+        for k in range(1, len(ENDS2)):
+            at_ends(k)
+        tt(v("U1"), T6, v("U0"), OP.subtract)
         rows("GT", 6, 16, "U1")
-        tt(ps(1), ps(1), v("OUT"), OP.mult)
-        copy(v("Z0"), ps(1))
-        rows("GT", 9, 16, "Z0")
-        tt(v("Z1"), ps(1), v("Z0"), OP.subtract)
-        rows("GT", 10, 16, "Z1")
-        for k, bank in ((3, 0), (2, 3), (1, 2), (0, 4)):
-            a = 1024 * k
-            bwd(ps(bank, 0, 64), "LM2", "BIG", VLS + a, 64, True, False)
-            tt(v("BIG", CMP + a, CMP + a + 1024), ind(v("PW"), w64("ML", k)), v("QB", a, a + 1024), OP.is_le)
-            bwd(ps(bank, 0, 64), "L1", "BIG", CMP + a, 64, False, True)
-            ts(w64("UL", k), ps(bank, 0, 64), -17.0, OP.add)
+        row[0] = None
+        for k in range(4):
+            ts(w64("ML", k), ps(BLOCKS[k], 0, 64), COFF, OP.add)
+        row[0] = "search"
+
+        def compare(a, b):
+            tt(v("BIG", CMP + 16 * a, CMP + 16 * b), ind(v("PW"), v("ML", a, b)), v("QB", 16 * a, 16 * b), OP.is_le)
+
+        def count(k):
+            o = ps(BLOCKS[k], 64, 128)
+            act(w64("T5", k), ps(BLOCKS[k], 0, 64), ACT.Copy, None, 256.0)
+            act(w64("C1", k), ps(BLOCKS[k], 0, 64), ACT.Identity, 127 - 15 / 64, 1 / 32)
+            mm(o, v("ID"), w64("T5", k), True, False)
+            mm(o, v("NIDBIG"), w64("C1", k), False, False, True)
+            mm(o, v("ID16"), w64("C1", k), False, False, True)
+            bwd(o, "L1", "BIG", CMP + 1024 * k, 64, False, True)
+
+        def found(k):
+            ts(w64("UL", k), ps(BLOCKS[k], 64, 128), 8176.0 * 128 - 8193, OP.add)
+
+        def new_sizes(k):
+            if k == 0:
+                tt(v("Z0"), ps(1), v("OUT"), OP.mult)
+                rows("GT", 9, 16, "Z0")
+                tt(ps(4), ps(1), v("OUT"), OP.mult)
+            else:
+                tt(v("Z1"), ps(4), v("Z0"), OP.subtract)
+                rows("GT", 10, 16, "Z1")
+        calls = {"compare": compare, "count": count, "found": found, "sizes": new_sizes}
+        for c in SEARCH:
+            calls[c[0]](*c[1:])
+        row[0] = None
         for a, n, tb, wb in TURN:
-            mm(v("b%d" % tb, 0, 256, 1, (0, n, 1)), v("IDB", 0, n), v("IT"), True, False)
-            mm(v("b%d" % tb, 256, 512, 1, (0, n, 1)), v("SEL", 0, n), v("IT"), False, False, True)
-            mm(ps(wb, 0, n), v("ID"), v("QW", a, a + n), True, False)
+            mm(ps(wb, 0, n), v("IDB"), v("QC", a, a + n), True, False)
         row[0] = "end"
 
         def part(name, k, a=0, b=256):
@@ -697,7 +765,7 @@ def rank_program(g, core, T, topo):
         def sums(k):
             a, n, tb, wb = TURN[k]
             for i in range(16):
-                mm(v("b%d" % tb, i, 512, 16, (0, n, 1)), v("G", 16 * a + i, 16 * (a + n), 16), v("WT"), False, i == 15, i > 0)
+                mm(v("b%d" % tb, i, 512, 16, (0, n, 1)), v("G", 16 * a + i, 16 * (a + n), 16), v("WT", i, 512, 16), i == 0, i == 15, i > 0)
 
         def steps(onv, k):
             a, n, tb, wb = TURN[k]
@@ -706,13 +774,16 @@ def rank_program(g, core, T, topo):
                 ts(part("RR", k), v("b%d" % tb, 0, 256, 1, p), v("COL", 48 + k, 49 + k, 1, p), OP.add, 0.0, OP.max)
             else:
                 act(part("RR", k), v("b%d" % tb, 0, 256, 1, p), ACT.Relu, v("COL", 48 + k, 49 + k, 1, p))
-            tt(part("AB", k), v("b%d" % tb, 256, 512, 1, p), part("RR", k), OP.min)
 
         def back(k):
             a, n, tb, wb = TURN[k]
+            tt(part("AB", k), v("b%d" % tb, 256, 512, 1, (0, n, 1)), part("RR", k), OP.min)
             for c in range(2):
                 mm(ps(wb, 0, n), part("AB", k, 128 * c, 128 * c + 128), v("NID", 0, n, 1, (0, n, 1)), False, c == 1, c > 0)
-            copy(v("QL", a, a + n), ps(wb, 0, n))
+
+        def home(k):
+            a, n, tb, wb = TURN[k]
+            ts(v("QL", a, a + n), ps(wb, 0, n), II, OP.add)
 
         def copies(onv, k):
             if onv:
@@ -741,7 +812,9 @@ def rank_program(g, core, T, topo):
                        v("IDA" if t == 0 else "NIDA", c0 - a0, c1 - a0, 1, (0, n, 1)), start, False, not start)
                     start = False
             bwd(o, "LV", "GQ", a, (b - a) // 16, False, True)
-            ts(v("XL", a // 16, b // 16), o, 0.0 if t == 0 else 2.0 * SL, OP.add)
+
+        def xl(bank, a, b):
+            ts(v("XL", a // 16, b // 16), ps(bank, 0, (b - a) // 16), 0.0 if t == 0 else 2.0 * SL, OP.add)
         XW = v("XX", SL * min(LESS[t] + (XSLOT[t],)), SL * (min(LESS[t] + (XSLOT[t],)) + 3))
         XN = XSLOT[t + 1]
 
@@ -760,7 +833,7 @@ def rank_program(g, core, T, topo):
                 s = v("GQ", a, a + w) if i < 14 else v("LZ%d" % t, a - 3584, a - 3584 + w)
                 mm(ps(6, 0, w), blk("LZ", i), s, False, i == 15, i > lo)
         land = v("LX") if last else xs(XN, 3584, 4096)
-        calls = {"run": run, "sums": sums, "steps": steps, "back": back, "copies": copies, "copy0": copy0, "xlist": xlist, "newx": newx,
+        calls = {"found": found, "run": run, "sums": sums, "steps": steps, "back": back, "home": home, "copies": copies, "copy0": copy0, "xlist": xlist, "xl": xl, "newx": newx,
                  "sizes": size_sums, "tables": lambda: tables(last),
                  "send sizes": lambda: send(v("GQ", 3584, 4096), v("LZ%d" % t, 0, 512), "rz%d" % t, "lz%d" % t),
                  "send strengths": lambda: send(v("XS"), land, "rx%d" % t, "lx%d" % t)}

import numpy as np
from concourse.bass import DstId, RemoteDMATransfer
from concourse.mybir import dt, AluOpType, AxisListType, ActivationFunctionType
import comms_topo

RO = 3
SL = 4224
BIGW = 8192.0
BIGT = 4096
THIRD = 11184811 / 2 ** 25
CUTS = (0, 48, 56, 64)
HOT = ((2, 4, 3), (4, 4, 3))
FILL = (7, 13)
ENDS1 = ((False, 134, 198), (True, 0, 64), (False, 198, 257), (True, 64, 134))
ENDS2 = ((False, 0, 64), (False, 64, 128), (False, 128, 192), (False, 192, 256))
SEARCH = (("compare", 64, 128), ("compare", 192, 256), ("compare", 128, 152), ("sizes", 0), ("compare", 152, 164), ("sizes", 1), ("count", 3),
          ("count", 1), ("compare", 164, 192), ("count", 2), ("found", 3), ("compare", 0, 64), ("count", 0), ("found", 1), ("found", 2))
V, S = True, False
TURN = ((192, 64, 4, 7), (64, 128, 6, 3), (0, 64, 0, 5))
XA, XB, XC, XD = (4, 3072, 4096), (7, 2048, 3072), (0, 1024, 2048), (4, 0, 1024)
XE, XF = (4, 3584, 4096), (7, 2048, 3584)
HEAD = (("run", S, 224, 256), ("run", V, 192, 224), ("sums", 0), ("run", S, 128, 192), ("run", V, 64, 96), ("found", 0), ("run", V, 96, 128),
        ("sums", 1), ("steps", V, 0), ("run", S, 0, 44), ("run", V, 44, 54), ("back", 0), ("run", V, 54, 64), ("sums", 2), ("steps", S, 1),
        ("copies", V, 0), ("home", 0), ("back", 1), ("copy0", S, 3584, 3840), ("copy0", V, 3840, 4096), ("send sizes",), ("steps", V, 2),
        ("copy0", S, 3072, 3584), ("copies", S, 1))
END = HEAD + (
    ("back", 2), ("home", 1), ("xlist",) + XA, ("copy0", V, 2048, 2560), ("copy0", S, 1024, 2048), ("home", 2), ("copy0", V, 2560, 3072), ("xl",) + XA,
    ("sizes", 12, 14), ("newx", S, 3584, 4096), ("send strengths",), ("copy0", V, 0, 768), ("copy0", S, 768, 1024), ("copies", S, 2),
    ("newx", V, 3072, 3584), ("sizes", 4, 12), ("sizes", 0, 4), ("xlist",) + XB, ("sizes", 14, 16), ("xlist",) + XC, ("xlist",) + XD, ("xl",) + XB,
    ("newx", S, 2048, 3072), ("tables",), ("xl",) + XC, ("xl",) + XD, ("newx", S, 1024, 2048), ("newx", V, 0, 1024))
END_LAST = HEAD + (
    ("xlist",) + XE, ("back", 2), ("home", 1), ("copy0", V, 2048, 2304), ("xl",) + XE, ("home", 2), ("newx", S, 3584, 4096), ("send strengths",),
    ("copy0", V, 2304, 3072), ("sizes", 12, 14), ("copy0", S, 1024, 2048), ("copy0", V, 0, 1024), ("copies", S, 2), ("xlist",) + XF, ("sizes", 8, 12),
    ("xlist",) + XC, ("xlist",) + XD, ("sizes", 0, 8), ("sizes", 14, 16), ("xl",) + XF, ("newx", V, 3072, 3584), ("newx", S, 2048, 3072), ("xl",) + XC,
    ("newx", V, 1024, 1536), ("newx", S, 1536, 2048), ("xl",) + XD, ("newx", V, 0, 512), ("newx", S, 512, 1024), ("tables",))
CYCLE, PE, WAKE, GATHER, SCATTER, SLACK, FAR = 0.00083, 0.00055, 0.18, 1.3, 2.5, 0.2, 4.0

SCRATCH = {
    "BIG": ("sbuf", [128, 20736], "bfloat16"),
    "XX": ("sbuf", [128, 5 * SL], "bfloat16"),
    "QB": ("sbuf", [128, 4096], "float32"),
    "WP": ("sbuf", [128, 2048], "bfloat16"),
    "INFO": ("sbuf", [128, 4112], "bfloat16"),
    "GH": ("sbuf", [128, 4128], "bfloat16"),
    "GT": ("sbuf", [128, 4128], "bfloat16"),
    "DI0": ("sbuf", [128, HOT[0][0], 128 * HOT[0][1] // HOT[0][0]], "bfloat16"),
    "DI1": ("sbuf", [128, HOT[1][0], 128 * HOT[1][1] // HOT[1][0]], "bfloat16"),
    "G": ("sbuf", [128, 4096], "bfloat16"),
    "GQ": ("sbuf", [128, 4096], "bfloat16"),
    "TH": ("sbuf", [128, 4096], "bfloat16"),
    "XS": ("sbuf", [128, 512], "bfloat16"),
    "LX": ("sbuf", [128, 512], "bfloat16"),
    "SEL": ("sbuf", [128, 1024], "bfloat16"),
    "STI": ("sbuf", [128, 384], "int32"),
    "EI": ("sbuf", [128, 256], "int32"),
    "RR": ("sbuf", [128, 768], "float32"),
    "AB": ("sbuf", [128, 768], "float32"),
    "CT": ("sbuf", [128, 768], "bfloat16"),
    "WT": ("sbuf", [128, 512], "bfloat16"),
    "CQ": ("sbuf", [128, 384], "bfloat16"),
    "AL": ("sbuf", [128, 128], "uint16"),
    "BL": ("sbuf", [128, 128], "uint16"),
    "EL": ("sbuf", [128, 264], "uint16"),
    "OFF": ("sbuf", [128, 16], "uint16"),
    "PI": ("sbuf", [128, 4], "int32"),
    "COL": ("sbuf", [128, 52], "float32"),
    "PW": ("sbuf", [128, 544], "float32"),
    "P0": ("sbuf", [128, 17, 32], "float32"),
    "LB0": ("sbuf", [128, 144], "float32"),
    "HB": ("sbuf", [128, 512], "bfloat16"),
}
for _n in ("ML", "UL", "QL", "XL"):
    SCRATCH[_n] = ("sbuf", [128, 256], "uint16")
for _t in range(RO):
    SCRATCH["LZ%d" % _t] = ("sbuf", [128, 528], "bfloat16")
for _n in ("LP", "LN", "L1", "LI", "LM1", "LE", "LJ", "LV", "LZ", "LT"):
    SCRATCH[_n] = ("sbuf", [128, 144], "bfloat16")
for _n in ("ID", "NID", "BLK", "IDP", "TRI", "TRI2", "SHF", "ONE"):
    SCRATCH[_n] = ("sbuf", [128, 128], "float32")
for _n in ("IDM", "MISS", "IDB", "NIDB", "ID2B", "IDBIG", "NIDBIG", "IDHB", "NIDH", "IDN64", "IDA", "NIDA", "SHFB", "BT", "ID16", "TRIB"):
    SCRATCH[_n] = ("sbuf", [128, 128], "bfloat16")
for _n in ("I16", "DM", "DO", "O16"):
    SCRATCH[_n] = ("sbuf", [128, 16], "float32")
SCRATCH["DG"] = ("sbuf", [128, 40], "float32")
SCRATCH["U17"] = ("sbuf", [128, 17], "float32")
SCRATCH["NB17"] = ("sbuf", [128, 17], "bfloat16")
for _n in ("HF", "TWE", "KDE", "HK", "OX", "OUT", "LQ", "HV", "T5"):
    SCRATCH[_n] = ("sbuf", [128, 256], "float32")
for _n in ("HL", "RL", "RS", "VC", "EE", "Y0", "Y1", "Y2", "Y3", "Y4"):
    SCRATCH[_n] = ("sbuf", [128, 264], "float32")
for _n in ("ONEB", "V0", "V1"):
    SCRATCH[_n] = ("sbuf", [128, 264], "bfloat16")
for _n in ("CP", "KD", "TW", "HM", "KI", "JL", "QC", "C1", "M0", "M1", "H0", "H1", "J0", "J1", "U0", "U1", "Z0", "Z1"):
    SCRATCH[_n] = ("sbuf", [128, 256], "bfloat16")
for _n in range(8):
    SCRATCH["b%d" % _n] = ("psum", [128, 512], "float32")

SEMAPHORES = (["sV", "sS", "sP", "sG"] + ["d%d" % _k for _k in range(80)] + ["a%d" % _k for _k in range(2 * RO + 2)]
              + ["%s%d" % (_a, _k) for _a in ("rx", "rz", "lx", "lz") for _k in range(RO)])

ALL = (0, 128, 1)
ACT = ActivationFunctionType
OP = AluOpType


def v(name, c0=0, c1=None, cs=1, p=ALL):
    if c1 is None:
        c1 = 4096 if name in ("y", "ye", "x", "ends") else SCRATCH[name][1][1]
    return (name, p, c0, c1, cs)


def v3(name, c0, c1, p=None):
    return (name, ALL, c0, c1, 1, p)


BO = 4096
VLS = 12544
CMP = 16640


def bg(c0, c1, cs=1):
    return v("BIG", BO + c0, BO + c1, cs)


def ind(win, off):
    return ("@", win, off)


def pmask(p):
    m = 0
    for k in range(p[0], p[1], p[2]):
        m |= 1 << k
    return m


def rank_program(g, core, T, topo):
    rank = T.rank_of(core)
    if rank is None:
        return
    ops = []
    masks = {}
    row = [None]
    KEPT = {"walk": "VS", "rows": "Y", "blocks": "VPS", "search": "VP", "end": "VPS"}

    def pm(p):
        if p not in masks:
            masks[p] = pmask(p)
        return masks[p]

    def flat(x, out):
        if isinstance(x, tuple):
            if x[0] == "@":
                out.append(x[1])
                out.append(x[2])
            else:
                out.append(x)
        return out

    def width(x):
        if x[0] == "@":
            return 16 * width(x[2])
        blocks = 1
        if len(x) == 6 and not isinstance(x[5], int):
            blocks = SCRATCH[x[0]][1][1] if x[5] is None else x[5][1] - x[5][0]
        return len(range(x[2], x[3], x[4])) * blocks

    def two(x):
        return SCRATCH.get(x[0], (0, 0, "x"))[2] in ("bfloat16", "uint16")

    def cost(q, out, ins, per):
        full = [x for x in ins if isinstance(x, tuple) and (x[0] == "@" or width(x) > 1)]
        n = max([width(out)] + [width(x) for x in full])
        if out[0] == "@":
            return 0.05 + n * SCATTER * CYCLE
        if any(x[0] == "@" for x in full):
            return 0.05 + n * GATHER * CYCLE
        if per is None:
            per = 0.5 if all(two(x) for x in full + [out]) else 1
        return max(64, n * per) * CYCLE + (0.015 if q == "V" else 0.035)

    def add(q, reads, writes, call, time, sem=None, n=1, own=True, lat=None, join=False):
        rd = []
        for x in reads:
            flat(x, rd)
        wr = []
        for x in writes:
            if x[0] == "@":
                wr.append(x[1])
                rd.append(x[2])
            else:
                wr.append(x)
        if join:
            o = ops[-1]
            o["r"] += rd
            o["w"] += [x for x in wr if x not in o["w"]]
            o["calls"].append(call)
            o["cost"] += time
            return
        ops.append({"q": q, "r": rd, "w": wr, "calls": [call], "sem": sem, "n": n, "own": own, "row": row[0], "cost": time,
                    "lat": WAKE if lat is None else lat})

    def ap(x):
        if not isinstance(x, tuple):
            return x
        if x[0] == "@":
            return ap(x[1]).indirect(ap(x[2]))
        if len(x) == 6:
            if isinstance(x[5], tuple):
                return T[x[0]][:, x[5][0]:x[5][1], x[2]:x[3]]
            return T[x[0]][:, :, x[2]:x[3]] if x[5] is None else T[x[0]][:, x[5], x[2]:x[3]]
        name, p, c0, c1, cs = x
        return T[name][p[0]:p[1]:p[2], c0:c1:cs] if (p[2] != 1 or cs != 1) else T[name][p[0]:p[1], c0:c1]

    def copy(out, i):
        add("V", [i], [out], lambda: g.vector.tensor_copy(ap(out), ap(i)), cost("V", out, [i], None))

    def tt(out, a, b, op):
        per = 1 if "psum" in (SCRATCH.get(a[0], "s")[0], SCRATCH[b[0]][0]) else 2
        add("V", [a, b], [out], lambda: g.vector.tensor_tensor(ap(out), ap(a), ap(b), op), cost("V", out, [a, b], per))

    def ts(out, a, s1, op0, s2=None, op1=None):
        if op1 is None:
            add("V", [a, s1], [out], lambda: g.vector.tensor_scalar(ap(out), ap(a), ap(s1), None, op0), cost("V", out, [a], None))
        else:
            add("V", [a, s1, s2], [out], lambda: g.vector.tensor_scalar(ap(out), ap(a), ap(s1), ap(s2), op0, op1), cost("V", out, [a], None))

    def red(out, i, op):
        add("V", [i], [out], lambda: g.vector.tensor_reduce(ap(out), ap(i), AxisListType.X, op), cost("V", out, [i], 1))

    def scan(out, d0, d1, init, op0, op1):
        add("V", [d0, d1, init], [out], lambda: g.vector.tensor_tensor_scan(ap(out), ap(d0), ap(d1), ap(init), op0, op1), cost("V", out, [d0, d1], None))

    def vtr(out, i):
        add("V", [i], [out], lambda: g.vector.transpose(ap(out), ap(i)), cost("V", out, [i], None))

    def fill(out, c):
        add("V", [], [out], lambda: g.vector.memset(ap(out), c), cost("V", out, [], None))

    def act(out, i, func, bias=None, scale=None):
        def call():
            kw = {}
            if bias is not None:
                kw["bias"] = ap(bias)
            if scale is not None:
                kw["scale"] = ap(scale)
            return g.scalar.activation(ap(out), ap(i), func, **kw)
        add("S", [i, scale, bias], [out], call, cost("S", out, [i], 1))

    def mm(out, l, r, start, stop, join=False):
        time = max(min(64, width(l)), width(r)) * (1 if two(l) else 4) * PE
        add("P", [l, r], [out], lambda: g.tensor.matmul(ap(out), ap(l), ap(r), start, stop), time, lat=WAKE + 0.1, join=join)

    def iota(out, pattern, base, cm, small=True):
        time = 0.13 + 2 * width(out) * CYCLE
        if small:
            add("G", [], [out], lambda: g.iota(ap(out), pattern, base, cm, allow_small_or_imprecise_dtypes=True), time)
        else:
            add("G", [], [out], lambda: g.iota(ap(out), pattern, base, cm), time)

    def asel(out, i, pattern, cop, fillv, base, cm):
        add("G", [i], [out], lambda: g.affine_select(ap(out), ap(i), pattern, cop, fillv, base, cm), 0.17 + 2 * width(out) * CYCLE)

    nd = [0, 0]

    def dma(out, i):
        sem = "d%d" % nd[0]
        nd[0] += 1
        add("Y", [i], [out], lambda: g.sync.dma_start(ap(out), ap(i)), 0.05, sem, 16, lat=1.6 + min(width(out), width(i)) / 1500)

    def dma_add(out, i, adds=True):
        sem = "a%d" % nd[1]
        nd[1] += 1
        if adds:
            add("G", [i, out], [out], lambda: g.dma_start(ap(out), ap(i), accum_op=OP.add, max_dma_last_dim=4096), 0.5, sem, 16, lat=6.0)
        else:
            add("G", [i], [out], lambda: g.dma_start(ap(out), ap(i)), 0.5, sem, 16, lat=6.0)

    def rows(name, r, c0, src):
        was, row[0] = row[0], "rows"
        dma(v(name, c0, c0 + 4096, 1, (r, 128, 16)), v(src, 0, 256))
        row[0] = was

    def blk(lname, i):
        return v(lname, 15 - i, 143 - i)

    def bwd(out, lname, src, c0, k, first=True, last=True):
        for i in range(16):
            mm(out, blk(lname, i), v(src, c0 + i, c0 + 16 * k, 16), first and i == 0, last and i == 15, i > 0)

    def gather(onv, out, win, lst, relu=False):
        if onv and relu:
            ts(out, ind(win, lst), 0.0, OP.max)
        elif onv:
            copy(out, ind(win, lst))
        else:
            act(out, ind(win, lst), ACT.Relu if relu else ACT.Copy)

    def xs(k, a=0, b=4096):
        return v("XX", SL * k + a, SL * k + b)

    def col(k):
        return v("COL", k, k + 1)

    def ps(k, a=0, b=256, step=1):
        return v("b%d" % k, a, b, step)

    def w64(name, h):
        return v(name, 64 * h, 64 * h + 64)

    def yy(s, h, c=2, step=2):
        return v("Y%d" % s, 132 * h + c, 132 * h + c + 128, step)

    dma(v("EI"), v("ends", 0, 4096, 1, (0, 8, 1)))
    dma(v("STI", 0, 128), v("start", 0, 128))
    dma(xs(0), v("x"))
    dma(v("WP", 0, 1024), v("w", 0, 1024))
    PIc = v("PI", 0, 1)
    iota(PIc, [[0, 1]], 0, 1, False)
    VC, VN, NEXT = v("VC", 0, 256), v("VC", 1, 257), ps(1, 256, 512)
    iota(v("VC", 0, 257), [[1, 257]], 0, 256)
    fill(v("ONE"), 1.0)
    asel(v("SHF"), v("ONE"), [[-1, 128]], OP.is_equal, 0.0, -1, 1)
    asel(v("ID"), v("ONE"), [[-1, 128]], OP.is_equal, 0.0, 0, 1)
    iota(v("LB0"), [[1, 144]], -15, 0)
    iota(v("I16"), [[1, 16]], 0, 0)
    ts(v("PI", 1, 2), PIc, 4, OP.arith_shift_right)
    ts(v("PI", 2, 3), PIc, 15, OP.bitwise_and)
    ts(v("PI", 3, 4), v("PI", 1, 2), 1, OP.bitwise_and)
    G16, GB, II, AA, LIM, COFF = col(0), col(1), col(2), col(3), col(4), col(5)
    ts(GB, v("PI", 1, 2), -4096.0, OP.mult)
    copy(II, v("PI", 2, 3))
    ts(col(42), v("PI", 2, 3), 15.0, OP.is_ge, 4096.0, OP.mult)
    for a in range(0, 4112, 514):
        fill(v("INFO", a, a + 514), 0.0)
    act(v("VC", 0, 257), v("VC", 0, 257), ACT.Identity, GB)
    act(NEXT, VN, ACT.Copy)
    fill(v("ONEB"), 1.0)
    ts(G16, v("PI", 1, 2), 16.0, OP.mult)
    copy(AA, v("PI", 3, 4))
    act(v("IDB"), v("ID"), ACT.Copy)

    def tables(last, cut=True):
        if not cut:
            copy(col(7), v("EI", 0, 1))
            copy(ps(6), v("EI"))
            mm(ps(6, 256, 257), v("SHF"), col(7), True, False)
            mm(ps(6, 256, 257), v("ID"), col(42), False, True)
        w = 256 if last else 257
        ts(v("EE", 0, w), ps(6, 0, w), LIM if cut else 4096.0, OP.min)
        if last:
            return
        tt(ps(5, 256, 512), ps(6, 1, 257), VN, OP.subtract)
        tt(v("TW"), ps(6, 1, 257), v("EE", 0, 256), OP.is_lt)
        tt(v("KD"), NEXT, v("EE", 0, 256), OP.is_lt)
        rows("INFO", 2, 1, "KD")
        tt(v("M0"), ps(5, 256, 512), v("TW"), OP.mult)
        rows("INFO", 0, 1, "M0")
        tt(ps(5), ps(5, 256, 512), v("TW"), OP.mult)
        tt(v("M1"), ps(5), v("M0"), OP.subtract)
        rows("INFO", 1, 1, "M1")
        act(v("HF"), v("KD"), ACT.Identity, 1.0, -1.0)
    tables(False, False)
    dma(v("WP", 1024, 2048), v("w", 1024, 2048))
    dma(v("STI", 128, 384), v("start", 128, 384))
    ts(v("LB0"), v("LB0"), G16, OP.is_equal)
    ts(v("I16"), v("I16"), II, OP.is_equal)
    ts(v("LP"), v("LB0"), BIGW, OP.mult)
    ts(v("LN"), v("LB0"), -BIGW, OP.mult)
    nw = [8]

    def weights(terms):
        c = None
        for r, wgt in terms:
            n = col(nw[0])
            nw[0] += 1
            act(n, v("I16", r, r + 1), ACT.Identity, c, float(wgt))
            c = n
        return c

    def weight(name, terms):
        act(v(name), v("LB0"), ACT.Copy, None, weights(terms))
    weight("LI", [(0, 1), (1, 1), (2, 1)])
    for k in range(5):
        fill(xs(k, 4096, SL), 255.0)
    ts(v("AL"), v("STI", 0, 128), 1.0, OP.add)
    for h in range(2):
        ts(yy(0, h), w64("STI", h), 4.0, OP.add)
        fill(ps(2 + h, 384, 512), BIGW)
    act(col(43), II, ACT.Copy, None, 256.0)
    act(v("V0", 0, 257), v("ONEB", 0, 257), ACT.Copy, None, col(43))
    iota(v("V1", 0, 257), [[1, 257]], 0, 0)
    for name in ("HL", "RL"):
        fill(v(name, 0, 1), 0.0)
    fill(v3("P0", 0, 32), 0.0)
    for t in range(RO - 1):
        fill(v("LZ%d" % t, 512, 528), 0.0)
    asel(v("TRI"), v("ONE"), [[1, 128]], OP.is_gt, 0.0, 0, -1)
    asel(v("TRI"), v("TRI"), [[-16, 8], [0, 16]], OP.is_ge, 0.0, 0, 1)
    asel(v("IDP"), v("ONE"), [[-8, 2], [-16, 8], [-1, 8]], OP.is_equal, 0.0, 0, 1)
    iota(v("QC"), [[16, 256]], 0, 0)
    iota(v("CP"), [[1, 16], [16, 16]], 1, 0)
    iota(v("CQ", 0, 256), [[0, 16], [1, 16]], 0, 0)
    for r in (1, 2):
        dma(v("CP", 0, 256, 1, (r, 128, 16)), v("CQ", 0, 256, 1, (r, 128, 16)))
    iota(v("CQ", 256, 384), [[0, 8], [BIGT, 16]], 0, 0)
    for k, piece in enumerate(TURN):
        iota(col(48 + k), [[0, 1]], 16 * piece[0] * BIGT, 16 * BIGT)
    iota(v("DM"), [[1, 16]], 12288, 16)
    iota(v("U17"), [[1, 17]], 0, 0)

    def growth_constants():
        ts(LIM, II, 14.0, OP.is_ge, 512.0, OP.mult)
        act(LIM, LIM, ACT.Identity, 3584.0)
        ts(col(6), G16, 16.0, OP.mult)
        ts(v("DM"), v("DM"), col(6), OP.subtract, 0.5, OP.mult)
        ts(v("U17"), v("U17"), II, OP.is_ge)
        ts(v("NB17", 0, 16), v("U17", 0, 16), -BIGW, OP.mult)
        fill(v("NB17", 16, 17), 0.0)
        act(COFF, AA, ACT.Copy, None, -16.0)

    iota(v("TH"), [[1, 16], [0, 256]], 0, -1)
    act(col(44), G16, ACT.Identity, -0.5)
    for name in ("GT", "GH"):
        dma_add(v(name, 0, 4096), xs(0), False)
        fill(v(name, 4096, 4128), 0.0)
        rows(name, 7, 16, "V0")
        rows(name, 8, 16, "V1")
    rows("GT", 11, 16, "ONEB")
    iota(v("SEL"), [[0, 1024]], 1, 0)
    asel(v("SEL"), v("SEL"), [[-1, 1024]], OP.is_equal, 0.0, 384, 1)
    asel(v("BLK"), v("ONE"), [[-16, 8], [0, 16]], OP.is_ge, 0.0, 0, 1)
    asel(v("BLK"), v("BLK"), [[16, 8], [0, 16]], OP.is_ge, 0.0, 15, -1)

    def late_constants():
        iota(v("QB"), [[1, 4096]], 0, 0)
        for a in range(0, 4096, 512):
            act(v("QB", a, a + 512), v("QB", a, a + 512), ACT.Copy, None, 0.5)
        asel(v("WT"), v("WT"), [[0, 4], [-16, 8], [0, 16]], OP.is_ge, 0.0, 0, 1)
        asel(v("WT"), v("WT"), [[0, 4], [16, 8], [0, 16]], OP.is_ge, 0.0, 15, -1)

    for name, src, k in (("NIDB", "ID", -1.0), ("ID2B", "ID", 2.0), ("IDBIG", "ID", BIGW), ("IDN64", "ID", -64.0), ("IDA", "ID", float(SL)),
                         ("NIDA", "ID", -float(SL)), ("IDM", "IDP", 4096.0), ("SHFB", "SHF", 1.0), ("L1", "LB0", 1.0), ("NID", "ID", -1.0),
                         ("ID16", "ID", 16.0), ("TRI2", "TRI", 2.0), ("TRIB", "TRI", 1.0), ("IDHB", "ID", 0.5), ("NIDH", "ID", -0.5), ("NIDBIG", "ID", -BIGW)):
        act(v(name), v(src), ACT.Copy, None, k)
    weight("LM1", [(0, 32), (1, -256), (2, -255)])
    weight("LE", [(0, BIGW)])
    weight("LJ", [(1, -1), (2, -1), (3, 2), (7, 1), (8, 1)])
    behind = weights([(1, BIGT), (2, BIGT), (5, -2 * BIGT), (6, -2 * BIGT), (7, -BIGT), (8, -BIGT)])
    size = weights([(1, 0.5), (2, 0.5), (3, 0.5), (4, 0.5), (5, -1), (6, -1), (7, -0.5), (8, -0.5)])
    act(col(47), size, ACT.Identity, behind, -float(BIGT))
    for k, c in enumerate((behind, col(47))):
        act(v("WT", 128 * k, 128 * k + 128), v("CQ", 256, 384), ACT.Identity, c, v("I16", 11, 12))
    act(v("WT", 256, 512), v("ONEB", 0, 256), ACT.Copy, None, size)
    weight("LV", [(7, 1), (8, 1)])
    weight("LZ", [(9, 1), (10, 1)])

    IG, MA, MB, OH = (0, 1024), (2048, 3072), (4096, 5120), (8192, 0)
    XSLOT = (0, 3, 4, 0)
    LESS = ((1, 2), (2, 1), (3, 2))

    for t in range(RO):
        X = xs(XSLOT[t], 0, 4112)
        last = t == RO - 1
        iota(v("BIG", 0, 4096), [[0, 4096]], 0, 0)
        if t == 0:
            late_constants()
        for c in range(2):
            iota(xs(LESS[t][c]), [[0, 4096]], -1 - c, 0)
            dma_add(xs(LESS[t][c]), xs(XSLOT[t]))

        def big(base, h):
            return bg(base[h], base[h] + 1024)

        def info(h, s):
            for onv, a, b in (((S, 0, 32), (V, 32, 64)) if h + s == 0 else ((S, 0, 64),)):
                gather(onv, bg(IG[h] + 16 * a, IG[h] + 16 * b), v("INFO", 0, 4112), v("AL", 64 * h + a, 64 * h + b))
            mm(ps(h, 0, 64), v("NIDB"), v("ONEB", 0, 64), True, False)
            mm(ps(h, 0, 64), v("ID"), yy(s, h), False, False, True)
            bwd(ps(h, 0, 64), "LI", "BIG", BO + IG[h], 64, False, True)

        def first(h, k):
            a, b = CUTS[k], CUTS[k + 1]
            tt(bg(MA[h] + 16 * a, MA[h] + 16 * b), ind(X, v("AL", 64 * h + a, 64 * h + b)), v("WP", 1024 * h + 16 * a, 1024 * h + 16 * b), OP.min)
            if b == 64:
                bwd(ps(2 + h, 385, 512, 2), "LP", "BIG", BO + MA[h], 64, True, False)

        def second_list(h, s):
            ts(w64("BL", h), ps(h, 0, 64), s - 3.0, OP.add)
            act(yy(s, h, 3), ps(h, 0, 64), ACT.Copy)

        def second(h):
            tt(big(MB, h), ind(X, w64("BL", h)), v("WP", 1024 * h, 1024 * h + 1024), OP.min)
            bwd(ps(2 + h, 385, 512, 2), "LN", "BIG", BO + MB[h], 64, False, True)

        def decide(h, s):
            scan(yy(s + 1, h, 1, 1), ps(2 + h, 384, 512), yy(s, h, 2, 1), 0.0, OP.max, OP.min)

        def first_list(h, s):
            ts(w64("AL", h), yy(s + 1, h), s - 2.0, OP.add)
            info(h, s + 1)

        def end_rows(a, b):
            act(v("GQ", 16 * a, 16 * b), ind(v("TH"), v("EL", a, b)), ACT.Sign, col(44))
        info(0, 0)
        info(1, 0)
        for k in range(len(CUTS) - 1):
            first(0, k)
        second_list(0, 0)
        second(0)
        first(1, 0)
        ts(v("EL", 0, 257), v("EE", 0, 257), -1.0, OP.add)
        row[0] = "walk"
        for n in range(7):
            h, s = n % 2, n // 2
            o, so = 1 - h, (n + 1) // 2
            decide(h, s)
            first(o, 1)
            if s < 3:
                first_list(h, s)
            second_list(o, so)
            first(o, 2)
            if s < 3:
                if n > 1:
                    end_rows(64 * n - 128, 64 * n - 64)
                second(o)
                first(h, 0)
            if s == 2:
                tt(w64("MISS", h), yy(2, h), yy(1, h), OP.is_lt)

        def digits(h):
            pieces, reps, _ = HOT[h]
            n = 64 // pieces

            def digit(r, low):
                return v3("DI%d" % h, n * (2 * r + low), n * (2 * r + low + 1))
            for a in (0, 64):
                o = v("b%d" % (4 + h), 0, 64, 1, (a, a + 64, 1))
                mm(o, w64("MISS", h), v("IDM", a, a + 64), True, False)
                mm(o, yy(4, h), v("IDP", a, a + 64), False, True, True)
            ts(digit(0, 0), ps(4 + h, 0, 64), 1.0 / 64, OP.mult, 129 + reps - 31.5 / 64, OP.add)
            for r in range(1, reps):
                act(digit(r, 0), digit(0, 0), ACT.Identity, -float(r))
            for a in (0, 64):
                o = v("b%d" % (6 + h), 0, 64, 1, (a, a + 64, 1))
                mm(o, yy(4, h), v("IDP", a, a + 64), True, False)
                mm(o, v("IDN64", a, a + 64), digit(0, 0), False, True, True)
            for r in range(reps):
                act(digit(r, 1), ps(6 + h, 0, 64), ACT.Identity, 65.0 * (129 + reps) - r)

        def hot(h, j):
            pieces, reps, _ = HOT[h]
            p, k = divmod(j, 64 // reps)
            w = 128 * reps // pieces
            return v3("DI%d" % h, 0, w, p), bg(OH[h] + w * j, OH[h] + w * j + w), 129.0 + reps + reps * k

        def mine(h, onv):
            pieces, reps, ns = HOT[h]
            return [j for j in range(64 * pieces // reps) if (j % (64 // reps) >= ns) == onv]

        def one_hot(h, a, b):
            for j in mine(h, V)[a:b]:
                d, o, c = hot(h, j)
                ts(o, d, c, OP.is_equal)

        def one_hot_scalar(h):
            row[0] = None
            for j in mine(h, S):
                d, o, c = hot(h, j)
                act(o, d, ACT.Abs, -c)
                act(o, o, ACT.Relu, 1.0, -1.0)
            row[0] = "walk"

        def counts(h, gh):
            bank = (4, 6, 3, 2)[gh]
            n = 64 // HOT[h][0]
            if h == 0:
                mm(ps(bank, 0, 64), v("SEL", 0, 128), v("ONEB", 0, 64), True, False)
            for x0 in range(16):
                gg = x0 // 8
                p, x = divmod(16 * gh + x0, n)
                c, end = OH[h] + 128 * n * p + x, OH[h] + 128 * n * (p + 1)
                mm(v("b%d" % bank, 0, 64, 1, (64 * gg, 64 * gg + 64, 1)), bg(c, end, 2 * n), bg(c + n, end, 2 * n),
                   False, False, x0 > 0)
            if h == 0:
                return
            mm(ps(bank, 0, 64), v("SEL", 0, 128), v("ONEB", 0, 64), False, True, True)
            o = v("HB", 64 * gh, 64 * gh + 64)
            if gh >= 3:
                copy(o, ps(bank, 0, 64))
            else:
                act(o, ps(bank, 0, 64), ACT.Copy)
            for cc in range(4):
                a = 384 - 128 * gh + cc
                mm(ps(7, 64 * cc, 64 * cc + 64), v("SEL", a, a + 512, 4), o, gh + cc == 0, gh + cc == 6, cc > 0)
        if not last:
            for h in range(2):
                ts(yy(0, h), w64("STI", 2 * t + 2 + h), 4.0, OP.add)
        digits(0)
        second(1)
        one_hot_scalar(0)
        one_hot(0, 0, FILL[0])
        decide(1, 3)
        one_hot(0, FILL[0], FILL[1])
        digits(1)
        one_hot_scalar(1)
        one_hot(0, FILL[1], 64)
        one_hot(1, 0, 64)
        mm(ps(0), v("ID"), v("EE", 0, 256), True, True)
        tt(v("TWE"), ps(0), v("TW"), OP.mult)
        tt(v("KDE"), ps(0), v("KD"), OP.mult)
        row[0] = None
        mm(ps(1), v("IDB"), v("V0", 0, 256), True, False)
        mm(ps(1), v("IDB"), v("V1", 0, 256), False, False)
        if not last:
            ts(v("AL"), v("STI", 128 * t + 128, 128 * t + 256), 1.0, OP.add)
        if t == 0:
            growth_constants()
        for h in range(2):
            for gh in range(4):
                counts(h, gh)
        tt(v("HM"), ps(7), v("HF"), OP.min)
        rows("GT", 0, 15, "HM")
        scan(v("HL", 1, 257), v("HM"), v("HM"), 0.0, OP.add, OP.max)
        mm(ps(3, 0, 255), v("IDB"), v("HM", 1, 256), True, False)
        mm(ps(3, 255, 256), v("SHFB"), v("HM", 0, 1), False, True)
        mm(ps(7, 256, 257), v("TRI"), v("HL", 256, 257), True, True)
        mm(ps(1), v("IDBIG"), v("HM"), False, True)
        tt(v("HK"), ps(3), v("KDE"), OP.mult)
        ts(ps(4), v("HL", 1, 257), ps(7, 256, 257), OP.add)
        copy(v("H0"), ps(4))
        tt(v("DO"), v("HL", 16, 257, 16), v("HL", 0, 256, 16), OP.subtract)
        ts(v("DO"), v("DO"), 15.5, OP.is_gt)
        tt(v("DO"), v("DO"), v("DM"), OP.mult)
        tt(v("H1"), ps(4), v("H0"), OP.subtract)
        rows("GH", 1, 16, "H0")
        rows("GH", 2, 16, "H1")
        for k, (lname, name) in enumerate((("IDB", "V0"), ("IDB", "V1"), ("NIDB", "H0"), ("NIDB", "H1"))):
            mm(ps(3), v(lname), v(name, 0, 256), k == 0, False)
        mm(ps(2), v("IDHB"), v("V0", 0, 256), True, False)
        mm(ps(2), v("IDHB"), v("V1", 0, 256), False, False)
        mm(ps(2), v("IDHB"), v("HM"), False, False)
        mm(ps(2), v("NIDH"), v("H0"), False, False)
        mm(ps(2), v("NIDH"), v("H1"), False, True)
        tt(v("O16"), ps(2, 0, 256, 16), v("DO"), OP.max)
        act(v("HV"), ps(2), ACT.Copy)
        GHW, GTW = v("GH", 16, 4112), v("GT", 16, 4112)
        mm(ps(0, 0, 257), v("NIDBIG"), v("ONEB", 0, 257), True, False)
        mm(ps(0, 1, 257), v("ID"), v("TWE"), False, False)
        for n, (onv, a, b) in enumerate(ENDS1):
            gather(onv, bg(16 * a, 16 * b), GTW, v("EL", a, b))
            bwd(ps(0, a, b), "LE", "BIG", BO + 16 * a, b - a, False, n == len(ENDS1) - 1)
        rows("GT", 1, 16, "H0")
        rows("GT", 2, 16, "H1")
        scan(v("RL", 1, 257), ps(0, 1, 257), v("HK"), 0.0, OP.max, OP.max)
        ts(v("DG", 0, 16), v("I16"), v("RL", 256, 257), OP.mult)
        mm(ps(7, 272, 288), v("TRI"), v("DG", 0, 16), True, True)
        red(col(40), ps(7, 272, 288), OP.max)
        ts(v("RS", 0, 257), v("RL", 0, 257), col(40), OP.max)
        tt(v("KI"), v("RS", 1, 257), ps(1), OP.is_gt)
        tt(v("OX"), v("RS", 0, 256), NEXT, OP.is_ge)
        scan(v("JL"), v("KI"), v("KI"), 0.0, OP.add, OP.max)
        rows("GH", 3, 16, "JL")
        scan(v("LQ"), v("OX"), v("KI"), BIGW, OP.mult, OP.add)
        act(v("OUT"), v("KI"), ACT.Identity, 1.0, -1.0)
        act(v("OUT"), v("OUT"), ACT.Identity, THIRD, 1.0 - THIRD)
        ts(v("C1", 0, 17), v("U17"), v("JL", 255, 256), OP.mult)
        ts(v("C1", 24, 40), v("I16"), v("LQ", 255, 256), OP.mult, -1.0, OP.mult)
        mm(ps(7, 272, 289), v("IDB"), v("NB17"), True, False)
        mm(ps(7, 272, 289), v("TRIB"), v("C1", 0, 17), False, False)
        mm(ps(7, 272, 288), v("TRIB"), v("C1", 24, 40), False, True)
        base, above = ps(7, 288, 289), col(41)
        tt(v("T5"), v("JL"), v("LQ"), OP.subtract)
        mm(ps(1), v("IDB"), v("ONEB", 0, 256), True, False)
        mm(ps(1), v("NIDB"), v("HM"), False, False)
        mm(ps(1), v("ID2B"), v("KI"), False, False)
        total = col(45)
        row[0] = "blocks"
        red(above, ps(7, 272, 288), OP.max)
        act(total, v("JL", 255, 256), ACT.Copy)
        act(v("HB", 256, 384), v("TRI2"), ACT.Copy, None, total)
        act(v("LT"), v("LB0"), ACT.Copy, None, total)
        act(v("BT"), v("BLK"), ACT.Copy, None, total)
        mm(ps(3), v("ID2B"), v("JL"), False, False)
        mm(ps(3), v("HB", 256, 384), v("ONEB", 0, 256), False, True)
        act(v("J0"), ps(3), ACT.Copy)
        rows("GT", 3, 16, "J0")
        T6 = ps(4, 256, 512)
        ts(ps(7, 304, 320), v("T5", 0, 256, 16), base, OP.add, above, OP.max)
        ts(T6, v("T5"), base, OP.add, above, OP.max)
        tt(v("DO"), ps(7, 304, 320), v("O16"), OP.add)
        tt(v3("P0", 0, 16, (1, 17)), T6, v("HV"), OP.add)
        ts(v("OFF"), v("DO"), 2.0, OP.mult)
        tt(v3("P0", 16, 32, (0, 16)), T6, v("HV"), OP.add)
        copy(ind(v("BIG"), v("OFF")), v("CP"))
        tt(v("J1"), ps(3), v("J0"), OP.subtract)
        rows("GT", 4, 16, "J1")
        for i in range(16):
            mm(ps(1), blk("LT", i), v("GQ", i, 4096, 16), False, False, i % 2 > 0)
        mm(ps(1), v("BT"), v("ONEB", 0, 256), False, False)
        BLOCKS = (0, 2, 5, 6)

        def at_ends(k):
            onv, a, b = ENDS2[k]
            gather(onv, v("G", 16 * a, 16 * b), GHW, v("EL", a, b))
            bwd(ps(1, a, b), "LJ", "G", 16 * a, b - a, False, k == len(ENDS2) - 1)
        at_ends(0)
        act(v("U0"), T6, ACT.Copy)
        rows("GT", 5, 16, "U0")
        for k in range(4):
            a = 1024 * k
            scan(v("BIG", VLS + a, VLS + a + 1024), v("BIG", a, a + 1024), v("BIG", a, a + 1024),
                 0.0 if k == 0 else v("BIG", VLS + a - 1, VLS + a), OP.max, OP.max)
            bwd(ps(BLOCKS[k], 0, 64), "LM1", "BIG", VLS + a, 64)
            if k < 3:
                a, b = 6 * k, min(17, 6 * k + 6)
                vtr(v("PW", 32 * a, 32 * b), v3("P0", 0, 32, (a, b)))
        mm(ps(1), v("NIDB"), v("J0"), False, False)
        mm(ps(1), v("NIDB"), v("J1"), False, False)
        for k in range(1, len(ENDS2)):
            at_ends(k)
        tt(v("U1"), T6, v("U0"), OP.subtract)
        rows("GT", 6, 16, "U1")
        row[0] = None
        for k in range(4):
            ts(w64("ML", k), ps(BLOCKS[k], 0, 64), COFF, OP.add)
        row[0] = "search"

        def compare(a, b):
            tt(v("BIG", CMP + 16 * a, CMP + 16 * b), ind(v("PW"), v("ML", a, b)), v("QB", 16 * a, 16 * b), OP.is_le)

        def count(k):
            o = ps(BLOCKS[k], 64, 128)
            act(w64("T5", k), ps(BLOCKS[k], 0, 64), ACT.Copy, None, 256.0)
            act(w64("C1", k), ps(BLOCKS[k], 0, 64), ACT.Identity, 127 - 15 / 64, 1 / 32)
            mm(o, v("ID"), w64("T5", k), True, False)
            mm(o, v("NIDBIG"), w64("C1", k), False, False, True)
            mm(o, v("ID16"), w64("C1", k), False, False, True)
            bwd(o, "L1", "BIG", CMP + 1024 * k, 64, False, True)

        def found(k):
            ts(w64("UL", k), ps(BLOCKS[k], 64, 128), 8176.0 * 128 - 8193, OP.add)

        def new_sizes(k):
            if k == 0:
                tt(v("Z0"), ps(1), v("OUT"), OP.mult)
                rows("GT", 9, 16, "Z0")
                tt(ps(4), ps(1), v("OUT"), OP.mult)
            else:
                tt(v("Z1"), ps(4), v("Z0"), OP.subtract)
                rows("GT", 10, 16, "Z1")
        calls = {"compare": compare, "count": count, "found": found, "sizes": new_sizes}
        for c in SEARCH:
            calls[c[0]](*c[1:])
        row[0] = None
        for a, n, tb, wb in TURN:
            mm(ps(wb, 0, n), v("IDB"), v("QC", a, a + n), True, False)
        row[0] = "end"

        def part(name, k, a=0, b=256):
            return v(name, 256 * k + a, 256 * k + b, 1, (0, TURN[k][1], 1))

        def run(onv, a, b):
            gather(onv, v("G", 16 * a, 16 * b), GTW, v("UL", a, b))

        def sums(k):
            a, n, tb, wb = TURN[k]
            for i in range(16):
                mm(v("b%d" % tb, i, 512, 16, (0, n, 1)), v("G", 16 * a + i, 16 * (a + n), 16), v("WT", i, 512, 16), i == 0, i == 15, i > 0)

        def steps(onv, k):
            a, n, tb, wb = TURN[k]
            p = (0, n, 1)
            if onv:
                ts(part("RR", k), v("b%d" % tb, 0, 256, 1, p), v("COL", 48 + k, 49 + k, 1, p), OP.add, 0.0, OP.max)
            else:
                act(part("RR", k), v("b%d" % tb, 0, 256, 1, p), ACT.Relu, v("COL", 48 + k, 49 + k, 1, p))

        def back(k):
            a, n, tb, wb = TURN[k]
            tt(part("AB", k), v("b%d" % tb, 256, 512, 1, (0, n, 1)), part("RR", k), OP.min)
            for c in range(2):
                mm(ps(wb, 0, n), part("AB", k, 128 * c, 128 * c + 128), v("NID", 0, n, 1, (0, n, 1)), False, c == 1, c > 0)

        def home(k):
            a, n, tb, wb = TURN[k]
            ts(v("QL", a, a + n), ps(wb, 0, n), II, OP.add)

        def copies(onv, k):
            if onv:
                ts(part("CT", k), part("RR", k), 1.0, OP.min)
            else:
                act(part("CT", k), part("RR", k), ACT.Sign)
        dst = T.cores[(rank + 1) % len(T.cores)]
        src = T.cores[(rank - 1) % len(T.cores)]

        def send(frm, to, rsem, lsem):
            rid, pid, _se = topo.addr(dst)
            add("G", [frm], [], lambda: g.remote_dma(ap(to), ap(frm), T.sem[rsem], T.sem[lsem], pid, rid, topo.mask(core, dst)),
                0.3, lsem, len(topo.engines(core, dst)), False, FAR)
            add("R", [], [to], None, 0.0, rsem, len(topo.engines(src, core)), lat=0.1)

        def copy0(onv, a, b):
            gather(onv, v("GQ", a, b), v("G", 0, 2048 if b <= 2048 else 4096), v("QL", a // 16, b // 16))

        def xlist(bank, a, b):
            o = ps(bank, 0, (b - a) // 16)
            lo, hi, start = a // 16, b // 16, True
            for k, (a0, n, tb, wb) in enumerate(TURN):
                c0, c1 = max(a0, lo), min(a0 + n, hi)
                for c in range(2 if c0 < c1 else 0):
                    mm(ps(bank, c0 - lo, c1 - lo), part("CT", k, 128 * c, 128 * c + 128),
                       v("IDA" if t == 0 else "NIDA", c0 - a0, c1 - a0, 1, (0, n, 1)), start, False, not start)
                    start = False
            bwd(o, "LV", "GQ", a, (b - a) // 16, False, True)

        def xl(bank, a, b):
            ts(v("XL", a // 16, b // 16), ps(bank, 0, (b - a) // 16), 0.0 if t == 0 else 2.0 * SL, OP.add)
        XW = v("XX", SL * min(LESS[t] + (XSLOT[t],)), SL * (min(LESS[t] + (XSLOT[t],)) + 3))
        XN = XSLOT[t + 1]

        def newx(onv, a, b):
            gather(onv, xs(XN, a, b) if a < 3584 else v("XS"), XW, v("XL", a // 16, b // 16), True)
            if last and a < 3584:
                dma(v("y", a, b), xs(XN, a, b))

        def size_sums(lo, hi):
            w = 256 if last else 257
            if lo == 12:
                mm(ps(6, 0, w), v("IDB"), v("V0", 0, w), True, False)
                mm(ps(6, 0, w), v("IDB"), v("V1", 0, w), False, False, True)
            for i in range(lo, hi):
                a = 256 * i
                s = v("GQ", a, a + w) if i < 14 else v("LZ%d" % t, a - 3584, a - 3584 + w)
                mm(ps(6, 0, w), blk("LZ", i), s, False, i == 15, i > lo)
        land = v("LX") if last else xs(XN, 3584, 4096)
        calls = {"found": found, "run": run, "sums": sums, "steps": steps, "back": back, "home": home, "copies": copies, "copy0": copy0, "xlist": xlist, "xl": xl, "newx": newx,
                 "sizes": size_sums, "tables": lambda: tables(last),
                 "send sizes": lambda: send(v("GQ", 3584, 4096), v("LZ%d" % t, 0, 512), "rz%d" % t, "lz%d" % t),
                 "send strengths": lambda: send(v("XS"), land, "rx%d" % t, "lx%d" % t)}
        for c in (END_LAST if last else END):
            calls[c[0]](*c[1:])
        row[0] = None
        if last:
            dma(v("ye", 0, 4096, 1, (0, 8, 1)), v("EE", 0, 256))
            dma(v("y", 3584, 4096), land)

    hist = {}
    lastq = {}
    for k, o in enumerate(ops):
        q = o["q"]
        o["k"] = k
        deps, order = {}, {}
        for wr, lst in ((0, o["r"]), (1, o["w"])):
            for x in lst:
                name = x[0]
                psum = SCRATCH.get(name, "d")[0] == "psum"
                m = pm(x[1])
                keep = []
                for h in hist.get(name, []):
                    ho, hw, hx = h
                    over = (pm(hx[1]) & m) and hx[2] < x[3] and x[2] < hx[3]
                    if psum and ho["q"] != q:
                        deps[ho["k"]] = ho
                    elif psum and q == "P":
                        order[ho["k"]] = ho
                        continue
                    elif over and (wr or hw):
                        deps[ho["k"]] = ho
                    if wr and not psum and hx[2] >= x[2] and hx[3] <= x[3] and (pm(hx[1]) & ~m) == 0 and x[4] == 1 and x[5:] in ((), (None,)):
                        continue
                    keep.append(h)
                hist[name] = keep
        key = q if q == "G" else (q, o["row"])
        if key in lastq and (q == "G" or o["row"] and q in KEPT[o["row"]]):
            order[lastq[key]["k"]] = lastq[key]
        if q == "R":
            order[k - 1] = ops[k - 1]
        lastq[key] = o
        deps.pop(k, None)
        order.pop(k, None)
        o["deps"], o["order"] = list(deps.values()), list(order.values())
        for wr, lst in ((0, o["r"]), (1, o["w"])):
            for x in lst:
                hist.setdefault(x[0], []).append((o, wr, x))

    for o in ops:
        o["next"] = []
    for o in ops:
        o["left"] = len(o["deps"]) + len(o["order"])
        for d in o["deps"] + o["order"]:
            d["next"].append(o)
    for o in reversed(ops):
        o["way"] = o["cost"] + o["lat"] + max([n["way"] for n in o["next"]] + [0.0])
    ready = {q: [] for q in "VSPGYR"}
    free = {q: 0.0 for q in ready}
    for o in ops:
        if o["left"] == 0:
            o["at"] = 0.0
            ready[o["q"]].append(o)

    def pick(q):
        now = free[q]
        top = max(ready[q], key=lambda z: (z["way"], -z["k"]))
        best, gain = top, None
        for o in ready[q]:
            if o is top or max(o["at"], now) >= max(top["at"], now):
                continue
            end = max(o["at"], now) + o["cost"]
            before = max(max(end, top["at"]) + top["way"], max(o["at"], now) + o["way"])
            after = max(top["at"] + top["way"], top["at"] + top["cost"] + o["way"])
            if before <= after + SLACK and (gain is None or o["way"] > gain):
                best, gain = o, o["way"]
        return best
    issued = []
    while len(issued) < len(ops):
        o = min((pick(q) for q in ready if ready[q]), key=lambda z: (max(z["at"], free[z["q"]]), z["k"]))
        q = o["q"]
        ready[q].remove(o)
        free[q] = max(o["at"], free[q]) + o["cost"]
        o["go"], o["end"] = free[q], free[q] + o["lat"]
        issued.append(o)
        for n in o["next"]:
            n["left"] -= 1
            if n["left"] == 0:
                n["at"] = max([d["end"] for d in n["deps"]] + [d["end"] if n["q"] == "R" else d["go"] for d in n["order"]])
                ready[n["q"]].append(n)

    qidx = {}
    known = {}
    need = set()
    for k, o in enumerate(issued):
        q = o["q"]
        o["k"] = k
        if o["sem"] is None:
            o["tok"] = (q, qidx.get(q, 0))
            qidx[q] = qidx.get(q, 0) + 1
        else:
            o["tok"] = ("*" + o["sem"], 0)
        kn = known.setdefault(q if q != "R" else ("R", k), {})
        waits = []
        best = {}
        for ho in o["deps"]:
            tq, ti = ho["tok"]
            if tq not in best or best[tq]["tok"][1] < ti:
                best[tq] = ho
        for ho in sorted(best.values(), key=lambda z: -z["k"]):
            tq, ti = ho["tok"]
            if kn.get(tq, -1) >= ti:
                continue
            waits.append(ho)
            need.add(ho["tok"])
            for a, b in ho["kn"].items():
                if kn.get(a, -1) < b:
                    kn[a] = b
            kn[tq] = max(kn.get(tq, -1), ti)
        o["waits"] = waits
        o["kn"] = dict(kn)
    cnt = {}
    eng_of = {"V": g.vector, "S": g.scalar, "P": g.tensor, "G": g, "Y": g.sync}
    sem_of = {"V": "sV", "S": "sS", "P": "sP", "G": "sG"}
    for o in issued:
        q = o["q"]
        if q == "R":
            o["val"] = o["n"]
            continue
        e = eng_of[q]
        for ho in o["waits"]:
            e.wait_ge(T.sem[ho["sem"] or sem_of[ho["q"]]], ho["val"])
        for call in o["calls"]:
            r = call()
        if o["sem"] is not None:
            o["val"] = o["n"]
            if o["own"]:
                r.then_inc(T.sem[o["sem"]], o["n"])
        elif o["tok"] in need:
            cnt[q] = cnt.get(q, 0) + 1
            o["val"] = cnt[q]
            r.then_inc(T.sem[sem_of[q]], 1)
    for q in ("V", "S", "P", "G"):
        if cnt.get(q, 0):
            g.wait_ge(T.sem[sem_of[q]], cnt[q])
    for o in issued:
        if o["sem"] is not None:
            g.wait_ge(T.sem[o["sem"]], o["n"])
